import numpy as np
import ml_dtypes


def mxq(x, axis, fmt="e4m3"):
    dtype, down = {"e4m3": (ml_dtypes.float8_e4m3fn, 7), "e5m2": (ml_dtypes.float8_e5m2, 14)}[fmt]
    v = np.moveaxis(np.asarray(x, np.float32).astype(ml_dtypes.bfloat16).astype(np.float64), axis, -1)
    blocks = v.reshape(v.shape[:-1] + (-1, 32))
    amax = np.abs(blocks).max(-1, keepdims=True)
    byte = np.maximum(np.where(amax > 0, np.frexp(amax)[1] - 1 + 127, 0) - down, 1)
    scale = np.exp2(byte - 127.0)
    codes = (blocks / scale).astype(np.float32).astype(dtype).astype(np.float64)
    return np.moveaxis((codes * scale).reshape(v.shape), -1, axis)


WIDE = False


def mx_kscale(k):
    if not WIDE:
        return np.ones(k)
    levels = np.array([10, -10, 5, -5, 0])
    if k % 512:
        return np.exp2(np.random.permutation(np.resize(levels, k // 32))).repeat(32)
    a = np.empty((k // 512, 16))
    for p in range(k // 512):
        a[p, :8] = np.random.permutation(np.resize(levels, 8))
        for g in range(8):
            far = levels[np.abs(levels - a[p, g]) >= 10]
            a[p, g + 8] = far[np.random.randint(len(far))]
    return np.exp2(a.ravel()).repeat(32)


def f64(x):
    return np.asarray(x).astype(np.float64)


def striped(idx):
    return np.tile(idx.reshape(-1, 16).T, (8, 1)).astype(np.uint16)


def unstriped(offs):
    return offs[:16].T.reshape(-1).astype(np.int64)


K, T, D, V, H, N = 512, 512, 4, 256, 1024, 512
P = 2 ** 7


def setup_inputs():
    n = np.random.standard_normal
    s = mx_kscale(K)[:, None]
    u = mx_kscale(H)
    return {
        "xT": (n((K, T)) * s).astype(np.float32),
        "w1": (n((K, H)) / np.sqrt(K) / s * u).astype(np.float32),
        "w2": (n((H, N)) / np.sqrt(H) / u[:, None]).astype(np.float32),
        "gate": np.tile(np.random.uniform(0.2, 1.0, (D, 1, V)) / np.sqrt(D), (1, P, 1)).astype(np.float32),
        "pos1": striped(np.random.permutation(T)[:V]),
        "pos2": striped(np.random.permutation(T)[:V]),
        "pos3": striped(np.random.permutation(T)[:V]),
        "pos4": striped(np.random.permutation(T)[:V]),
    }


def reference(xT, w1, w2, gate, pos1, pos2, pos3, pos4):
    h = mxq(f64(w1), 0, "e4m3").T @ mxq(f64(xT), 0, "e4m3")
    z = sum(f64(gate)[d, :1] * h[:, unstriped(p)] for d, p in enumerate((pos1, pos2, pos3, pos4)))
    return mxq(f64(w2), 0, "e4m3").T @ mxq(z, 0, "e4m3")

@@ -1,0 +1,227 @@
+from contextlib import ExitStack
+
+import concourse.mybir as mybir
+
+F32 = mybir.dt.float32
+BF16 = mybir.dt.bfloat16
+U32 = mybir.dt.uint32
+U16 = mybir.dt.uint16
+U8 = mybir.dt.uint8
+FP8X4 = mybir.dt.float8_e4m3fn_x4
+MULT = mybir.AluOpType.mult
+ADD = mybir.AluOpType.add
+
+K, T, D, V, H, N = 512, 512, 4, 256, 1024, 512
+FLOPS = 2 * K * H * T + 2 * H * N * V
+
+P = 128
+J = 4
+KP = P * J
+X_V = 352
+VH = 128
+
+
+def tile_picked_gcn_mlp_none_sub_l_kernel(tc, xT, w1, w2, gate, pos1, pos2, pos3, pos4, out):
+    nc = tc.nc
+    with ExitStack() as ctx:
+        lists = ctx.enter_context(tc.tile_pool(name="lists", bufs=1))
+        keep = ctx.enter_context(tc.tile_pool(name="keep", bufs=1))
+        psum = ctx.enter_context(tc.psum_pool(name="psum", bufs=8))
+
+        pos = [lists.tile([P, V // 16], U16, name=f"pos{d}") for d in range(D)]
+        gates = [keep.tile([P, V], F32, name=f"gate{d}") for d in range(D)]
+
+        x_raw = keep.tile([P, J, T], F32, name="x_raw")
+        w1_first = [keep.tile([P, J // 2, KP], F32, name=f"w1_first{c}") for c in range(2)]
+        w1_rest = keep.tile([P, J, KP], F32, name="w1_rest")
+        w2_raw = [keep.tile([P, J, N], F32, name=f"w2_raw{g}") for g in range(2)]
+
+        x_view = xT.rearrange("(p j) t -> p j t", j=J)
+        w1_view = w1.rearrange("(p j) i -> p j i", j=J)
+        w2_view = w2.rearrange("(g p j) n -> g p j n", g=2, j=J)
+        out_view = out.rearrange("(a p) v -> p a v", p=P)
+
+        nc.sync.dma_start(x_raw[:], x_view)
+        for c in range(2):
+            nc.sync.dma_start(w1_first[c][:], w1_view[:, 2 * c : 2 * c + 2, 0:KP])
+        for d, src in enumerate((pos1, pos2, pos3, pos4)):
+            nc.sync.dma_start(pos[d][:], src)
+            nc.sync.dma_start(gates[d][:], gate[d])
+        nc.sync.dma_start(w1_rest[:], w1_view[:, :, KP:H])
+        for g in range(2):
+            nc.sync.dma_start(w2_raw[g][:], w2_view[g])
+
+        w1_grouped = [keep.tile([P, J, P, J], BF16, name=f"w1_grouped{g}", align_bytes=64) for g in range(2)]
+        w1_codes = [keep.tile([P, J, P], U32, name=f"w1_codes{g}", align_bytes=64) for g in range(2)]
+        w1_scales = [keep.tile([P, J, P], U8, name=f"w1_scales{g}", align_bytes=64) for g in range(2)]
+        x_grouped = keep.tile([P, T, J], BF16, name="x_grouped", align_bytes=64)
+        x_codes = keep.tile([P, T], U32, name="x_codes", align_bytes=64)
+        x_scales = keep.tile([P, T], U8, name="x_scales", align_bytes=64)
+        w2_grouped = [keep.tile([P, N, J], BF16, name=f"w2_grouped{g}", align_bytes=64) for g in range(2)]
+        w2_codes = [keep.tile([P, N], U32, name=f"w2_codes{g}", align_bytes=64) for g in range(2)]
+        w2_scales = [keep.tile([P, N], U8, name=f"w2_scales{g}", align_bytes=64) for g in range(2)]
+
+        def group_w1_first(copy, c, t):
+            copy(
+                out=w1_grouped[0][:, t, :, 2 * c : 2 * c + 2],
+                in_=w1_first[c][:].rearrange("p j (m t) -> p t m j", t=J)[:, t, :, :],
+            )
+
+        def group_w1_rest(copy, ma, mb):
+            copy(
+                out=w1_grouped[1][:, :, ma:mb, :].rearrange("p t m j -> p m j t"),
+                in_=w1_rest[:, :, J * ma : J * mb].rearrange("p j (m t) -> p m j t", t=J),
+            )
+
+        def quantize_w1(g, t0, t1):
+            nc.vector.quantize_mx(
+                out=w1_codes[g][:, t0:t1, :].rearrange("p t m -> p (t m)").bitcast(FP8X4),
+                scales=w1_scales[g][:, t0:t1, :].rearrange("p t m -> p (t m)"),
+                in_=w1_grouped[g][:, t0:t1, :, :].rearrange("p t m j -> p (t m j)"),
+            )
+
+        def group_cols(copy, dst, src, a, b):
+            copy(
+                out=dst[:, a:b, :].rearrange("p (c i) j -> p c j i", i=4),
+                in_=src[:, :, a:b].rearrange("p j (c i) -> p c j i", i=4),
+            )
+
+        def quantize_cols(codes, scales, grouped, c0, c1, g0):
+            nc.vector.quantize_mx(
+                out=codes[:, c0:c1].bitcast(FP8X4),
+                scales=scales[:, c0:c1],
+                in_=grouped[:, g0 : g0 + c1 - c0, :].rearrange("p n j -> p (n j)"),
+            )
+
+        vcopy, scopy = nc.vector.tensor_copy, nc.scalar.copy
+
+        h = [[keep.tile([P, T], F32, name=f"h{g}_{t}") for t in range(J)] for g in range(2)]
+
+        def project(g, t, n0, n1, copy=nc.scalar.copy):
+            bank = psum.tile([P, 512], F32, name="bank")
+            nc.tensor.matmul_mx(
+                out=bank[:, : n1 - n0],
+                lhsT=w1_codes[g][:, t, :].bitcast(FP8X4),
+                lhsT_scale=w1_scales[g][:, t, :],
+                rhs=x_codes[:, n0:n1].bitcast(FP8X4),
+                rhs_scale=x_scales[:, n0:n1],
+                start=True,
+                stop=True,
+            )
+            copy(out=h[g][t][:, n0:n1], in_=bank[:, : n1 - n0])
+
+        group_cols(vcopy, x_grouped, x_raw, 0, X_V)
+        group_cols(scopy, x_grouped, x_raw, X_V, T)
+        for n in range(2):
+            quantize_cols(x_codes, x_scales, x_grouped, n * 256, (n + 1) * 256, n * 256)
+        for t in range(J):
+            group_w1_first(vcopy if t < 2 else scopy, 0, t)
+        group_w1_first(vcopy, 1, 0)
+        quantize_w1(0, 0, 1)
+        group_w1_first(scopy, 1, 1)
+        project(0, 0, 0, 256)
+        project(0, 0, 256, 512, vcopy)
+        quantize_w1(0, 1, 2)
+        group_w1_first(scopy, 1, 2)
+        project(0, 1, 0, T)
+        group_w1_first(scopy, 1, 3)
+
+        prods = [[keep.tile([P, J, V], F32, name=f"prod{g}_{d}") for d in range(D)] for g in range(2)]
+        sums = [[keep.tile([P, J, V], F32, name=f"sum{g}_{s}") for s in range(2)] for g in range(2)]
+        z_grouped = [keep.tile([P, V, J], BF16, name=f"z_grouped{g}", align_bytes=64) for g in range(2)]
+        z_codes = [keep.tile([P, V], U32, name=f"z_codes{g}", align_bytes=64) for g in range(2)]
+        z_scales = [keep.tile([P, V], U8, name=f"z_scales{g}", align_bytes=64) for g in range(2)]
+
+        def gather(g, d, t, v0=0, v1=V):
+            offs = pos[d][:] if v1 - v0 == V else pos[d][:, v0 // 16 : v1 // 16]
+            nc.vector.tensor_tensor(prods[g][d][:, t, v0:v1], h[g][t][:].indirect(offs), gates[d][:, v0:v1], MULT)
+
+        def add(dst, a, b):
+            nc.vector.tensor_tensor(
+                dst[:].rearrange("p t v -> p (t v)"), a[:].rearrange("p t v -> p (t v)"), b[:].rearrange("p t v -> p (t v)"), ADD
+            )
+
+        def last_add(g, v0, v1):
+            nc.vector.tensor_tensor(
+                z_grouped[g][:, v0:v1, :].rearrange("p (c i) t -> p c t i", i=4),
+                sums[g][1][:, :, v0:v1].rearrange("p t (c i) -> p c t i", i=4),
+                prods[g][3][:, :, v0:v1].rearrange("p t (c i) -> p c t i", i=4),
+                ADD,
+            )
+
+        acc = {}
+
+        def second(g):
+            for a in range(N // P):
+                if g == 0:
+                    acc[a] = psum.tile([P, 512], F32, name="bank")
+                nc.tensor.matmul_mx(
+                    out=acc[a][:, :V],
+                    lhsT=w2_codes[g][:, a * P : (a + 1) * P].bitcast(FP8X4),
+                    lhsT_scale=w2_scales[g][:, a * P : (a + 1) * P],
+                    rhs=z_codes[g][:].bitcast(FP8X4),
+                    rhs_scale=z_scales[g][:],
+                    start=(g == 0),
+                    stop=(g == 1),
+                )
+
+        def emit(a, copy, dma):
+            o = keep.tile([P, V], F32, name=f"o{a}")
+            copy(out=o[:], in_=acc[a][:, :V])
+            dma(out=out_view[:, a, :], in_=o[:])
+
+        gather(0, 0, 0)
+        gather(0, 1, 0)
+        quantize_w1(0, 2, 4)
+        for t in (2, 3):
+            project(0, t, 0, T)
+        for t in range(1, J):
+            for d in range(2):
+                gather(0, d, t)
+        for m in range(0, P, 64):
+            group_w1_rest(scopy, m, m + 64)
+        gather(0, 2, 0)
+        add(sums[0][0], prods[0][0], prods[0][1])
+        for t in range(1, J):
+            gather(0, 2, t)
+        gather(0, 3, 0)
+        add(sums[0][1], sums[0][0], prods[0][2])
+        gather(0, 3, 1)
+        quantize_w1(1, 0, J)
+        for t in range(J):
+            project(1, t, 0, T)
+        gather(0, 3, 2)
+        gather(0, 3, 3)
+        for g in range(2):
+            group_cols(scopy, w2_grouped[g], w2_raw[g], 0, N)
+
+        gather(1, 0, 0)
+        last_add(0, 0, V)
+        for t in range(1, J):
+            gather(1, 0, t)
+        gather(1, 1, 0)
+        quantize_cols(z_codes[0], z_scales[0], z_grouped[0], 0, V, 0)
+        for t in range(1, J):
+            gather(1, 1, t)
+        gather(1, 2, 0)
+        add(sums[1][0], prods[1][0], prods[1][1])
+        gather(1, 2, 1)
+        quantize_cols(w2_codes[0], w2_scales[0], w2_grouped[0], 0, N, 0)
+        second(0)
+        gather(1, 2, 2)
+        gather(1, 2, 3)
+        gather(1, 3, 0)
+        add(sums[1][1], sums[1][0], prods[1][2])
+        gather(1, 3, 1)
+        quantize_cols(w2_codes[1], w2_scales[1], w2_grouped[1], 0, N, 0)
+        gather(1, 3, 2)
+        gather(1, 3, 3)
+        last_add(1, 0, VH)
+        last_add(1, VH, V)
+        quantize_cols(z_codes[1], z_scales[1], z_grouped[1], 0, VH, 0)
+        quantize_cols(z_codes[1], z_scales[1], z_grouped[1], VH, V, VH)
+        second(1)
+        emit(0, nc.vector.tensor_copy, nc.sync.dma_start)
+        emit(1, nc.scalar.copy, nc.scalar.dma_start)
+        emit(2, nc.vector.tensor_copy, nc.sync.dma_start)
+        emit(3, nc.scalar.copy, nc.scalar.dma_start)

@@ -1,6 +1,7 @@
 from contextlib import ExitStack
 
 import concourse.mybir as mybir
+from concourse.masks import make_identity
 
 F32 = mybir.dt.float32
 BF16 = mybir.dt.bfloat16
@@ -9,7 +10,6 @@ U16 = mybir.dt.uint16
 U8 = mybir.dt.uint8
 FP8X4 = mybir.dt.float8_e4m3fn_x4
 MULT = mybir.AluOpType.mult
-ADD = mybir.AluOpType.add
 
 K, T, D, V, H, N = 512, 512, 4, 256, 1024, 512
 FLOPS = 2 * K * H * T + 2 * H * N * V
@@ -17,8 +17,11 @@ FLOPS = 2 * K * H * T + 2 * H * N * V
 P = 128
 J = 4
 KP = P * J
-X_V = 352
-VH = 128
+TILES = H // P
+X_CUTS = (0, 256, 384, 512)
+W2_PIECE = 128
+W1_CUTS = (0, 1, 2, 4, 8)
+H_BANK = (None, 0, 1, 6, 7, 4, 5, 0)
 
 
 def tile_picked_gcn_mlp_none_sub_l_kernel(tc, xT, w1, w2, gate, pos1, pos2, pos3, pos4, out):
@@ -26,14 +29,20 @@ def tile_picked_gcn_mlp_none_sub_l_kernel(tc, xT, w1, w2, gate, pos1, pos2, pos3
     with ExitStack() as ctx:
         lists = ctx.enter_context(tc.tile_pool(name="lists", bufs=1))
         keep = ctx.enter_context(tc.tile_pool(name="keep", bufs=1))
-        psum = ctx.enter_context(tc.psum_pool(name="psum", bufs=8))
+        psum = ctx.enter_context(tc.psum_pool(name="psum", bufs=1))
+
+        banks = [psum.tile([P, 512], F32, name=f"bank{b}") for b in range(8)]
+        sum_banks, word_banks, out_banks = [banks[2:4], banks[4:6]], banks[6:8], banks[0:4]
 
         pos = [lists.tile([P, V // 16], U16, name=f"pos{d}") for d in range(D)]
         gates = [keep.tile([P, V], F32, name=f"gate{d}") for d in range(D)]
+        ident = keep.tile([P, P], F32, name="ident")
+        make_identity(nc, ident[:])
 
-        x_raw = keep.tile([P, J, T], F32, name="x_raw")
-        w1_first = [keep.tile([P, J // 2, KP], F32, name=f"w1_first{c}") for c in range(2)]
-        w1_rest = keep.tile([P, J, KP], F32, name="w1_rest")
+        chunks = list(zip(X_CUTS[:-1], X_CUTS[1:]))
+        x_raw = [keep.tile([P, J, b - a], F32, name=f"x_raw{a}") for a, b in chunks]
+        lots = list(zip(W1_CUTS[:-1], W1_CUTS[1:]))
+        w1_raw = [keep.tile([P, J, (b - a) * P], F32, name=f"w1_raw{a}") for a, b in lots]
         w2_raw = [keep.tile([P, J, N], F32, name=f"w2_raw{g}") for g in range(2)]
 
         x_view = xT.rearrange("(p j) t -> p j t", j=J)
@@ -41,122 +50,113 @@ def tile_picked_gcn_mlp_none_sub_l_kernel(tc, xT, w1, w2, gate, pos1, pos2, pos3
         w2_view = w2.rearrange("(g p j) n -> g p j n", g=2, j=J)
         out_view = out.rearrange("(a p) v -> p a v", p=P)
 
-        nc.sync.dma_start(x_raw[:], x_view)
-        for c in range(2):
-            nc.sync.dma_start(w1_first[c][:], w1_view[:, 2 * c : 2 * c + 2, 0:KP])
+        def load_w1(q):
+            nc.sync.dma_start(w1_raw[q][:], w1_view[:, :, lots[q][0] * P : lots[q][1] * P])
+
+        load_w1(0)
+        for c, (a, b) in enumerate(chunks):
+            nc.sync.dma_start(x_raw[c][:], x_view[:, :, a:b])
+        load_w1(1)
         for d, src in enumerate((pos1, pos2, pos3, pos4)):
             nc.sync.dma_start(pos[d][:], src)
             nc.sync.dma_start(gates[d][:], gate[d])
-        nc.sync.dma_start(w1_rest[:], w1_view[:, :, KP:H])
+            if d == 1:
+                load_w1(2)
+        load_w1(3)
         for g in range(2):
             nc.sync.dma_start(w2_raw[g][:], w2_view[g])
 
-        w1_grouped = [keep.tile([P, J, P, J], BF16, name=f"w1_grouped{g}", align_bytes=64) for g in range(2)]
-        w1_codes = [keep.tile([P, J, P], U32, name=f"w1_codes{g}", align_bytes=64) for g in range(2)]
-        w1_scales = [keep.tile([P, J, P], U8, name=f"w1_scales{g}", align_bytes=64) for g in range(2)]
-        x_grouped = keep.tile([P, T, J], BF16, name="x_grouped", align_bytes=64)
+        w1_grouped = [keep.tile([P, (b - a) * P, J], BF16, name=f"w1_grouped{a}", align_bytes=64) for a, b in lots]
+        w1_codes = keep.tile([P, H], U32, name="w1_codes", align_bytes=64)
+        w1_scales = keep.tile([P, H], U8, name="w1_scales", align_bytes=64)
+        x_grouped = [keep.tile([P, b - a, J], BF16, name=f"x_grouped{a}", align_bytes=64) for a, b in chunks]
         x_codes = keep.tile([P, T], U32, name="x_codes", align_bytes=64)
         x_scales = keep.tile([P, T], U8, name="x_scales", align_bytes=64)
         w2_grouped = [keep.tile([P, N, J], BF16, name=f"w2_grouped{g}", align_bytes=64) for g in range(2)]
         w2_codes = [keep.tile([P, N], U32, name=f"w2_codes{g}", align_bytes=64) for g in range(2)]
         w2_scales = [keep.tile([P, N], U8, name=f"w2_scales{g}", align_bytes=64) for g in range(2)]
-
-        def group_w1_first(copy, c, t):
-            copy(
-                out=w1_grouped[0][:, t, :, 2 * c : 2 * c + 2],
-                in_=w1_first[c][:].rearrange("p j (m t) -> p t m j", t=J)[:, t, :, :],
-            )
-
-        def group_w1_rest(copy, ma, mb):
-            copy(
-                out=w1_grouped[1][:, :, ma:mb, :].rearrange("p t m j -> p m j t"),
-                in_=w1_rest[:, :, J * ma : J * mb].rearrange("p j (m t) -> p m j t", t=J),
-            )
-
-        def quantize_w1(g, t0, t1):
-            nc.vector.quantize_mx(
-                out=w1_codes[g][:, t0:t1, :].rearrange("p t m -> p (t m)").bitcast(FP8X4),
-                scales=w1_scales[g][:, t0:t1, :].rearrange("p t m -> p (t m)"),
-                in_=w1_grouped[g][:, t0:t1, :, :].rearrange("p t m j -> p (t m j)"),
-            )
-
-        def group_cols(copy, dst, src, a, b):
-            copy(
-                out=dst[:, a:b, :].rearrange("p (c i) j -> p c j i", i=4),
-                in_=src[:, :, a:b].rearrange("p j (c i) -> p c j i", i=4),
-            )
-
-        def quantize_cols(codes, scales, grouped, c0, c1, g0):
-            nc.vector.quantize_mx(
-                out=codes[:, c0:c1].bitcast(FP8X4),
-                scales=scales[:, c0:c1],
-                in_=grouped[:, g0 : g0 + c1 - c0, :].rearrange("p n j -> p (n j)"),
-            )
-
-        vcopy, scopy = nc.vector.tensor_copy, nc.scalar.copy
-
-        h = [[keep.tile([P, T], F32, name=f"h{g}_{t}") for t in range(J)] for g in range(2)]
-
-        def project(g, t, n0, n1, copy=nc.scalar.copy):
-            bank = psum.tile([P, 512], F32, name="bank")
-            nc.tensor.matmul_mx(
-                out=bank[:, : n1 - n0],
-                lhsT=w1_codes[g][:, t, :].bitcast(FP8X4),
-                lhsT_scale=w1_scales[g][:, t, :],
-                rhs=x_codes[:, n0:n1].bitcast(FP8X4),
-                rhs_scale=x_scales[:, n0:n1],
-                start=True,
-                stop=True,
-            )
-            copy(out=h[g][t][:, n0:n1], in_=bank[:, : n1 - n0])
-
-        group_cols(vcopy, x_grouped, x_raw, 0, X_V)
-        group_cols(scopy, x_grouped, x_raw, X_V, T)
-        for n in range(2):
-            quantize_cols(x_codes, x_scales, x_grouped, n * 256, (n + 1) * 256, n * 256)
-        for t in range(J):
-            group_w1_first(vcopy if t < 2 else scopy, 0, t)
-        group_w1_first(vcopy, 1, 0)
-        quantize_w1(0, 0, 1)
-        group_w1_first(scopy, 1, 1)
-        project(0, 0, 0, 256)
-        project(0, 0, 256, 512, vcopy)
-        quantize_w1(0, 1, 2)
-        group_w1_first(scopy, 1, 2)
-        project(0, 1, 0, T)
-        group_w1_first(scopy, 1, 3)
-
-        prods = [[keep.tile([P, J, V], F32, name=f"prod{g}_{d}") for d in range(D)] for g in range(2)]
-        sums = [[keep.tile([P, J, V], F32, name=f"sum{g}_{s}") for s in range(2)] for g in range(2)]
+        h = [keep.tile([P, T], F32, name=f"h{i}") for i in range(TILES)]
+        prods = [[keep.tile([P, V], F32, name=f"prod{i}_{d}")[:] if i in (0, 2, 5) else None for d in range(D)] for i in range(TILES)]
+        z_turned = [[keep.tile([P, 2, P, 2], BF16, name=f"z_turned{g}_{s}") for s in range(2)] for g in range(2)]
         z_grouped = [keep.tile([P, V, J], BF16, name=f"z_grouped{g}", align_bytes=64) for g in range(2)]
+        for d in range(D):
+            prods[1][d] = w1_raw[2][:, d, :]
+            prods[3][d] = w1_raw[3][:, d, V:]
+            prods[4][d] = w2_raw[0][:, d, V:]
+            prods[6][d] = z_turned[0][d][:].rearrange("v u p e -> v (u p e)").bitcast(F32) if d < 2 else w2_raw[1][:, d, V:]
+            prods[7][d] = w2_grouped[1][:, d * P : (d + 1) * P, :].rearrange("p n j -> p (n j)").bitcast(F32)
         z_codes = [keep.tile([P, V], U32, name=f"z_codes{g}", align_bytes=64) for g in range(2)]
         z_scales = [keep.tile([P, V], U8, name=f"z_scales{g}", align_bytes=64) for g in range(2)]
 
-        def gather(g, d, t, v0=0, v1=V):
-            offs = pos[d][:] if v1 - v0 == V else pos[d][:, v0 // 16 : v1 // 16]
-            nc.vector.tensor_tensor(prods[g][d][:, t, v0:v1], h[g][t][:].indirect(offs), gates[d][:, v0:v1], MULT)
+        vcopy, scopy = nc.vector.tensor_copy, nc.scalar.copy
 
-        def add(dst, a, b):
-            nc.vector.tensor_tensor(
-                dst[:].rearrange("p t v -> p (t v)"), a[:].rearrange("p t v -> p (t v)"), b[:].rearrange("p t v -> p (t v)"), ADD
+        def group(copy, dst, src):
+            copy(out=dst.rearrange("p (c i) j -> p c j i", i=4), in_=src.rearrange("p j (c i) -> p c j i", i=4))
+
+        def quantize(codes, scales, grouped):
+            nc.vector.quantize_mx(out=codes.bitcast(FP8X4), scales=scales, in_=grouped.rearrange("p n j -> p (n j)"))
+
+        def prepare_w1(q):
+            a, b = lots[q]
+            for c in range(0, (b - a) * P, P):
+                group(scopy, w1_grouped[q][:, c : c + P, :], w1_raw[q][:, :, c : c + P])
+            quantize(w1_codes[:, a * P : b * P], w1_scales[:, a * P : b * P], w1_grouped[q][:])
+
+        def group_w2(piece):
+            g, a = divmod(piece * W2_PIECE, N)
+            group(scopy, w2_grouped[g][:, a : a + W2_PIECE, :], w2_raw[g][:, :, a : a + W2_PIECE])
+
+        def project(i, a, b, bank, copy):
+            nc.tensor.matmul_mx(
+                out=bank[:, : b - a],
+                lhsT=w1_codes[:, i * P : (i + 1) * P].bitcast(FP8X4),
+                lhsT_scale=w1_scales[:, i * P : (i + 1) * P],
+                rhs=x_codes[:, a:b].bitcast(FP8X4),
+                rhs_scale=x_scales[:, a:b],
+                start=True,
+                stop=True,
+            )
+            copy(out=h[i][:, a:b], in_=bank[:, : b - a])
+
+        def banks_of(i):
+            return word_banks if i == TILES - 1 else sum_banks[i // J]
+
+        def gather_and_add(i):
+            t = i % J
+            for d in range(D):
+                nc.vector.tensor_tensor(prods[i][d], h[i][:].indirect(pos[d][:]), gates[d][:], MULT)
+                for s in range(2):
+                    nc.tensor.matmul(
+                        banks_of(i)[s][:, t * P : (t + 1) * P],
+                        lhsT=prods[i][d][:, s * P : (s + 1) * P],
+                        rhs=ident[:],
+                        start=(d == 0),
+                        stop=(d == D - 1),
+                        is_transpose=True,
+                    )
+
+        def round_sums(i0, i1, s, copy):
+            g, t0, t1 = i0 // J, i0 % J, (i1 - 1) % J + 1
+            copy(
+                out=z_turned[g][s][:, :, 32 * t0 : 32 * t1, :],
+                in_=banks_of(i0)[s][:, t0 * P : t1 * P].rearrange("v (p u e) -> v u p e", u=2, e=2),
             )
 
-        def last_add(g, v0, v1):
-            nc.vector.tensor_tensor(
-                z_grouped[g][:, v0:v1, :].rearrange("p (c i) t -> p c t i", i=4),
-                sums[g][1][:, :, v0:v1].rearrange("p t (c i) -> p c t i", i=4),
-                prods[g][3][:, :, v0:v1].rearrange("p t (c i) -> p c t i", i=4),
-                ADD,
+        def turn_back(g, s, copy):
+            bank = word_banks[s]
+            for u in range(2):
+                nc.tensor.transpose(
+                    bank[:, u * P : (u + 1) * P], z_turned[g][s][:, u, :, :].rearrange("v p e -> v (p e)").bitcast(F32), ident[:]
+                )
+            copy(
+                out=z_grouped[g][:, s * P : (s + 1) * P, :].rearrange("p v j -> p (v j)").bitcast(F32).rearrange("p (v u) -> p v u", u=2),
+                in_=bank[:, : 2 * P].rearrange("p (u v) -> p v u", u=2),
             )
-
-        acc = {}
 
         def second(g):
             for a in range(N // P):
-                if g == 0:
-                    acc[a] = psum.tile([P, 512], F32, name="bank")
                 nc.tensor.matmul_mx(
-                    out=acc[a][:, :V],
+                    out=out_banks[a][:, :V],
                     lhsT=w2_codes[g][:, a * P : (a + 1) * P].bitcast(FP8X4),
                     lhsT_scale=w2_scales[g][:, a * P : (a + 1) * P],
                     rhs=z_codes[g][:].bitcast(FP8X4),
@@ -167,61 +167,55 @@ def tile_picked_gcn_mlp_none_sub_l_kernel(tc, xT, w1, w2, gate, pos1, pos2, pos3
 
         def emit(a, copy, dma):
             o = keep.tile([P, V], F32, name=f"o{a}")
-            copy(out=o[:], in_=acc[a][:, :V])
+            copy(out=o[:], in_=out_banks[a][:, :V])
             dma(out=out_view[:, a, :], in_=o[:])
 
-        gather(0, 0, 0)
-        gather(0, 1, 0)
-        quantize_w1(0, 2, 4)
-        for t in (2, 3):
-            project(0, t, 0, T)
-        for t in range(1, J):
-            for d in range(2):
-                gather(0, d, t)
-        for m in range(0, P, 64):
-            group_w1_rest(scopy, m, m + 64)
-        gather(0, 2, 0)
-        add(sums[0][0], prods[0][0], prods[0][1])
-        for t in range(1, J):
-            gather(0, 2, t)
-        gather(0, 3, 0)
-        add(sums[0][1], sums[0][0], prods[0][2])
-        gather(0, 3, 1)
-        quantize_w1(1, 0, J)
-        for t in range(J):
-            project(1, t, 0, T)
-        gather(0, 3, 2)
-        gather(0, 3, 3)
-        for g in range(2):
-            group_cols(scopy, w2_grouped[g], w2_raw[g], 0, N)
+        prepare_w1(0)
+        for c, (a, b) in enumerate(chunks):
+            group(scopy if c == 1 else vcopy, x_grouped[c][:], x_raw[c][:])
+            quantize(x_codes[:, a:b], x_scales[:, a:b], x_grouped[c][:])
+        for c, (a, b) in enumerate(chunks):
+            project(0, a, b, banks[(1, 6, 7)[c]], vcopy if c == 2 else scopy)
+        prepare_w1(1)
 
-        gather(1, 0, 0)
-        last_add(0, 0, V)
-        for t in range(1, J):
-            gather(1, 0, t)
-        gather(1, 1, 0)
-        quantize_cols(z_codes[0], z_scales[0], z_grouped[0], 0, V, 0)
-        for t in range(1, J):
-            gather(1, 1, t)
-        gather(1, 2, 0)
-        add(sums[1][0], prods[1][0], prods[1][1])
-        gather(1, 2, 1)
-        quantize_cols(w2_codes[0], w2_scales[0], w2_grouped[0], 0, N, 0)
+        project(1, 0, T, banks[H_BANK[1]], scopy)
+        gather_and_add(0)
+        prepare_w1(2)
+        project(2, 0, T, banks[H_BANK[2]], scopy)
+        project(3, 0, T, banks[H_BANK[3]], scopy)
+        gather_and_add(1)
+        prepare_w1(3)
+        gather_and_add(2)
+        for piece in range(4):
+            group_w2(piece)
+        for i in range(4, TILES):
+            project(i, 0, T, banks[H_BANK[i]], scopy)
+        gather_and_add(3)
+        quantize(w2_codes[0][:], w2_scales[0][:], w2_grouped[0][:])
+        gather_and_add(4)
+        for s in range(2):
+            round_sums(0, J, s, scopy)
+        group_w2(4)
+        group_w2(5)
+        for s in range(2):
+            turn_back(0, s, scopy)
+        group_w2(6)
+        group_w2(7)
+        gather_and_add(5)
+        quantize(z_codes[0][:], z_scales[0][:], z_grouped[0][:])
+        quantize(w2_codes[1][:], w2_scales[1][:], w2_grouped[1][:])
         second(0)
-        gather(1, 2, 2)
-        gather(1, 2, 3)
-        gather(1, 3, 0)
-        add(sums[1][1], sums[1][0], prods[1][2])
-        gather(1, 3, 1)
-        quantize_cols(w2_codes[1], w2_scales[1], w2_grouped[1], 0, N, 0)
-        gather(1, 3, 2)
-        gather(1, 3, 3)
-        last_add(1, 0, VH)
-        last_add(1, VH, V)
-        quantize_cols(z_codes[1], z_scales[1], z_grouped[1], 0, VH, 0)
-        quantize_cols(z_codes[1], z_scales[1], z_grouped[1], VH, V, VH)
+        gather_and_add(6)
+        for s in range(2):
+            round_sums(J, TILES - 1, s, scopy)
+        gather_and_add(7)
+        round_sums(TILES - 1, TILES, 0, scopy)
+        round_sums(TILES - 1, TILES, 1, vcopy)
+        turn_back(1, 0, scopy)
+        turn_back(1, 1, vcopy)
+        quantize(z_codes[1][:], z_scales[1][:], z_grouped[1][:])
         second(1)
-        emit(0, nc.vector.tensor_copy, nc.sync.dma_start)
-        emit(1, nc.scalar.copy, nc.scalar.dma_start)
-        emit(2, nc.vector.tensor_copy, nc.sync.dma_start)
-        emit(3, nc.scalar.copy, nc.scalar.dma_start)
+        emit(0, vcopy, nc.sync.dma_start)
+        emit(1, scopy, nc.scalar.dma_start)
+        emit(2, vcopy, nc.sync.dma_start)
+        emit(3, scopy, nc.scalar.dma_start)

@@ -19,9 +19,11 @@ J = 4
 KP = P * J
 TILES = H // P
 X_CUTS = (0, 256, 384, 512)
+X_VECTOR = (256, 0, 128)
 W2_PIECE = 128
-W1_CUTS = (0, 1, 2, 4, 8)
-H_BANK = (None, 0, 1, 6, 7, 4, 5, 0)
+H_BYTES = ("h0", "w1_raw2", "w1_raw3", "h3", "w1_raw5", "h5", "w2_raw0", "w2_raw1")
+W1_CUTS = (0, 1, 2, 3, 5, 8)
+H_BANK = (None, 0, 1, 6, 7, 4, 5, 6)
 
 
 def tile_picked_gcn_mlp_none_sub_l_kernel(tc, xT, w1, w2, gate, pos1, pos2, pos3, pos4, out):
@@ -32,18 +34,19 @@ def tile_picked_gcn_mlp_none_sub_l_kernel(tc, xT, w1, w2, gate, pos1, pos2, pos3
         psum = ctx.enter_context(tc.psum_pool(name="psum", bufs=1))
 
         banks = [psum.tile([P, 512], F32, name=f"bank{b}") for b in range(8)]
-        sum_banks, word_banks, out_banks = [banks[2:4], banks[4:6]], banks[6:8], banks[0:4]
+        sum_banks, word_banks, out_banks = banks[2:4], banks[6:8], banks[0:2] + banks[4:6]
 
         pos = [lists.tile([P, V // 16], U16, name=f"pos{d}") for d in range(D)]
-        gates = [keep.tile([P, V], F32, name=f"gate{d}") for d in range(D)]
+        gate_pairs = [keep.tile([P, 2, V], F32, name=f"gates{q}") for q in range(2)]
+        gates = [gate_pairs[d // 2][:, d % 2, :] for d in range(D)]
         ident = keep.tile([P, P], F32, name="ident")
         make_identity(nc, ident[:])
 
         chunks = list(zip(X_CUTS[:-1], X_CUTS[1:]))
         x_raw = [keep.tile([P, J, b - a], F32, name=f"x_raw{a}") for a, b in chunks]
         lots = list(zip(W1_CUTS[:-1], W1_CUTS[1:]))
-        w1_raw = [keep.tile([P, J, (b - a) * P], F32, name=f"w1_raw{a}") for a, b in lots]
-        w2_raw = [keep.tile([P, J, N], F32, name=f"w2_raw{g}") for g in range(2)]
+        w1_raw = [keep.tile([P, J, (b - a) * P], F32, name=f"w1_raw{a}", tag=f"w1_raw{a}", align_bytes=64) for a, b in lots]
+        w2_raw = [keep.tile([P, J, N], F32, name=f"w2_raw{g}", tag=f"w2_raw{g}", align_bytes=64) for g in range(2)]
 
         x_view = xT.rearrange("(p j) t -> p j t", j=J)
         w1_view = w1.rearrange("(p j) i -> p j i", j=J)
@@ -57,12 +60,16 @@ def tile_picked_gcn_mlp_none_sub_l_kernel(tc, xT, w1, w2, gate, pos1, pos2, pos3
         for c, (a, b) in enumerate(chunks):
             nc.sync.dma_start(x_raw[c][:], x_view[:, :, a:b])
         load_w1(1)
-        for d, src in enumerate((pos1, pos2, pos3, pos4)):
-            nc.sync.dma_start(pos[d][:], src)
-            nc.sync.dma_start(gates[d][:], gate[d])
-            if d == 1:
-                load_w1(2)
+        gate_view = gate.rearrange("(q e) p v -> q p e v", e=2)
+        nc.sync.dma_start(pos[0][:], pos1)
+        nc.sync.dma_start(pos[1][:], pos2)
+        nc.sync.dma_start(gate_pairs[0][:], gate_view[0])
+        load_w1(2)
+        nc.sync.dma_start(gate_pairs[1][:], gate_view[1])
+        nc.sync.dma_start(pos[2][:], pos3)
+        nc.sync.dma_start(pos[3][:], pos4)
         load_w1(3)
+        load_w1(4)
         for g in range(2):
             nc.sync.dma_start(w2_raw[g][:], w2_view[g])
 
@@ -73,18 +80,12 @@ def tile_picked_gcn_mlp_none_sub_l_kernel(tc, xT, w1, w2, gate, pos1, pos2, pos3
         x_codes = keep.tile([P, T], U32, name="x_codes", align_bytes=64)
         x_scales = keep.tile([P, T], U8, name="x_scales", align_bytes=64)
         w2_grouped = [keep.tile([P, N, J], BF16, name=f"w2_grouped{g}", align_bytes=64) for g in range(2)]
-        w2_codes = [keep.tile([P, N], U32, name=f"w2_codes{g}", align_bytes=64) for g in range(2)]
+        w2_codes = [keep.tile([P, N], U32, name="w2_codes0", align_bytes=64)]
         w2_scales = [keep.tile([P, N], U8, name=f"w2_scales{g}", align_bytes=64) for g in range(2)]
-        h = [keep.tile([P, T], F32, name=f"h{i}") for i in range(TILES)]
-        prods = [[keep.tile([P, V], F32, name=f"prod{i}_{d}")[:] if i in (0, 2, 5) else None for d in range(D)] for i in range(TILES)]
-        z_turned = [[keep.tile([P, 2, P, 2], BF16, name=f"z_turned{g}_{s}") for s in range(2)] for g in range(2)]
+        h = {}
+        prods = [[keep.tile([P, V], F32, name=f"prod{i}_{d}")[:] for d in range(D)] for i in range(TILES)]
+        z_turned = {1: keep.tile([P, 2, 2, P, 2], BF16, name="z_turned1")}
         z_grouped = [keep.tile([P, V, J], BF16, name=f"z_grouped{g}", align_bytes=64) for g in range(2)]
-        for d in range(D):
-            prods[1][d] = w1_raw[2][:, d, :]
-            prods[3][d] = w1_raw[3][:, d, V:]
-            prods[4][d] = w2_raw[0][:, d, V:]
-            prods[6][d] = z_turned[0][d][:].rearrange("v u p e -> v (u p e)").bitcast(F32) if d < 2 else w2_raw[1][:, d, V:]
-            prods[7][d] = w2_grouped[1][:, d * P : (d + 1) * P, :].rearrange("p n j -> p (n j)").bitcast(F32)
         z_codes = [keep.tile([P, V], U32, name=f"z_codes{g}", align_bytes=64) for g in range(2)]
         z_scales = [keep.tile([P, V], U8, name=f"z_scales{g}", align_bytes=64) for g in range(2)]
 
@@ -100,13 +101,17 @@ def tile_picked_gcn_mlp_none_sub_l_kernel(tc, xT, w1, w2, gate, pos1, pos2, pos3
             a, b = lots[q]
             for c in range(0, (b - a) * P, P):
                 group(scopy, w1_grouped[q][:, c : c + P, :], w1_raw[q][:, :, c : c + P])
-            quantize(w1_codes[:, a * P : b * P], w1_scales[:, a * P : b * P], w1_grouped[q][:])
+            for i in range(a, b, 2):
+                e = min(i + 2, b)
+                quantize(w1_codes[:, i * P : e * P], w1_scales[:, i * P : e * P], w1_grouped[q][:, (i - a) * P : (e - a) * P, :])
 
         def group_w2(piece):
             g, a = divmod(piece * W2_PIECE, N)
             group(scopy, w2_grouped[g][:, a : a + W2_PIECE, :], w2_raw[g][:, :, a : a + W2_PIECE])
 
         def project(i, a, b, bank, copy):
+            if i not in h:
+                h[i] = keep.tile([P, T], F32, name=f"h{i}", tag=H_BYTES[i], align_bytes=64)
             nc.tensor.matmul_mx(
                 out=bank[:, : b - a],
                 lhsT=w1_codes[:, i * P : (i + 1) * P].bitcast(FP8X4),
@@ -119,13 +124,15 @@ def tile_picked_gcn_mlp_none_sub_l_kernel(tc, xT, w1, w2, gate, pos1, pos2, pos3
             copy(out=h[i][:, a:b], in_=bank[:, : b - a])
 
         def banks_of(i):
-            return word_banks if i == TILES - 1 else sum_banks[i // J]
+            return word_banks if i == TILES - 1 else sum_banks
 
-        def gather_and_add(i):
+        def gather_and_add(i, steps=tuple((d, (0, 1)) for d in range(D))):
             t = i % J
-            for d in range(D):
-                nc.vector.tensor_tensor(prods[i][d], h[i][:].indirect(pos[d][:]), gates[d][:], MULT)
-                for s in range(2):
+            for d, halves in steps:
+                v0, v1 = halves[0] * P, (halves[-1] + 1) * P
+                offsets = pos[d][:, v0 // 16 : v1 // 16]
+                nc.vector.tensor_tensor(prods[i][d][:, v0:v1], h[i][:].indirect(offsets), gates[d][:, v0:v1], MULT)
+                for s in halves:
                     nc.tensor.matmul(
                         banks_of(i)[s][:, t * P : (t + 1) * P],
                         lhsT=prods[i][d][:, s * P : (s + 1) * P],
@@ -138,7 +145,7 @@ def tile_picked_gcn_mlp_none_sub_l_kernel(tc, xT, w1, w2, gate, pos1, pos2, pos3
         def round_sums(i0, i1, s, copy):
             g, t0, t1 = i0 // J, i0 % J, (i1 - 1) % J + 1
             copy(
-                out=z_turned[g][s][:, :, 32 * t0 : 32 * t1, :],
+                out=z_turned[g][:, s, :, 32 * t0 : 32 * t1, :],
                 in_=banks_of(i0)[s][:, t0 * P : t1 * P].rearrange("v (p u e) -> v u p e", u=2, e=2),
             )
 
@@ -146,23 +153,23 @@ def tile_picked_gcn_mlp_none_sub_l_kernel(tc, xT, w1, w2, gate, pos1, pos2, pos3
             bank = word_banks[s]
             for u in range(2):
                 nc.tensor.transpose(
-                    bank[:, u * P : (u + 1) * P], z_turned[g][s][:, u, :, :].rearrange("v p e -> v (p e)").bitcast(F32), ident[:]
+                    bank[:, u * P : (u + 1) * P], z_turned[g][:, s, u, :, :].rearrange("v p e -> v (p e)").bitcast(F32), ident[:]
                 )
             copy(
                 out=z_grouped[g][:, s * P : (s + 1) * P, :].rearrange("p v j -> p (v j)").bitcast(F32).rearrange("p (v u) -> p v u", u=2),
                 in_=bank[:, : 2 * P].rearrange("p (u v) -> p v u", u=2),
             )
 
-        def second(g):
+        def second(g, v0, v1):
             for a in range(N // P):
                 nc.tensor.matmul_mx(
-                    out=out_banks[a][:, :V],
+                    out=out_banks[a][:, v0:v1],
                     lhsT=w2_codes[g][:, a * P : (a + 1) * P].bitcast(FP8X4),
                     lhsT_scale=w2_scales[g][:, a * P : (a + 1) * P],
-                    rhs=z_codes[g][:].bitcast(FP8X4),
-                    rhs_scale=z_scales[g][:],
+                    rhs=z_codes[g][:, v0:v1].bitcast(FP8X4),
+                    rhs_scale=z_scales[g][:, v0:v1],
                     start=(g == 0),
-                    stop=(g == 1),
+                    stop=(g == 1 and v1 == V),
                 )
 
         def emit(a, copy, dma):
@@ -172,49 +179,61 @@ def tile_picked_gcn_mlp_none_sub_l_kernel(tc, xT, w1, w2, gate, pos1, pos2, pos3
 
         prepare_w1(0)
         for c, (a, b) in enumerate(chunks):
-            group(scopy if c == 1 else vcopy, x_grouped[c][:], x_raw[c][:])
+            cut = X_VECTOR[c]
+            if cut > 0:
+                group(vcopy, x_grouped[c][:, :cut, :], x_raw[c][:, :, :cut])
+            if cut < b - a:
+                group(scopy, x_grouped[c][:, cut:, :], x_raw[c][:, :, cut:])
             quantize(x_codes[:, a:b], x_scales[:, a:b], x_grouped[c][:])
         for c, (a, b) in enumerate(chunks):
             project(0, a, b, banks[(1, 6, 7)[c]], vcopy if c == 2 else scopy)
         prepare_w1(1)
 
-        project(1, 0, T, banks[H_BANK[1]], scopy)
-        gather_and_add(0)
-        prepare_w1(2)
-        project(2, 0, T, banks[H_BANK[2]], scopy)
-        project(3, 0, T, banks[H_BANK[3]], scopy)
-        gather_and_add(1)
-        prepare_w1(3)
-        gather_and_add(2)
-        for piece in range(4):
-            group_w2(piece)
-        for i in range(4, TILES):
+        def project_all(i):
             project(i, 0, T, banks[H_BANK[i]], scopy)
+
+        prepare_w1(2)
+        project_all(1)
+        gather_and_add(0)
+        prepare_w1(3)
+        project_all(2)
+        gather_and_add(1)
+        prepare_w1(4)
+        project_all(3)
+        gather_and_add(2)
+        group_w2(0)
+        group_w2(1)
+        project_all(4)
+        project_all(5)
         gather_and_add(3)
+        group_w2(2)
+        group_w2(3)
         quantize(w2_codes[0][:], w2_scales[0][:], w2_grouped[0][:])
-        gather_and_add(4)
+        z_turned[0] = keep.tile([P, 2, 2, P, 2], BF16, name="z_turned0", tag="w2_raw0", align_bytes=64)
         for s in range(2):
             round_sums(0, J, s, scopy)
-        group_w2(4)
-        group_w2(5)
         for s in range(2):
             turn_back(0, s, scopy)
-        group_w2(6)
-        group_w2(7)
-        gather_and_add(5)
         quantize(z_codes[0][:], z_scales[0][:], z_grouped[0][:])
-        quantize(w2_codes[1][:], w2_scales[1][:], w2_grouped[1][:])
-        second(0)
+        project_all(6)
+        second(0, 0, V)
+        gather_and_add(4)
+        for piece in range(4, 8):
+            group_w2(piece)
+        project_all(7)
+        gather_and_add(5)
         gather_and_add(6)
         for s in range(2):
             round_sums(J, TILES - 1, s, scopy)
-        gather_and_add(7)
-        round_sums(TILES - 1, TILES, 0, scopy)
-        round_sums(TILES - 1, TILES, 1, vcopy)
-        turn_back(1, 0, scopy)
-        turn_back(1, 1, vcopy)
-        quantize(z_codes[1][:], z_scales[1][:], z_grouped[1][:])
-        second(1)
+        gather_and_add(7, ((0, (0, 1)), (1, (0, 1)), (2, (0,)), (3, (0,)), (2, (1,)), (3, (1,))))
+        w2_codes.append(keep.tile([P, N], U32, name="w2_codes1", tag=H_BYTES[TILES - 1], align_bytes=64))
+        quantize(w2_codes[1][:], w2_scales[1][:], w2_grouped[1][:])
+        for s in range(2):
+            round_sums(TILES - 1, TILES, s, scopy)
+            turn_back(1, s, scopy)
+            quantize(z_codes[1][:, s * P : (s + 1) * P], z_scales[1][:, s * P : (s + 1) * P], z_grouped[1][:, s * P : (s + 1) * P, :])
+        for s in range(2):
+            second(1, s * P, (s + 1) * P)
         emit(0, vcopy, nc.sync.dma_start)
         emit(1, scopy, nc.scalar.dma_start)
         emit(2, vcopy, nc.sync.dma_start)

@@ -19,7 +19,7 @@ J = 4
 KP = P * J
 TILES = H // P
 X_CUTS = (0, 256, 384, 512)
-X_VECTOR = (256, 0, 128)
+X_VECTOR = (160, 0, 128)
 W2_PIECE = 128
 H_BYTES = ("h0", "w1_raw2", "w1_raw3", "h3", "w1_raw5", "h5", "w2_raw0", "w2_raw1")
 W1_CUTS = (0, 1, 2, 3, 5, 8)
@@ -80,13 +80,11 @@ def tile_picked_gcn_mlp_none_sub_l_kernel(tc, xT, w1, w2, gate, pos1, pos2, pos3
         x_codes = keep.tile([P, T], U32, name="x_codes", align_bytes=64)
         x_scales = keep.tile([P, T], U8, name="x_scales", align_bytes=64)
         w2_grouped = [keep.tile([P, N, J], BF16, name=f"w2_grouped{g}", align_bytes=64) for g in range(2)]
-        w2_codes = [keep.tile([P, N], U32, name="w2_codes0", align_bytes=64)]
         w2_scales = [keep.tile([P, N], U8, name=f"w2_scales{g}", align_bytes=64) for g in range(2)]
         h = {}
         prods = [[keep.tile([P, V], F32, name=f"prod{i}_{d}")[:] for d in range(D)] for i in range(TILES)]
         z_turned = {1: keep.tile([P, 2, 2, P, 2], BF16, name="z_turned1")}
         z_grouped = [keep.tile([P, V, J], BF16, name=f"z_grouped{g}", align_bytes=64) for g in range(2)]
-        z_codes = [keep.tile([P, V], U32, name=f"z_codes{g}", align_bytes=64) for g in range(2)]
         z_scales = [keep.tile([P, V], U8, name=f"z_scales{g}", align_bytes=64) for g in range(2)]
 
         vcopy, scopy = nc.vector.tensor_copy, nc.scalar.copy
@@ -208,15 +206,12 @@ def tile_picked_gcn_mlp_none_sub_l_kernel(tc, xT, w1, w2, gate, pos1, pos2, pos3
         gather_and_add(3)
         group_w2(2)
         group_w2(3)
-        quantize(w2_codes[0][:], w2_scales[0][:], w2_grouped[0][:])
         z_turned[0] = keep.tile([P, 2, 2, P, 2], BF16, name="z_turned0", tag="w2_raw0", align_bytes=64)
         for s in range(2):
             round_sums(0, J, s, scopy)
         for s in range(2):
             turn_back(0, s, scopy)
-        quantize(z_codes[0][:], z_scales[0][:], z_grouped[0][:])
         project_all(6)
-        second(0, 0, V)
         gather_and_add(4)
         for piece in range(4, 8):
             group_w2(piece)
@@ -226,15 +221,19 @@ def tile_picked_gcn_mlp_none_sub_l_kernel(tc, xT, w1, w2, gate, pos1, pos2, pos3
         for s in range(2):
             round_sums(J, TILES - 1, s, scopy)
         gather_and_add(7, ((0, (0, 1)), (1, (0, 1)), (2, (0,)), (3, (0,)), (2, (1,)), (3, (1,))))
-        w2_codes.append(keep.tile([P, N], U32, name="w2_codes1", tag=H_BYTES[TILES - 1], align_bytes=64))
-        quantize(w2_codes[1][:], w2_scales[1][:], w2_grouped[1][:])
+        late = keep.tile([P, 2 * N + V], U32, name="late_codes", tag=H_BYTES[TILES - 1], align_bytes=64)
+        w2_codes = [late[:, g * N : (g + 1) * N] for g in range(2)]
+        z_codes = [late[:, 2 * N :], keep.tile([P, V], U32, name="z_codes1", align_bytes=64)[:]]
+        quantize(z_codes[0], z_scales[0][:], z_grouped[0][:])
+        for g in range(2):
+            quantize(w2_codes[g], w2_scales[g][:], w2_grouped[g][:])
         for s in range(2):
             round_sums(TILES - 1, TILES, s, scopy)
             turn_back(1, s, scopy)
             quantize(z_codes[1][:, s * P : (s + 1) * P], z_scales[1][:, s * P : (s + 1) * P], z_grouped[1][:, s * P : (s + 1) * P, :])
-        for s in range(2):
-            second(1, s * P, (s + 1) * P)
+        for g in range(2):
+            second(g, 0, V)
         emit(0, vcopy, nc.sync.dma_start)
-        emit(1, scopy, nc.scalar.dma_start)
+        emit(1, scopy, nc.sync.dma_start)
         emit(2, vcopy, nc.sync.dma_start)
         emit(3, scopy, nc.scalar.dma_start)

@@ -19,7 +19,7 @@ J = 4
 KP = P * J
 TILES = H // P
 X_CUTS = (0, 256, 384, 512)
-X_VECTOR = (160, 0, 128)
+X_VECTOR = (208, 0, 128)
 W2_PIECE = 128
 H_BYTES = ("h0", "w1_raw2", "w1_raw3", "h3", "w1_raw5", "h5", "w2_raw0", "w2_raw1")
 W1_CUTS = (0, 1, 2, 3, 5, 8)
@@ -43,7 +43,9 @@ def tile_picked_gcn_mlp_none_sub_l_kernel(tc, xT, w1, w2, gate, pos1, pos2, pos3
         make_identity(nc, ident[:])
 
         chunks = list(zip(X_CUTS[:-1], X_CUTS[1:]))
-        x_raw = [keep.tile([P, J, b - a], F32, name=f"x_raw{a}") for a, b in chunks]
+        x_first = keep.tile([P, J, X_CUTS[2]], F32, name="x_first")
+        x_last = keep.tile([P, J, T - X_CUTS[2]], F32, name="x_last")
+        x_raw = [x_first[:, :, : X_CUTS[1]], x_first[:, :, X_CUTS[1] :], x_last[:]]
         lots = list(zip(W1_CUTS[:-1], W1_CUTS[1:]))
         w1_raw = [keep.tile([P, J, (b - a) * P], F32, name=f"w1_raw{a}", tag=f"w1_raw{a}", align_bytes=64) for a, b in lots]
         w2_raw = [keep.tile([P, J, N], F32, name=f"w2_raw{g}", tag=f"w2_raw{g}", align_bytes=64) for g in range(2)]
@@ -57,8 +59,8 @@ def tile_picked_gcn_mlp_none_sub_l_kernel(tc, xT, w1, w2, gate, pos1, pos2, pos3
             nc.sync.dma_start(w1_raw[q][:], w1_view[:, :, lots[q][0] * P : lots[q][1] * P])
 
         load_w1(0)
-        for c, (a, b) in enumerate(chunks):
-            nc.sync.dma_start(x_raw[c][:], x_view[:, :, a:b])
+        nc.sync.dma_start(x_first[:], x_view[:, :, : X_CUTS[2]])
+        nc.sync.dma_start(x_last[:], x_view[:, :, X_CUTS[2] :])
         load_w1(1)
         gate_view = gate.rearrange("(q e) p v -> q p e v", e=2)
         nc.sync.dma_start(pos[0][:], pos1)

@@ -16,14 +16,21 @@ FLOPS = 2 * K * H * T + 2 * H * N * V
 
 P = 128
 J = 4
-KP = P * J
 TILES = H // P
+LAST = TILES - 1
+HALVES = V // P
+PASSES = H // (P * J)
+BANK = 512
+
 X_CUTS = (0, 256, 384, 512)
 X_VECTOR = (208, 0, 128)
+X_BANK = (1, 6, 7)
+W1_CUTS = (0, 1, 2, 3, 5, 8)
 W2_PIECE = 128
 H_BYTES = ("h0", "w1_raw2", "w1_raw3", "h3", "w1_raw5", "h5", "w2_raw0", "w2_raw1")
-W1_CUTS = (0, 1, 2, 3, 5, 8)
-H_BANK = (None, 0, 1, 6, 7, 4, 5, 6)
+H_BANK = {1: 0, 2: 1, 3: 6, 4: 7, 5: 4, 6: 5, 7: 6}
+WHOLE_STEPS = tuple((d, (0, 1)) for d in range(D))
+LAST_STEPS = WHOLE_STEPS[:2] + tuple((d, (s,)) for s in range(HALVES) for d in (2, 3))
 
 
 def tile_picked_gcn_mlp_none_sub_l_kernel(tc, xT, w1, w2, gate, pos1, pos2, pos3, pos4, out):
@@ -33,26 +40,25 @@ def tile_picked_gcn_mlp_none_sub_l_kernel(tc, xT, w1, w2, gate, pos1, pos2, pos3
         keep = ctx.enter_context(tc.tile_pool(name="keep", bufs=1))
         psum = ctx.enter_context(tc.psum_pool(name="psum", bufs=1))
 
-        banks = [psum.tile([P, 512], F32, name=f"bank{b}") for b in range(8)]
+        banks = [psum.tile([P, BANK], F32, name=f"bank{b}") for b in range(8)]
         sum_banks, word_banks, out_banks = banks[2:4], banks[6:8], banks[0:2] + banks[4:6]
 
         pos = [lists.tile([P, V // 16], U16, name=f"pos{d}") for d in range(D)]
-        gate_pairs = [keep.tile([P, 2, V], F32, name=f"gates{q}") for q in range(2)]
-        gates = [gate_pairs[d // 2][:, d % 2, :] for d in range(D)]
+        gates = [keep.tile([P, V], F32, name=f"gate{d}")[:] for d in range(D)]
         ident = keep.tile([P, P], F32, name="ident")
         make_identity(nc, ident[:])
 
-        chunks = list(zip(X_CUTS[:-1], X_CUTS[1:]))
+        pieces = list(zip(X_CUTS[:-1], X_CUTS[1:]))
         x_first = keep.tile([P, J, X_CUTS[2]], F32, name="x_first")
         x_last = keep.tile([P, J, T - X_CUTS[2]], F32, name="x_last")
         x_raw = [x_first[:, :, : X_CUTS[1]], x_first[:, :, X_CUTS[1] :], x_last[:]]
         lots = list(zip(W1_CUTS[:-1], W1_CUTS[1:]))
         w1_raw = [keep.tile([P, J, (b - a) * P], F32, name=f"w1_raw{a}", tag=f"w1_raw{a}", align_bytes=64) for a, b in lots]
-        w2_raw = [keep.tile([P, J, N], F32, name=f"w2_raw{g}", tag=f"w2_raw{g}", align_bytes=64) for g in range(2)]
+        w2_raw = [keep.tile([P, J, N], F32, name=f"w2_raw{g}", tag=f"w2_raw{g}", align_bytes=64) for g in range(PASSES)]
 
         x_view = xT.rearrange("(p j) t -> p j t", j=J)
         w1_view = w1.rearrange("(p j) i -> p j i", j=J)
-        w2_view = w2.rearrange("(g p j) n -> g p j n", g=2, j=J)
+        w2_view = w2.rearrange("(g p j) n -> g p j n", g=PASSES, j=J)
         out_view = out.rearrange("(a p) v -> p a v", p=P)
 
         def load_w1(q):
@@ -62,32 +68,29 @@ def tile_picked_gcn_mlp_none_sub_l_kernel(tc, xT, w1, w2, gate, pos1, pos2, pos3
         nc.sync.dma_start(x_first[:], x_view[:, :, : X_CUTS[2]])
         nc.sync.dma_start(x_last[:], x_view[:, :, X_CUTS[2] :])
         load_w1(1)
-        gate_view = gate.rearrange("(q e) p v -> q p e v", e=2)
-        nc.sync.dma_start(pos[0][:], pos1)
-        nc.sync.dma_start(pos[1][:], pos2)
-        nc.sync.dma_start(gate_pairs[0][:], gate_view[0])
-        load_w1(2)
-        nc.sync.dma_start(gate_pairs[1][:], gate_view[1])
-        nc.sync.dma_start(pos[2][:], pos3)
-        nc.sync.dma_start(pos[3][:], pos4)
+        for d, src in enumerate((pos1, pos2, pos3, pos4)):
+            nc.sync.dma_start(pos[d][:], src)
+            nc.sync.dma_start(gates[d], gate[d])
+            if d == 1:
+                load_w1(2)
         load_w1(3)
         load_w1(4)
-        for g in range(2):
+        for g in range(PASSES):
             nc.sync.dma_start(w2_raw[g][:], w2_view[g])
 
         w1_grouped = [keep.tile([P, (b - a) * P, J], BF16, name=f"w1_grouped{a}", align_bytes=64) for a, b in lots]
         w1_codes = keep.tile([P, H], U32, name="w1_codes", align_bytes=64)
         w1_scales = keep.tile([P, H], U8, name="w1_scales", align_bytes=64)
-        x_grouped = [keep.tile([P, b - a, J], BF16, name=f"x_grouped{a}", align_bytes=64) for a, b in chunks]
+        x_grouped = [keep.tile([P, b - a, J], BF16, name=f"x_grouped{a}", align_bytes=64) for a, b in pieces]
         x_codes = keep.tile([P, T], U32, name="x_codes", align_bytes=64)
         x_scales = keep.tile([P, T], U8, name="x_scales", align_bytes=64)
-        w2_grouped = [keep.tile([P, N, J], BF16, name=f"w2_grouped{g}", align_bytes=64) for g in range(2)]
-        w2_scales = [keep.tile([P, N], U8, name=f"w2_scales{g}", align_bytes=64) for g in range(2)]
+        w2_grouped = [keep.tile([P, N, J], BF16, name=f"w2_grouped{g}", align_bytes=64) for g in range(PASSES)]
+        w2_scales = [keep.tile([P, N], U8, name=f"w2_scales{g}", align_bytes=64) for g in range(PASSES)]
         h = {}
         prods = [[keep.tile([P, V], F32, name=f"prod{i}_{d}")[:] for d in range(D)] for i in range(TILES)]
-        z_turned = {1: keep.tile([P, 2, 2, P, 2], BF16, name="z_turned1")}
-        z_grouped = [keep.tile([P, V, J], BF16, name=f"z_grouped{g}", align_bytes=64) for g in range(2)]
-        z_scales = [keep.tile([P, V], U8, name=f"z_scales{g}", align_bytes=64) for g in range(2)]
+        z_turned = {1: keep.tile([P, HALVES, 2, P, 2], BF16, name="z_turned1")}
+        z_grouped = [keep.tile([P, V, J], BF16, name=f"z_grouped{g}", align_bytes=64) for g in range(PASSES)]
+        z_scales = [keep.tile([P, V], U8, name=f"z_scales{g}", align_bytes=64) for g in range(PASSES)]
 
         vcopy, scopy = nc.vector.tensor_copy, nc.scalar.copy
 
@@ -105,13 +108,11 @@ def tile_picked_gcn_mlp_none_sub_l_kernel(tc, xT, w1, w2, gate, pos1, pos2, pos3
                 e = min(i + 2, b)
                 quantize(w1_codes[:, i * P : e * P], w1_scales[:, i * P : e * P], w1_grouped[q][:, (i - a) * P : (e - a) * P, :])
 
-        def group_w2(piece):
-            g, a = divmod(piece * W2_PIECE, N)
-            group(scopy, w2_grouped[g][:, a : a + W2_PIECE, :], w2_raw[g][:, :, a : a + W2_PIECE])
+        def group_w2(g, first, end):
+            for a in range(first, end, W2_PIECE):
+                group(scopy, w2_grouped[g][:, a : a + W2_PIECE, :], w2_raw[g][:, :, a : a + W2_PIECE])
 
         def project(i, a, b, bank, copy):
-            if i not in h:
-                h[i] = keep.tile([P, T], F32, name=f"h{i}", tag=H_BYTES[i], align_bytes=64)
             nc.tensor.matmul_mx(
                 out=bank[:, : b - a],
                 lhsT=w1_codes[:, i * P : (i + 1) * P].bitcast(FP8X4),
@@ -123,10 +124,17 @@ def tile_picked_gcn_mlp_none_sub_l_kernel(tc, xT, w1, w2, gate, pos1, pos2, pos3
             )
             copy(out=h[i][:, a:b], in_=bank[:, : b - a])
 
-        def banks_of(i):
-            return word_banks if i == TILES - 1 else sum_banks
+        def new_h(i):
+            h[i] = keep.tile([P, T], F32, name=f"h{i}", tag=H_BYTES[i], align_bytes=64)
 
-        def gather_and_add(i, steps=tuple((d, (0, 1)) for d in range(D))):
+        def project_all(i):
+            new_h(i)
+            project(i, 0, T, banks[H_BANK[i]], scopy)
+
+        def banks_of(i):
+            return word_banks if i == LAST else sum_banks
+
+        def gather_and_add(i, steps):
             t = i % J
             for d, halves in steps:
                 v0, v1 = halves[0] * P, (halves[-1] + 1) * P
@@ -142,100 +150,86 @@ def tile_picked_gcn_mlp_none_sub_l_kernel(tc, xT, w1, w2, gate, pos1, pos2, pos3
                         is_transpose=True,
                     )
 
-        def round_sums(i0, i1, s, copy):
+        def round_sums(i0, i1, s):
             g, t0, t1 = i0 // J, i0 % J, (i1 - 1) % J + 1
-            copy(
-                out=z_turned[g][:, s, :, 32 * t0 : 32 * t1, :],
+            scopy(
+                out=z_turned[g][:, s, :, P // J * t0 : P // J * t1, :],
                 in_=banks_of(i0)[s][:, t0 * P : t1 * P].rearrange("v (p u e) -> v u p e", u=2, e=2),
             )
 
-        def turn_back(g, s, copy):
+        def turn_back(g, s):
             bank = word_banks[s]
             for u in range(2):
                 nc.tensor.transpose(
                     bank[:, u * P : (u + 1) * P], z_turned[g][:, s, u, :, :].rearrange("v p e -> v (p e)").bitcast(F32), ident[:]
                 )
-            copy(
+            scopy(
                 out=z_grouped[g][:, s * P : (s + 1) * P, :].rearrange("p v j -> p (v j)").bitcast(F32).rearrange("p (v u) -> p v u", u=2),
                 in_=bank[:, : 2 * P].rearrange("p (u v) -> p v u", u=2),
             )
 
-        def second(g, v0, v1):
-            for a in range(N // P):
-                nc.tensor.matmul_mx(
-                    out=out_banks[a][:, v0:v1],
-                    lhsT=w2_codes[g][:, a * P : (a + 1) * P].bitcast(FP8X4),
-                    lhsT_scale=w2_scales[g][:, a * P : (a + 1) * P],
-                    rhs=z_codes[g][:, v0:v1].bitcast(FP8X4),
-                    rhs_scale=z_scales[g][:, v0:v1],
-                    start=(g == 0),
-                    stop=(g == 1 and v1 == V),
-                )
-
-        def emit(a, copy, dma):
-            o = keep.tile([P, V], F32, name=f"o{a}")
-            copy(out=o[:], in_=out_banks[a][:, :V])
-            dma(out=out_view[:, a, :], in_=o[:])
-
         prepare_w1(0)
-        for c, (a, b) in enumerate(chunks):
+        for c, (a, b) in enumerate(pieces):
             cut = X_VECTOR[c]
             if cut > 0:
                 group(vcopy, x_grouped[c][:, :cut, :], x_raw[c][:, :, :cut])
             if cut < b - a:
                 group(scopy, x_grouped[c][:, cut:, :], x_raw[c][:, :, cut:])
             quantize(x_codes[:, a:b], x_scales[:, a:b], x_grouped[c][:])
-        for c, (a, b) in enumerate(chunks):
-            project(0, a, b, banks[(1, 6, 7)[c]], vcopy if c == 2 else scopy)
+        new_h(0)
+        for c, (a, b) in enumerate(pieces):
+            project(0, a, b, banks[X_BANK[c]], vcopy if b == T else scopy)
         prepare_w1(1)
 
-        def project_all(i):
-            project(i, 0, T, banks[H_BANK[i]], scopy)
-
-        prepare_w1(2)
-        project_all(1)
-        gather_and_add(0)
-        prepare_w1(3)
-        project_all(2)
-        gather_and_add(1)
-        prepare_w1(4)
-        project_all(3)
-        gather_and_add(2)
-        group_w2(0)
-        group_w2(1)
+        for i in range(J - 1):
+            prepare_w1(i + 2)
+            project_all(i + 1)
+            gather_and_add(i, WHOLE_STEPS)
+        group_w2(0, 0, N // 2)
         project_all(4)
         project_all(5)
-        gather_and_add(3)
-        group_w2(2)
-        group_w2(3)
-        z_turned[0] = keep.tile([P, 2, 2, P, 2], BF16, name="z_turned0", tag="w2_raw0", align_bytes=64)
-        for s in range(2):
-            round_sums(0, J, s, scopy)
-        for s in range(2):
-            turn_back(0, s, scopy)
+        gather_and_add(3, WHOLE_STEPS)
+        group_w2(0, N // 2, N)
+
+        z_turned[0] = keep.tile([P, HALVES, 2, P, 2], BF16, name="z_turned0", tag="w2_raw0", align_bytes=64)
+        for s in range(HALVES):
+            round_sums(0, J, s)
+        for s in range(HALVES):
+            turn_back(0, s)
+
         project_all(6)
-        gather_and_add(4)
-        for piece in range(4, 8):
-            group_w2(piece)
-        project_all(7)
-        gather_and_add(5)
-        gather_and_add(6)
-        for s in range(2):
-            round_sums(J, TILES - 1, s, scopy)
-        gather_and_add(7, ((0, (0, 1)), (1, (0, 1)), (2, (0,)), (3, (0,)), (2, (1,)), (3, (1,))))
-        late = keep.tile([P, 2 * N + V], U32, name="late_codes", tag=H_BYTES[TILES - 1], align_bytes=64)
-        w2_codes = [late[:, g * N : (g + 1) * N] for g in range(2)]
-        z_codes = [late[:, 2 * N :], keep.tile([P, V], U32, name="z_codes1", align_bytes=64)[:]]
+        gather_and_add(4, WHOLE_STEPS)
+        group_w2(1, 0, N)
+        project_all(LAST)
+        gather_and_add(5, WHOLE_STEPS)
+        gather_and_add(6, WHOLE_STEPS)
+        for s in range(HALVES):
+            round_sums(J, LAST, s)
+        gather_and_add(LAST, LAST_STEPS)
+
+        late_codes = keep.tile([P, PASSES * N + V], U32, name="late_codes", tag=H_BYTES[LAST], align_bytes=64)
+        w2_codes = [late_codes[:, g * N : (g + 1) * N] for g in range(PASSES)]
+        z_codes = [late_codes[:, PASSES * N :], keep.tile([P, V], U32, name="z_codes1", align_bytes=64)[:]]
         quantize(z_codes[0], z_scales[0][:], z_grouped[0][:])
-        for g in range(2):
+        for g in range(PASSES):
             quantize(w2_codes[g], w2_scales[g][:], w2_grouped[g][:])
-        for s in range(2):
-            round_sums(TILES - 1, TILES, s, scopy)
-            turn_back(1, s, scopy)
+        for s in range(HALVES):
+            round_sums(LAST, TILES, s)
+            turn_back(1, s)
             quantize(z_codes[1][:, s * P : (s + 1) * P], z_scales[1][:, s * P : (s + 1) * P], z_grouped[1][:, s * P : (s + 1) * P, :])
-        for g in range(2):
-            second(g, 0, V)
-        emit(0, vcopy, nc.sync.dma_start)
-        emit(1, scopy, nc.sync.dma_start)
-        emit(2, vcopy, nc.sync.dma_start)
-        emit(3, scopy, nc.scalar.dma_start)
+        for g in range(PASSES):
+            for a in range(N // P):
+                nc.tensor.matmul_mx(
+                    out=out_banks[a][:, :V],
+                    lhsT=w2_codes[g][:, a * P : (a + 1) * P].bitcast(FP8X4),
+                    lhsT_scale=w2_scales[g][:, a * P : (a + 1) * P],
+                    rhs=z_codes[g].bitcast(FP8X4),
+                    rhs_scale=z_scales[g][:],
+                    start=(g == 0),
+                    stop=(g == PASSES - 1),
+                )
+
+        for a in range(N // P):
+            result = keep.tile([P, V], F32, name=f"result{a}")
+            (scopy if a % 2 else vcopy)(out=result[:], in_=out_banks[a][:, :V])
+            (nc.scalar if a == N // P - 1 else nc.sync).dma_start(out=out_view[:, a, :], in_=result[:])

@@ -30,7 +30,7 @@ W2_PIECE = 128
 H_BYTES = ("h0", "w1_raw2", "w1_raw3", "h3", "w1_raw5", "h5", "w2_raw0", "w2_raw1")
 H_BANK = {1: 0, 2: 1, 3: 6, 4: 7, 5: 4, 6: 5, 7: 6}
 WHOLE_STEPS = tuple((d, (0, 1)) for d in range(D))
-LAST_STEPS = WHOLE_STEPS[:2] + tuple((d, (s,)) for s in range(HALVES) for d in (2, 3))
+LAST_STEPS = WHOLE_STEPS[:3] + tuple((3, (s,)) for s in range(HALVES))
 
 
 def tile_picked_gcn_mlp_none_sub_l_kernel(tc, xT, w1, w2, gate, pos1, pos2, pos3, pos4, out):

@@ -19,6 +19,7 @@ J = 4
 TILES = H // P
 LAST = TILES - 1
 HALVES = V // P
+PAIRED = TILES - 2
 PASSES = H // (P * J)
 BANK = 512
 
@@ -88,7 +89,8 @@ def tile_picked_gcn_mlp_none_sub_l_kernel(tc, xT, w1, w2, gate, pos1, pos2, pos3
         w2_scales = [keep.tile([P, N], U8, name=f"w2_scales{g}", align_bytes=64) for g in range(PASSES)]
         h = {}
         prods = [[keep.tile([P, V], F32, name=f"prod{i}_{d}")[:] for d in range(D)] for i in range(TILES)]
-        z_turned = {1: keep.tile([P, HALVES, 2, P, 2], BF16, name="z_turned1")}
+        z_turned = {}
+        turned1 = [keep.tile([P, 2, P, 2], BF16, name=f"z_turned1_{s}") for s in range(HALVES)]
         z_grouped = [keep.tile([P, V, J], BF16, name=f"z_grouped{g}", align_bytes=64) for g in range(PASSES)]
         z_scales = [keep.tile([P, V], U8, name=f"z_scales{g}", align_bytes=64) for g in range(PASSES)]
 
@@ -102,8 +104,15 @@ def tile_picked_gcn_mlp_none_sub_l_kernel(tc, xT, w1, w2, gate, pos1, pos2, pos3
 
         def prepare_w1(q):
             a, b = lots[q]
-            for c in range(0, (b - a) * P, P):
+            for i in range(a, min(b, PAIRED)):
+                c = (i - a) * P
                 group(scopy, w1_grouped[q][:, c : c + P, :], w1_raw[q][:, :, c : c + P])
+            if b > PAIRED:
+                c = (PAIRED - a) * P
+                dst = w1_grouped[q][:, c:, :].rearrange("k (u p e) j -> k p j u e", u=2, e=2)
+                src = w1_raw[q][:, :, c:].rearrange("k j (p u e) -> k p j u e", u=2, e=2)
+                for r in range(0, P // 2, P // 4):
+                    scopy(out=dst[:, r : r + P // 4], in_=src[:, r : r + P // 4])
             for i in range(a, b, 2):
                 e = min(i + 2, b)
                 quantize(w1_codes[:, i * P : e * P], w1_scales[:, i * P : e * P], w1_grouped[q][:, (i - a) * P : (e - a) * P, :])
@@ -131,9 +140,6 @@ def tile_picked_gcn_mlp_none_sub_l_kernel(tc, xT, w1, w2, gate, pos1, pos2, pos3
             new_h(i)
             project(i, 0, T, banks[H_BANK[i]], scopy)
 
-        def banks_of(i):
-            return word_banks if i == LAST else sum_banks
-
         def gather_and_add(i, steps):
             t = i % J
             for d, halves in steps:
@@ -142,7 +148,7 @@ def tile_picked_gcn_mlp_none_sub_l_kernel(tc, xT, w1, w2, gate, pos1, pos2, pos3
                 nc.vector.tensor_tensor(prods[i][d][:, v0:v1], h[i][:].indirect(offsets), gates[d][:, v0:v1], MULT)
                 for s in halves:
                     nc.tensor.matmul(
-                        banks_of(i)[s][:, t * P : (t + 1) * P],
+                        (banks[4:6] if i == LAST else sum_banks)[s][:, t * P : (t + 1) * P],
                         lhsT=prods[i][d][:, s * P : (s + 1) * P],
                         rhs=ident[:],
                         start=(d == 0),
@@ -154,15 +160,21 @@ def tile_picked_gcn_mlp_none_sub_l_kernel(tc, xT, w1, w2, gate, pos1, pos2, pos3
             g, t0, t1 = i0 // J, i0 % J, (i1 - 1) % J + 1
             scopy(
                 out=z_turned[g][:, s, :, P // J * t0 : P // J * t1, :],
-                in_=banks_of(i0)[s][:, t0 * P : t1 * P].rearrange("v (p u e) -> v u p e", u=2, e=2),
+                in_=sum_banks[s][:, t0 * P : t1 * P].rearrange("v (p u e) -> v u p e", u=2, e=2),
             )
 
-        def turn_back(g, s):
+        def round_pairs(u, s):
+            t = 2 + u
+            scopy(out=turned1[s][:, u, P // 2 :, :].rearrange("v p e -> v (p e)"), in_=(banks[4:6] if u else sum_banks)[s][:, t * P : (t + 1) * P])
+
+        def turn_back(g, s, u):
+            src = turned1[s][:, u] if g else z_turned[g][:, s, u, :, :]
+            nc.tensor.transpose(
+                word_banks[s][:, u * P : (u + 1) * P], src.rearrange("v p e -> v (p e)").bitcast(F32), ident[:]
+            )
+
+        def interleave(g, s):
             bank = word_banks[s]
-            for u in range(2):
-                nc.tensor.transpose(
-                    bank[:, u * P : (u + 1) * P], z_turned[g][:, s, u, :, :].rearrange("v p e -> v (p e)").bitcast(F32), ident[:]
-                )
             scopy(
                 out=z_grouped[g][:, s * P : (s + 1) * P, :].rearrange("p v j -> p (v j)").bitcast(F32).rearrange("p (v u) -> p v u", u=2),
                 in_=bank[:, : 2 * P].rearrange("p (u v) -> p v u", u=2),
@@ -195,7 +207,9 @@ def tile_picked_gcn_mlp_none_sub_l_kernel(tc, xT, w1, w2, gate, pos1, pos2, pos3
         for s in range(HALVES):
             round_sums(0, J, s)
         for s in range(HALVES):
-            turn_back(0, s)
+            turn_back(0, s, 0)
+            turn_back(0, s, 1)
+            interleave(0, s)
 
         project_all(6)
         gather_and_add(4, WHOLE_STEPS)
@@ -204,18 +218,22 @@ def tile_picked_gcn_mlp_none_sub_l_kernel(tc, xT, w1, w2, gate, pos1, pos2, pos3
         gather_and_add(5, WHOLE_STEPS)
         gather_and_add(6, WHOLE_STEPS)
         for s in range(HALVES):
-            round_sums(J, LAST, s)
+            scopy(out=turned1[s][:, :, : P // 2, :], in_=sum_banks[s][:, : 2 * P].rearrange("v (p u e) -> v u p e", u=2, e=2))
+            round_pairs(0, s)
+            turn_back(1, s, 0)
         gather_and_add(LAST, LAST_STEPS)
 
         late_codes = keep.tile([P, PASSES * N + V], U32, name="late_codes", tag=H_BYTES[LAST], align_bytes=64)
         w2_codes = [late_codes[:, g * N : (g + 1) * N] for g in range(PASSES)]
         z_codes = [late_codes[:, PASSES * N :], keep.tile([P, V], U32, name="z_codes1", align_bytes=64)[:]]
+        quantize(w2_codes[0], w2_scales[0][:], w2_grouped[0][:])
+        quantize(w2_codes[1][:, : N // 2], w2_scales[1][:, : N // 2], w2_grouped[1][:, : N // 2, :])
         quantize(z_codes[0], z_scales[0][:], z_grouped[0][:])
-        for g in range(PASSES):
-            quantize(w2_codes[g], w2_scales[g][:], w2_grouped[g][:])
+        quantize(w2_codes[1][:, N // 2 :], w2_scales[1][:, N // 2 :], w2_grouped[1][:, N // 2 :, :])
         for s in range(HALVES):
-            round_sums(LAST, TILES, s)
-            turn_back(1, s)
+            round_pairs(1, s)
+            turn_back(1, s, 1)
+            interleave(1, s)
             quantize(z_codes[1][:, s * P : (s + 1) * P], z_scales[1][:, s * P : (s + 1) * P], z_grouped[1][:, s * P : (s + 1) * P, :])
         for g in range(PASSES):
             for a in range(N // P):

@@ -31,7 +31,8 @@ W2_PIECE = 128
 H_BYTES = ("h0", "w1_raw2", "w1_raw3", "h3", "w1_raw5", "h5", "w2_raw0", "w2_raw1")
 H_BANK = {1: 0, 2: 1, 3: 6, 4: 7, 5: 4, 6: 5, 7: 6}
 WHOLE_STEPS = tuple((d, (0, 1)) for d in range(D))
-LAST_STEPS = WHOLE_STEPS[:3] + tuple((3, (s,)) for s in range(HALVES))
+LAST_STEPS = WHOLE_STEPS[:-1] + tuple((D - 1, (s,)) for s in range(HALVES))
+FIRST_PASS_BLOCKS = (3, 2, 0, 1)
 
 
 def tile_picked_gcn_mlp_none_sub_l_kernel(tc, xT, w1, w2, gate, pos1, pos2, pos3, pos4, out):
@@ -43,6 +44,7 @@ def tile_picked_gcn_mlp_none_sub_l_kernel(tc, xT, w1, w2, gate, pos1, pos2, pos3
 
         banks = [psum.tile([P, BANK], F32, name=f"bank{b}") for b in range(8)]
         sum_banks, word_banks, out_banks = banks[2:4], banks[6:8], banks[0:2] + banks[4:6]
+        last_banks = out_banks[2:]
 
         pos = [lists.tile([P, V // 16], U16, name=f"pos{d}") for d in range(D)]
         gates = [keep.tile([P, V], F32, name=f"gate{d}")[:] for d in range(D)]
@@ -89,8 +91,7 @@ def tile_picked_gcn_mlp_none_sub_l_kernel(tc, xT, w1, w2, gate, pos1, pos2, pos3
         w2_scales = [keep.tile([P, N], U8, name=f"w2_scales{g}", align_bytes=64) for g in range(PASSES)]
         h = {}
         prods = [[keep.tile([P, V], F32, name=f"prod{i}_{d}")[:] for d in range(D)] for i in range(TILES)]
-        z_turned = {}
-        turned1 = [keep.tile([P, 2, P, 2], BF16, name=f"z_turned1_{s}") for s in range(HALVES)]
+        z_turned = {1: [keep.tile([P, 2, P, 2], BF16, name=f"z_turned1_{s}")[:] for s in range(HALVES)]}
         z_grouped = [keep.tile([P, V, J], BF16, name=f"z_grouped{g}", align_bytes=64) for g in range(PASSES)]
         z_scales = [keep.tile([P, V], U8, name=f"z_scales{g}", align_bytes=64) for g in range(PASSES)]
 
@@ -140,6 +141,9 @@ def tile_picked_gcn_mlp_none_sub_l_kernel(tc, xT, w1, w2, gate, pos1, pos2, pos3
             new_h(i)
             project(i, 0, T, banks[H_BANK[i]], scopy)
 
+        def banks_of(i):
+            return last_banks if i == LAST else sum_banks
+
         def gather_and_add(i, steps):
             t = i % J
             for d, halves in steps:
@@ -148,7 +152,7 @@ def tile_picked_gcn_mlp_none_sub_l_kernel(tc, xT, w1, w2, gate, pos1, pos2, pos3
                 nc.vector.tensor_tensor(prods[i][d][:, v0:v1], h[i][:].indirect(offsets), gates[d][:, v0:v1], MULT)
                 for s in halves:
                     nc.tensor.matmul(
-                        (banks[4:6] if i == LAST else sum_banks)[s][:, t * P : (t + 1) * P],
+                        banks_of(i)[s][:, t * P : (t + 1) * P],
                         lhsT=prods[i][d][:, s * P : (s + 1) * P],
                         rhs=ident[:],
                         start=(d == 0),
@@ -159,25 +163,25 @@ def tile_picked_gcn_mlp_none_sub_l_kernel(tc, xT, w1, w2, gate, pos1, pos2, pos3
         def round_sums(i0, i1, s):
             g, t0, t1 = i0 // J, i0 % J, (i1 - 1) % J + 1
             scopy(
-                out=z_turned[g][:, s, :, P // J * t0 : P // J * t1, :],
+                out=z_turned[g][s][:, :, P // J * t0 : P // J * t1, :],
                 in_=sum_banks[s][:, t0 * P : t1 * P].rearrange("v (p u e) -> v u p e", u=2, e=2),
             )
 
-        def round_pairs(u, s):
-            t = 2 + u
-            scopy(out=turned1[s][:, u, P // 2 :, :].rearrange("v p e -> v (p e)"), in_=(banks[4:6] if u else sum_banks)[s][:, t * P : (t + 1) * P])
-
-        def turn_back(g, s, u):
-            src = turned1[s][:, u] if g else z_turned[g][:, s, u, :, :]
-            nc.tensor.transpose(
-                word_banks[s][:, u * P : (u + 1) * P], src.rearrange("v p e -> v (p e)").bitcast(F32), ident[:]
+        def round_pairs(i, s):
+            t = i % J
+            scopy(
+                out=z_turned[1][s][:, i - PAIRED, P // 2 :, :].rearrange("v p e -> v (p e)"),
+                in_=banks_of(i)[s][:, t * P : (t + 1) * P],
             )
 
+        def turn_back(g, s, u):
+            words = z_turned[g][s][:, u, :, :].rearrange("v p e -> v (p e)").bitcast(F32)
+            nc.tensor.transpose(word_banks[s][:, u * P : (u + 1) * P], words, ident[:])
+
         def interleave(g, s):
-            bank = word_banks[s]
             scopy(
                 out=z_grouped[g][:, s * P : (s + 1) * P, :].rearrange("p v j -> p (v j)").bitcast(F32).rearrange("p (v u) -> p v u", u=2),
-                in_=bank[:, : 2 * P].rearrange("p (u v) -> p v u", u=2),
+                in_=word_banks[s][:, : 2 * P].rearrange("p (u v) -> p v u", u=2),
             )
 
         prepare_w1(0)
@@ -203,7 +207,8 @@ def tile_picked_gcn_mlp_none_sub_l_kernel(tc, xT, w1, w2, gate, pos1, pos2, pos3
         gather_and_add(3, WHOLE_STEPS)
         group_w2(0, N // 2, N)
 
-        z_turned[0] = keep.tile([P, HALVES, 2, P, 2], BF16, name="z_turned0", tag="w2_raw0", align_bytes=64)
+        z_turned0 = keep.tile([P, HALVES, 2, P, 2], BF16, name="z_turned0", tag="w2_raw0", align_bytes=64)
+        z_turned[0] = [z_turned0[:, s, :, :, :] for s in range(HALVES)]
         for s in range(HALVES):
             round_sums(0, J, s)
         for s in range(HALVES):
@@ -216,27 +221,33 @@ def tile_picked_gcn_mlp_none_sub_l_kernel(tc, xT, w1, w2, gate, pos1, pos2, pos3
         group_w2(1, 0, N)
         project_all(LAST)
         gather_and_add(5, WHOLE_STEPS)
-        gather_and_add(6, WHOLE_STEPS)
+        gather_and_add(PAIRED, WHOLE_STEPS)
         for s in range(HALVES):
-            scopy(out=turned1[s][:, :, : P // 2, :], in_=sum_banks[s][:, : 2 * P].rearrange("v (p u e) -> v u p e", u=2, e=2))
-            round_pairs(0, s)
+            round_sums(J, PAIRED, s)
+            round_pairs(PAIRED, s)
             turn_back(1, s, 0)
         gather_and_add(LAST, LAST_STEPS)
 
         late_codes = keep.tile([P, PASSES * N + V], U32, name="late_codes", tag=H_BYTES[LAST], align_bytes=64)
         w2_codes = [late_codes[:, g * N : (g + 1) * N] for g in range(PASSES)]
         z_codes = [late_codes[:, PASSES * N :], keep.tile([P, V], U32, name="z_codes1", align_bytes=64)[:]]
-        quantize(w2_codes[0], w2_scales[0][:], w2_grouped[0][:])
-        quantize(w2_codes[1][:, : N // 2], w2_scales[1][:, : N // 2], w2_grouped[1][:, : N // 2, :])
+
+        def quantize_w2(g, first, end):
+            cols = slice(first * P, end * P)
+            quantize(w2_codes[g][:, cols], w2_scales[g][:, cols], w2_grouped[g][:, cols, :])
+
         quantize(z_codes[0], z_scales[0][:], z_grouped[0][:])
-        quantize(w2_codes[1][:, N // 2 :], w2_scales[1][:, N // 2 :], w2_grouped[1][:, N // 2 :, :])
+        quantize_w2(0, 3, 4)
+        quantize_w2(1, 0, 4)
+        quantize_w2(0, 2, 3)
+        quantize_w2(0, 0, 2)
         for s in range(HALVES):
-            round_pairs(1, s)
+            round_pairs(LAST, s)
             turn_back(1, s, 1)
             interleave(1, s)
             quantize(z_codes[1][:, s * P : (s + 1) * P], z_scales[1][:, s * P : (s + 1) * P], z_grouped[1][:, s * P : (s + 1) * P, :])
-        for g in range(PASSES):
-            for a in range(N // P):
+        for g, blocks in enumerate((FIRST_PASS_BLOCKS, range(N // P))):
+            for a in blocks:
                 nc.tensor.matmul_mx(
                     out=out_banks[a][:, :V],
                     lhsT=w2_codes[g][:, a * P : (a + 1) * P].bitcast(FP8X4),

@@ -10,6 +10,7 @@ U16 = mybir.dt.uint16
 U8 = mybir.dt.uint8
 FP8X4 = mybir.dt.float8_e4m3fn_x4
 MULT = mybir.AluOpType.mult
+COPY = mybir.ActivationFunctionType.Copy
 
 K, T, D, V, H, N = 512, 512, 4, 256, 1024, 512
 FLOPS = 2 * K * H * T + 2 * H * N * V
@@ -28,10 +29,26 @@ X_VECTOR = (208, 0, 128)
 X_BANK = (1, 6, 7)
 W1_CUTS = (0, 1, 2, 3, 5, 8)
 W2_PIECE = 128
-H_BYTES = ("h0", "w1_raw2", "w1_raw3", "h3", "w1_raw5", "h5", "w2_raw0", "w2_raw1")
-H_BANK = {1: 0, 2: 1, 3: 6, 4: 7, 5: 4, 6: 5, 7: 6}
-WHOLE_STEPS = tuple((d, (0, 1)) for d in range(D))
-LAST_STEPS = WHOLE_STEPS[:-1] + tuple((D - 1, (s,)) for s in range(HALVES))
+KB = 1024
+RAW_AT = {"w1_raw2": 0, "w1_raw3": 2 * KB, "w1_raw5": 6 * KB, "w2_raw1": 22 * KB, "prod3_3": 14 * KB, "prod5_0": 18 * KB, "prod5_1": 19 * KB, "prod5_2": 20 * KB, "prod5_3": 21 * KB, "h7": 30 * KB, "w1_grouped5": 36 * KB}
+TENANTS = {
+    "h1": ("w1_raw2", 0),
+    "h2": ("w1_raw3", 0),
+    "prod1_3": ("w1_raw3", 2),
+    "h3": ("w1_raw5", 0),
+    "h4": ("w1_raw5", 2),
+    "prod2_1": ("w1_raw5", 4),
+    "prod2_2": ("w1_raw5", 5),
+    "prod2_3": ("w1_grouped5", 0),
+    "z_turned1_0": ("w2_raw1", 0),
+    "z_turned1_1": ("w2_raw1", 1),
+    "late_codes": ("h7", 0),
+    "w2_grouped0": ("prod3_3", 0),
+    **{f"prod{LAST}_{d}": (f"prod5_{d}", 0) for d in (0, 2, 3)},
+}
+H_BANK = {1: 0, 2: 1, 3: 6, 4: 7, 5: 4, 6: 5, 7: 0}
+PLAIN = 2
+SHARED = 6
 FIRST_PASS_BLOCKS = (3, 2, 0, 1)
 
 
@@ -40,24 +57,34 @@ def tile_picked_gcn_mlp_none_sub_l_kernel(tc, xT, w1, w2, gate, pos1, pos2, pos3
     with ExitStack() as ctx:
         lists = ctx.enter_context(tc.tile_pool(name="lists", bufs=1))
         keep = ctx.enter_context(tc.tile_pool(name="keep", bufs=1))
+        shared = ctx.enter_context(tc.tile_pool(name="shared", bufs=1))
         psum = ctx.enter_context(tc.psum_pool(name="psum", bufs=1))
 
         banks = [psum.tile([P, BANK], F32, name=f"bank{b}") for b in range(8)]
-        sum_banks, word_banks, out_banks = banks[2:4], banks[6:8], banks[0:2] + banks[4:6]
+        sum_banks, word_banks, out_banks = [banks[2:4], banks[2:4]], banks[6:8], banks[6:8] + banks[4:6]
         last_banks = out_banks[2:]
 
         pos = [lists.tile([P, V // 16], U16, name=f"pos{d}") for d in range(D)]
-        gates = [keep.tile([P, V], F32, name=f"gate{d}")[:] for d in range(D)]
+        gate_pairs = [keep.tile([P, 2, V], F32, name=f"gates{a}") for a in range(D // 2)]
+        gates = [gate_pairs[d // 2][:, d % 2, :] for d in range(D)]
         ident = keep.tile([P, P], F32, name="ident")
         make_identity(nc, ident[:])
+
+        def new_tile(name, shape, dtype):
+            if name in RAW_AT:
+                return shared.tile(shape, dtype, name=name, offset=RAW_AT[name], align_bytes=64)
+            if name in TENANTS:
+                raw, kb = TENANTS[name]
+                return shared.tile(shape, dtype, name=name, offset=RAW_AT[raw] + kb * KB, align_bytes=64)
+            return keep.tile(shape, dtype, name=name, align_bytes=64)
 
         pieces = list(zip(X_CUTS[:-1], X_CUTS[1:]))
         x_first = keep.tile([P, J, X_CUTS[2]], F32, name="x_first")
         x_last = keep.tile([P, J, T - X_CUTS[2]], F32, name="x_last")
         x_raw = [x_first[:, :, : X_CUTS[1]], x_first[:, :, X_CUTS[1] :], x_last[:]]
         lots = list(zip(W1_CUTS[:-1], W1_CUTS[1:]))
-        w1_raw = [keep.tile([P, J, (b - a) * P], F32, name=f"w1_raw{a}", tag=f"w1_raw{a}", align_bytes=64) for a, b in lots]
-        w2_raw = [keep.tile([P, J, N], F32, name=f"w2_raw{g}", tag=f"w2_raw{g}", align_bytes=64) for g in range(PASSES)]
+        w1_raw = [new_tile(f"w1_raw{a}", [P, J, (b - a) * P], F32) for a, b in lots]
+        w2_raw = [new_tile(f"w2_raw{g}", [P, J, N], F32) for g in range(PASSES)]
 
         x_view = xT.rearrange("(p j) t -> p j t", j=J)
         w1_view = w1.rearrange("(p j) i -> p j i", j=J)
@@ -71,27 +98,35 @@ def tile_picked_gcn_mlp_none_sub_l_kernel(tc, xT, w1, w2, gate, pos1, pos2, pos3
         nc.sync.dma_start(x_first[:], x_view[:, :, : X_CUTS[2]])
         nc.sync.dma_start(x_last[:], x_view[:, :, X_CUTS[2] :])
         load_w1(1)
-        for d, src in enumerate((pos1, pos2, pos3, pos4)):
-            nc.sync.dma_start(pos[d][:], src)
-            nc.sync.dma_start(gates[d], gate[d])
-            if d == 1:
-                load_w1(2)
+        gate_view = gate.rearrange("(a d) p v -> a p d v", d=2)
+        nc.sync.dma_start(pos[0][:], pos1)
+        nc.sync.dma_start(pos[1][:], pos2)
+        nc.sync.dma_start(gate_pairs[0][:], gate_view[0])
+        load_w1(2)
+        nc.sync.dma_start(pos[2][:], pos3)
+        nc.sync.dma_start(gate_pairs[1][:], gate_view[1])
+        nc.sync.dma_start(pos[3][:], pos4)
         load_w1(3)
         load_w1(4)
-        for g in range(PASSES):
-            nc.sync.dma_start(w2_raw[g][:], w2_view[g])
+        nc.sync.dma_start(w2_raw[0][:], w2_view[0])
+        nc.sync.dma_start(w2_raw[1][:], w2_view[1])
 
-        w1_grouped = [keep.tile([P, (b - a) * P, J], BF16, name=f"w1_grouped{a}", align_bytes=64) for a, b in lots]
+        w1_grouped = [new_tile(f"w1_grouped{a}", [P, (b - a) * P, J], BF16) for a, b in lots]
         w1_codes = keep.tile([P, H], U32, name="w1_codes", align_bytes=64)
         w1_scales = keep.tile([P, H], U8, name="w1_scales", align_bytes=64)
         x_grouped = [keep.tile([P, b - a, J], BF16, name=f"x_grouped{a}", align_bytes=64) for a, b in pieces]
         x_codes = keep.tile([P, T], U32, name="x_codes", align_bytes=64)
         x_scales = keep.tile([P, T], U8, name="x_scales", align_bytes=64)
-        w2_grouped = [keep.tile([P, N, J], BF16, name=f"w2_grouped{g}", align_bytes=64) for g in range(PASSES)]
+        w2_grouped = [new_tile(f"w2_grouped{g}", [P, N, J], BF16) for g in range(PASSES)]
         w2_scales = [keep.tile([P, N], U8, name=f"w2_scales{g}", align_bytes=64) for g in range(PASSES)]
-        h = {}
-        prods = [[keep.tile([P, V], F32, name=f"prod{i}_{d}")[:] for d in range(D)] for i in range(TILES)]
-        z_turned = {1: [keep.tile([P, 2, P, 2], BF16, name=f"z_turned1_{s}")[:] for s in range(HALVES)]}
+        h = [new_tile(f"h{i}", [P, T], F32) for i in range(TILES)]
+        picked = {i: new_tile(f"picked{i}", [P, PLAIN, V], F32) for i in range(SHARED, TILES)}
+        pairs = {i: new_tile(f"prod{i}_0", [P, PLAIN, V], F32) for i in range(SHARED, TILES)}
+        prods = [
+            [pairs[i][:, d, :] if i in pairs and d < PLAIN else new_tile(f"prod{i}_{d}", [P, V], F32)[:] for d in range(D)]
+            for i in range(TILES)
+        ]
+        z_turned = [[new_tile(f"z_turned{g}_{s}", [P, 2, P, 2], BF16)[:] for s in range(HALVES)] for g in range(PASSES)]
         z_grouped = [keep.tile([P, V, J], BF16, name=f"z_grouped{g}", align_bytes=64) for g in range(PASSES)]
         z_scales = [keep.tile([P, V], U8, name=f"z_scales{g}", align_bytes=64) for g in range(PASSES)]
 
@@ -118,9 +153,9 @@ def tile_picked_gcn_mlp_none_sub_l_kernel(tc, xT, w1, w2, gate, pos1, pos2, pos3
                 e = min(i + 2, b)
                 quantize(w1_codes[:, i * P : e * P], w1_scales[:, i * P : e * P], w1_grouped[q][:, (i - a) * P : (e - a) * P, :])
 
-        def group_w2(g, first, end):
+        def group_w2(copy, g, first, end):
             for a in range(first, end, W2_PIECE):
-                group(scopy, w2_grouped[g][:, a : a + W2_PIECE, :], w2_raw[g][:, :, a : a + W2_PIECE])
+                group(copy, w2_grouped[g][:, a : a + W2_PIECE, :], w2_raw[g][:, :, a : a + W2_PIECE])
 
         def project(i, a, b, bank, copy):
             nc.tensor.matmul_mx(
@@ -134,22 +169,30 @@ def tile_picked_gcn_mlp_none_sub_l_kernel(tc, xT, w1, w2, gate, pos1, pos2, pos3
             )
             copy(out=h[i][:, a:b], in_=bank[:, : b - a])
 
-        def new_h(i):
-            h[i] = keep.tile([P, T], F32, name=f"h{i}", tag=H_BYTES[i], align_bytes=64)
+        def pick(i):
+            for d in range(PLAIN if i in picked else 0):
+                nc.scalar.activation(picked[i][:, d, :], h[i][:].indirect(pos[d][:]), COPY)
 
         def project_all(i):
-            new_h(i)
             project(i, 0, T, banks[H_BANK[i]], scopy)
+            pick(i)
 
         def banks_of(i):
-            return last_banks if i == LAST else sum_banks
+            return last_banks if i == LAST else sum_banks[i // J]
 
-        def gather_and_add(i, steps):
+        def weigh(i):
+            nc.vector.tensor_tensor(pairs[i][:], picked[i][:], gate_pairs[0][:], MULT)
+
+        def gather_and_add(i):
             t = i % J
+            steps = [(d, (0, 1)) for d in range(D)]
+            if i == LAST:
+                steps = steps[:-1] + [(D - 1, (s,)) for s in range(HALVES)]
             for d, halves in steps:
                 v0, v1 = halves[0] * P, (halves[-1] + 1) * P
-                offsets = pos[d][:, v0 // 16 : v1 // 16]
-                nc.vector.tensor_tensor(prods[i][d][:, v0:v1], h[i][:].indirect(offsets), gates[d][:, v0:v1], MULT)
+                if i not in picked or d >= PLAIN:
+                    offsets = pos[d][:, v0 // 16 : v1 // 16]
+                    nc.vector.tensor_tensor(prods[i][d][:, v0:v1], h[i][:].indirect(offsets), gates[d][:, v0:v1], MULT)
                 for s in halves:
                     nc.tensor.matmul(
                         banks_of(i)[s][:, t * P : (t + 1) * P],
@@ -164,7 +207,7 @@ def tile_picked_gcn_mlp_none_sub_l_kernel(tc, xT, w1, w2, gate, pos1, pos2, pos3
             g, t0, t1 = i0 // J, i0 % J, (i1 - 1) % J + 1
             scopy(
                 out=z_turned[g][s][:, :, P // J * t0 : P // J * t1, :],
-                in_=sum_banks[s][:, t0 * P : t1 * P].rearrange("v (p u e) -> v u p e", u=2, e=2),
+                in_=sum_banks[g][s][:, t0 * P : t1 * P].rearrange("v (p u e) -> v u p e", u=2, e=2),
             )
 
         def round_pairs(i, s):
@@ -192,43 +235,40 @@ def tile_picked_gcn_mlp_none_sub_l_kernel(tc, xT, w1, w2, gate, pos1, pos2, pos3
             if cut < b - a:
                 group(scopy, x_grouped[c][:, cut:, :], x_raw[c][:, :, cut:])
             quantize(x_codes[:, a:b], x_scales[:, a:b], x_grouped[c][:])
-        new_h(0)
         for c, (a, b) in enumerate(pieces):
             project(0, a, b, banks[X_BANK[c]], vcopy if b == T else scopy)
         prepare_w1(1)
-
-        for i in range(J - 1):
-            prepare_w1(i + 2)
-            project_all(i + 1)
-            gather_and_add(i, WHOLE_STEPS)
-        group_w2(0, 0, N // 2)
-        project_all(4)
-        project_all(5)
-        gather_and_add(3, WHOLE_STEPS)
-        group_w2(0, N // 2, N)
-
-        z_turned0 = keep.tile([P, HALVES, 2, P, 2], BF16, name="z_turned0", tag="w2_raw0", align_bytes=64)
-        z_turned[0] = [z_turned0[:, s, :, :, :] for s in range(HALVES)]
+        prepare_w1(2)
+        project_all(1)
+        gather_and_add(0)
+        prepare_w1(3)
+        project_all(2)
+        gather_and_add(1)
+        prepare_w1(4)
+        for i in range(3, TILES):
+            project_all(i)
+        gather_and_add(2)
+        gather_and_add(3)
         for s in range(HALVES):
             round_sums(0, J, s)
         for s in range(HALVES):
             turn_back(0, s, 0)
             turn_back(0, s, 1)
             interleave(0, s)
-
-        project_all(6)
-        gather_and_add(4, WHOLE_STEPS)
-        group_w2(1, 0, N)
-        project_all(LAST)
-        gather_and_add(5, WHOLE_STEPS)
-        gather_and_add(PAIRED, WHOLE_STEPS)
+        gather_and_add(4)
+        gather_and_add(5)
+        group_w2(scopy, 0, 0, N)
+        group_w2(scopy, 1, 0, N)
+        weigh(PAIRED)
+        gather_and_add(PAIRED)
+        weigh(LAST)
         for s in range(HALVES):
             round_sums(J, PAIRED, s)
             round_pairs(PAIRED, s)
             turn_back(1, s, 0)
-        gather_and_add(LAST, LAST_STEPS)
+        gather_and_add(LAST)
 
-        late_codes = keep.tile([P, PASSES * N + V], U32, name="late_codes", tag=H_BYTES[LAST], align_bytes=64)
+        late_codes = new_tile("late_codes", [P, PASSES * N + V], U32)
         w2_codes = [late_codes[:, g * N : (g + 1) * N] for g in range(PASSES)]
         z_codes = [late_codes[:, PASSES * N :], keep.tile([P, V], U32, name="z_codes1", align_bytes=64)[:]]
 

@@ -133,7 +133,7 @@ def tile_picked_gcn_mlp_none_sub_l_kernel(tc, xT, w1, w2, gate, pos1, pos2, pos3
         vcopy, scopy = nc.vector.tensor_copy, nc.scalar.copy
 
         def group(copy, dst, src):
-            copy(out=dst.rearrange("p (c i) j -> p c j i", i=4), in_=src.rearrange("p j (c i) -> p c j i", i=4))
+            copy(out=dst.rearrange("p (c i) j -> p c j i", i=2), in_=src.rearrange("p j (c i) -> p c j i", i=2))
 
         def quantize(codes, scales, grouped):
             nc.vector.quantize_mx(out=codes.bitcast(FP8X4), scales=scales, in_=grouped.rearrange("p n j -> p (n j)"))
@@ -145,8 +145,8 @@ def tile_picked_gcn_mlp_none_sub_l_kernel(tc, xT, w1, w2, gate, pos1, pos2, pos3
                 group(scopy, w1_grouped[q][:, c : c + P, :], w1_raw[q][:, :, c : c + P])
             if b > PAIRED:
                 c = (PAIRED - a) * P
-                dst = w1_grouped[q][:, c:, :].rearrange("k (u p e) j -> k p j u e", u=2, e=2)
-                src = w1_raw[q][:, :, c:].rearrange("k j (p u e) -> k p j u e", u=2, e=2)
+                dst = w1_grouped[q][:, c:, :].rearrange("k (u p e) j -> k p u j e", u=2, e=2)
+                src = w1_raw[q][:, :, c:].rearrange("k j (p u e) -> k p u j e", u=2, e=2)
                 for r in range(0, P // 2, P // 4):
                     scopy(out=dst[:, r : r + P // 4], in_=src[:, r : r + P // 4])
             for i in range(a, b, 2):

@@ -28,27 +28,36 @@ X_CUTS = (0, 256, 384, 512)
 X_VECTOR = (208, 0, 128)
 X_BANK = (1, 6, 7)
 W1_CUTS = (0, 1, 2, 3, 5, 8)
+VECTOR_W1_TILE = 1
 W2_PIECE = 128
 KB = 1024
-RAW_AT = {"w1_raw2": 0, "w1_raw3": 2 * KB, "w1_raw5": 6 * KB, "w2_raw1": 22 * KB, "prod3_3": 14 * KB, "prod5_0": 18 * KB, "prod5_1": 19 * KB, "prod5_2": 20 * KB, "prod5_3": 21 * KB, "h7": 30 * KB, "w1_grouped5": 36 * KB}
-TENANTS = {
+HOST_AT = {
+    "w1_raw2": 0,
+    "w1_raw3": 2 * KB,
+    "w1_raw5": 6 * KB,
+    "prod3_3": 14 * KB,
+    **{f"prod5_{d}": (18 + d) * KB for d in range(D)},
+    "w2_raw1": 22 * KB,
+    "h7": 30 * KB,
+    "w1_grouped5": 36 * KB,
+}
+FOLLOWS = {
     "h1": ("w1_raw2", 0),
     "h2": ("w1_raw3", 0),
-    "prod1_3": ("w1_raw3", 2),
     "h3": ("w1_raw5", 0),
     "h4": ("w1_raw5", 2),
+    "prod1_3": ("w1_raw3", 2),
     "prod2_1": ("w1_raw5", 4),
     "prod2_2": ("w1_raw5", 5),
     "prod2_3": ("w1_grouped5", 0),
+    "w2_grouped0": ("prod3_3", 0),
     "z_turned1_0": ("w2_raw1", 0),
     "z_turned1_1": ("w2_raw1", 1),
-    "late_codes": ("h7", 0),
-    "w2_grouped0": ("prod3_3", 0),
     **{f"prod{LAST}_{d}": (f"prod5_{d}", 0) for d in (0, 2, 3)},
+    "late_codes": ("h7", 0),
 }
 H_BANK = {1: 0, 2: 1, 3: 6, 4: 7, 5: 4, 6: 5, 7: 0}
-PLAIN = 2
-SHARED = 6
+PLAIN = {0: range(3, 4), PAIRED: range(2), LAST: range(2)}
 FIRST_PASS_BLOCKS = (3, 2, 0, 1)
 
 
@@ -61,7 +70,7 @@ def tile_picked_gcn_mlp_none_sub_l_kernel(tc, xT, w1, w2, gate, pos1, pos2, pos3
         psum = ctx.enter_context(tc.psum_pool(name="psum", bufs=1))
 
         banks = [psum.tile([P, BANK], F32, name=f"bank{b}") for b in range(8)]
-        sum_banks, word_banks, out_banks = [banks[2:4], banks[2:4]], banks[6:8], banks[6:8] + banks[4:6]
+        sum_banks, word_banks, out_banks = banks[2:4], banks[6:8], banks[6:8] + banks[4:6]
         last_banks = out_banks[2:]
 
         pos = [lists.tile([P, V // 16], U16, name=f"pos{d}") for d in range(D)]
@@ -71,11 +80,11 @@ def tile_picked_gcn_mlp_none_sub_l_kernel(tc, xT, w1, w2, gate, pos1, pos2, pos3
         make_identity(nc, ident[:])
 
         def new_tile(name, shape, dtype):
-            if name in RAW_AT:
-                return shared.tile(shape, dtype, name=name, offset=RAW_AT[name], align_bytes=64)
-            if name in TENANTS:
-                raw, kb = TENANTS[name]
-                return shared.tile(shape, dtype, name=name, offset=RAW_AT[raw] + kb * KB, align_bytes=64)
+            if name in HOST_AT:
+                return shared.tile(shape, dtype, name=name, offset=HOST_AT[name], align_bytes=64)
+            if name in FOLLOWS:
+                host, kb = FOLLOWS[name]
+                return shared.tile(shape, dtype, name=name, offset=HOST_AT[host] + kb * KB, align_bytes=64)
             return keep.tile(shape, dtype, name=name, align_bytes=64)
 
         pieces = list(zip(X_CUTS[:-1], X_CUTS[1:]))
@@ -120,10 +129,13 @@ def tile_picked_gcn_mlp_none_sub_l_kernel(tc, xT, w1, w2, gate, pos1, pos2, pos3
         w2_grouped = [new_tile(f"w2_grouped{g}", [P, N, J], BF16) for g in range(PASSES)]
         w2_scales = [keep.tile([P, N], U8, name=f"w2_scales{g}", align_bytes=64) for g in range(PASSES)]
         h = [new_tile(f"h{i}", [P, T], F32) for i in range(TILES)]
-        picked = {i: new_tile(f"picked{i}", [P, PLAIN, V], F32) for i in range(SHARED, TILES)}
-        pairs = {i: new_tile(f"prod{i}_0", [P, PLAIN, V], F32) for i in range(SHARED, TILES)}
+        picked = {i: new_tile(f"picked{i}", [P, len(ds), V], F32) for i, ds in PLAIN.items()}
+        weighed = {i: new_tile(f"prod{i}_{ds[0]}", [P, len(ds), V], F32) for i, ds in PLAIN.items()}
         prods = [
-            [pairs[i][:, d, :] if i in pairs and d < PLAIN else new_tile(f"prod{i}_{d}", [P, V], F32)[:] for d in range(D)]
+            [
+                weighed[i][:, d - PLAIN[i][0], :] if d in PLAIN.get(i, ()) else new_tile(f"prod{i}_{d}", [P, V], F32)[:]
+                for d in range(D)
+            ]
             for i in range(TILES)
         ]
         z_turned = [[new_tile(f"z_turned{g}_{s}", [P, 2, P, 2], BF16)[:] for s in range(HALVES)] for g in range(PASSES)]
@@ -142,7 +154,7 @@ def tile_picked_gcn_mlp_none_sub_l_kernel(tc, xT, w1, w2, gate, pos1, pos2, pos3
             a, b = lots[q]
             for i in range(a, min(b, PAIRED)):
                 c = (i - a) * P
-                group(scopy, w1_grouped[q][:, c : c + P, :], w1_raw[q][:, :, c : c + P])
+                group(vcopy if i == VECTOR_W1_TILE else scopy, w1_grouped[q][:, c : c + P, :], w1_raw[q][:, :, c : c + P])
             if b > PAIRED:
                 c = (PAIRED - a) * P
                 dst = w1_grouped[q][:, c:, :].rearrange("k (u p e) j -> k p u j e", u=2, e=2)
@@ -153,9 +165,9 @@ def tile_picked_gcn_mlp_none_sub_l_kernel(tc, xT, w1, w2, gate, pos1, pos2, pos3
                 e = min(i + 2, b)
                 quantize(w1_codes[:, i * P : e * P], w1_scales[:, i * P : e * P], w1_grouped[q][:, (i - a) * P : (e - a) * P, :])
 
-        def group_w2(copy, g, first, end):
-            for a in range(first, end, W2_PIECE):
-                group(copy, w2_grouped[g][:, a : a + W2_PIECE, :], w2_raw[g][:, :, a : a + W2_PIECE])
+        def group_w2(g):
+            for a in range(0, N, W2_PIECE):
+                group(scopy, w2_grouped[g][:, a : a + W2_PIECE, :], w2_raw[g][:, :, a : a + W2_PIECE])
 
         def project(i, a, b, bank, copy):
             nc.tensor.matmul_mx(
@@ -170,18 +182,19 @@ def tile_picked_gcn_mlp_none_sub_l_kernel(tc, xT, w1, w2, gate, pos1, pos2, pos3
             copy(out=h[i][:, a:b], in_=bank[:, : b - a])
 
         def pick(i):
-            for d in range(PLAIN if i in picked else 0):
-                nc.scalar.activation(picked[i][:, d, :], h[i][:].indirect(pos[d][:]), COPY)
+            for d in PLAIN.get(i, ()):
+                nc.scalar.activation(picked[i][:, d - PLAIN[i][0], :], h[i][:].indirect(pos[d][:]), COPY)
 
         def project_all(i):
             project(i, 0, T, banks[H_BANK[i]], scopy)
             pick(i)
 
         def banks_of(i):
-            return last_banks if i == LAST else sum_banks[i // J]
+            return last_banks if i == LAST else sum_banks
 
         def weigh(i):
-            nc.vector.tensor_tensor(pairs[i][:], picked[i][:], gate_pairs[0][:], MULT)
+            first, last = PLAIN[i][0], PLAIN[i][-1]
+            nc.vector.tensor_tensor(weighed[i][:], picked[i][:], gate_pairs[first // 2][:, first % 2 : last % 2 + 1, :], MULT)
 
         def gather_and_add(i):
             t = i % J
@@ -190,7 +203,9 @@ def tile_picked_gcn_mlp_none_sub_l_kernel(tc, xT, w1, w2, gate, pos1, pos2, pos3
                 steps = steps[:-1] + [(D - 1, (s,)) for s in range(HALVES)]
             for d, halves in steps:
                 v0, v1 = halves[0] * P, (halves[-1] + 1) * P
-                if i not in picked or d >= PLAIN:
+                if i == 0 and d in PLAIN[0]:
+                    weigh(0)
+                if d not in PLAIN.get(i, ()):
                     offsets = pos[d][:, v0 // 16 : v1 // 16]
                     nc.vector.tensor_tensor(prods[i][d][:, v0:v1], h[i][:].indirect(offsets), gates[d][:, v0:v1], MULT)
                 for s in halves:
@@ -207,7 +222,7 @@ def tile_picked_gcn_mlp_none_sub_l_kernel(tc, xT, w1, w2, gate, pos1, pos2, pos3
             g, t0, t1 = i0 // J, i0 % J, (i1 - 1) % J + 1
             scopy(
                 out=z_turned[g][s][:, :, P // J * t0 : P // J * t1, :],
-                in_=sum_banks[g][s][:, t0 * P : t1 * P].rearrange("v (p u e) -> v u p e", u=2, e=2),
+                in_=sum_banks[s][:, t0 * P : t1 * P].rearrange("v (p u e) -> v u p e", u=2, e=2),
             )
 
         def round_pairs(i, s):
@@ -237,9 +252,11 @@ def tile_picked_gcn_mlp_none_sub_l_kernel(tc, xT, w1, w2, gate, pos1, pos2, pos3
             quantize(x_codes[:, a:b], x_scales[:, a:b], x_grouped[c][:])
         for c, (a, b) in enumerate(pieces):
             project(0, a, b, banks[X_BANK[c]], vcopy if b == T else scopy)
+
         prepare_w1(1)
         prepare_w1(2)
         project_all(1)
+        pick(0)
         gather_and_add(0)
         prepare_w1(3)
         project_all(2)
@@ -255,10 +272,11 @@ def tile_picked_gcn_mlp_none_sub_l_kernel(tc, xT, w1, w2, gate, pos1, pos2, pos3
             turn_back(0, s, 0)
             turn_back(0, s, 1)
             interleave(0, s)
+
         gather_and_add(4)
         gather_and_add(5)
-        group_w2(scopy, 0, 0, N)
-        group_w2(scopy, 1, 0, N)
+        for g in range(PASSES):
+            group_w2(g)
         weigh(PAIRED)
         gather_and_add(PAIRED)
         weigh(LAST)

@@ -1,7 +1,6 @@
 from contextlib import ExitStack
 
 import concourse.mybir as mybir
-from concourse.masks import make_identity
 
 F32 = mybir.dt.float32
 BF16 = mybir.dt.bfloat16
@@ -10,6 +9,10 @@ U16 = mybir.dt.uint16
 U8 = mybir.dt.uint8
 FP8X4 = mybir.dt.float8_e4m3fn_x4
 MULT = mybir.AluOpType.mult
+ADD = mybir.AluOpType.add
+MAX = mybir.AluOpType.max
+IS_GE = mybir.AluOpType.is_ge
+IS_EQUAL = mybir.AluOpType.is_equal
 COPY = mybir.ActivationFunctionType.Copy
 
 K, T, D, V, H, N = 512, 512, 4, 256, 1024, 512
@@ -26,39 +29,30 @@ BANK = 512
 
 X_CUTS = (0, 256, 384, 512)
 X_VECTOR = (208, 0, 128)
-X_BANK = (1, 6, 7)
+X_BANK = (0, 1, 4)
 W1_CUTS = (0, 1, 2, 3, 5, 8)
 VECTOR_W1_TILE = 1
-W2_PIECE = 128
-KB = 1024
-HOST_AT = {
-    "w1_raw2": 0,
-    "w1_raw3": 2 * KB,
-    "w1_raw5": 6 * KB,
-    "prod3_3": 14 * KB,
-    **{f"prod5_{d}": (18 + d) * KB for d in range(D)},
-    "w2_raw1": 22 * KB,
-    "h7": 30 * KB,
-    "w1_grouped5": 36 * KB,
+QUAD = 32
+SMALL = 2.0**-32
+TINY = 2.0**-126
+LATE = 128
+Q = 256
+PLACE = {
+    "w1_grouped1": 0, "w1_grouped2": 0,
+    "w1_raw2": 100, "h1": 100,
+    "w1_raw3": 108, "h2": 108, "prod1_1": 116,
+    "w1_raw5": 124, "h4": 124,
+    "prod2_0": 4, "w1_grouped6": 4,
+    "prod2_1": 64, "w1_grouped7": 64,
+    "prod6_0": 28, "w2_middle": 28,
+    "x_first": 72, "ratio0": 72, "ratio1": 76, "ratio2": 80,
+    "prod5_0": 8, "w2_grouped0": 8,
+    "z_turned0_1": 24, "w2_grouped1": 24,
+    "late_grouped": 37, "h7": 40, "late_codes": 44,
 }
-FOLLOWS = {
-    "h1": ("w1_raw2", 0),
-    "h2": ("w1_raw3", 0),
-    "h3": ("w1_raw5", 0),
-    "h4": ("w1_raw5", 2),
-    "prod1_3": ("w1_raw3", 2),
-    "prod2_1": ("w1_raw5", 4),
-    "prod2_2": ("w1_raw5", 5),
-    "prod2_3": ("w1_grouped5", 0),
-    "w2_grouped0": ("prod3_3", 0),
-    "z_turned1_0": ("w2_raw1", 0),
-    "z_turned1_1": ("w2_raw1", 1),
-    **{f"prod{LAST}_{d}": (f"prod5_{d}", 0) for d in (0, 2, 3)},
-    "late_codes": ("h7", 0),
-}
-H_BANK = {1: 0, 2: 1, 3: 6, 4: 7, 5: 4, 6: 5, 7: 0}
-PLAIN = {0: range(3, 4), PAIRED: range(2), LAST: range(2)}
-FIRST_PASS_BLOCKS = (3, 2, 0, 1)
+H_BANK = {1: 5, 2: 0, 3: 1, 4: 6, 5: 7, 6: 0, 7: 1}
+BLOCKS = (2, 3, 0, 1)
+LAST_BLOCKS = (2, 3, 1, 0)
 
 
 def tile_picked_gcn_mlp_none_sub_l_kernel(tc, xT, w1, w2, gate, pos1, pos2, pos3, pos4, out):
@@ -70,25 +64,37 @@ def tile_picked_gcn_mlp_none_sub_l_kernel(tc, xT, w1, w2, gate, pos1, pos2, pos3
         psum = ctx.enter_context(tc.psum_pool(name="psum", bufs=1))
 
         banks = [psum.tile([P, BANK], F32, name=f"bank{b}") for b in range(8)]
-        sum_banks, word_banks, out_banks = banks[2:4], banks[6:8], banks[6:8] + banks[4:6]
-        last_banks = out_banks[2:]
+        sum_banks = [banks[2:4], banks[4:6]]
+        word_banks = banks[2:4]
+        last_banks = banks[6:8]
+        out_places = [word_banks[0][:, :V], word_banks[1][:, :V], last_banks[1][:, :V], last_banks[1][:, V:]]
 
         pos = [lists.tile([P, V // 16], U16, name=f"pos{d}") for d in range(D)]
-        gate_pairs = [keep.tile([P, 2, V], F32, name=f"gates{a}") for a in range(D // 2)]
-        gates = [gate_pairs[d // 2][:, d % 2, :] for d in range(D)]
+        vcopy, scopy = nc.vector.tensor_copy, nc.scalar.copy
+
+        ones = keep.tile([P, QUAD], F32, name="ones")
+        column = keep.tile([P, QUAD], F32, name="column", align_bytes=64)
+        row = keep.tile([P, QUAD], F32, name="row", align_bytes=64)
         ident = keep.tile([P, P], F32, name="ident")
-        make_identity(nc, ident[:])
+        nc.vector.memset(ones[:], 1.0)
+        nc.vector.memset(ident[:], 0.0)
+        nc.vector.tensor_tensor_scan(column[:], ones[:], ones[:], 0.0, MULT, ADD)
+        nc.vector.transpose(row[:], column[:])
+        for a in range(0, P, QUAD):
+            nc.vector.tensor_tensor(ident[a : a + QUAD, a : a + QUAD], column[a : a + QUAD, :], row[a : a + QUAD, :], IS_EQUAL)
+
+        gate_rows = keep.tile([P, V], F32, name="gate_rows")
+        nc.vector.memset(gate_rows[QUAD : 2 * QUAD, :], 0.0)
+        nc.vector.memset(gate_rows[2 * QUAD :, :], 0.0)
+        nc.sync.dma_start(gate_rows[:QUAD, :], gate.rearrange("d p v -> (d p) v")[:: D * P // QUAD, :])
 
         def new_tile(name, shape, dtype):
-            if name in HOST_AT:
-                return shared.tile(shape, dtype, name=name, offset=HOST_AT[name], align_bytes=64)
-            if name in FOLLOWS:
-                host, kb = FOLLOWS[name]
-                return shared.tile(shape, dtype, name=name, offset=HOST_AT[host] + kb * KB, align_bytes=64)
+            if name in PLACE:
+                return shared.tile(shape, dtype, name=name, offset=PLACE[name] * Q, align_bytes=64)
             return keep.tile(shape, dtype, name=name, align_bytes=64)
 
         pieces = list(zip(X_CUTS[:-1], X_CUTS[1:]))
-        x_first = keep.tile([P, J, X_CUTS[2]], F32, name="x_first")
+        x_first = new_tile("x_first", [P, J, X_CUTS[2]], F32)
         x_last = keep.tile([P, J, T - X_CUTS[2]], F32, name="x_last")
         x_raw = [x_first[:, :, : X_CUTS[1]], x_first[:, :, X_CUTS[1] :], x_last[:]]
         lots = list(zip(W1_CUTS[:-1], W1_CUTS[1:]))
@@ -107,42 +113,27 @@ def tile_picked_gcn_mlp_none_sub_l_kernel(tc, xT, w1, w2, gate, pos1, pos2, pos3
         nc.sync.dma_start(x_first[:], x_view[:, :, : X_CUTS[2]])
         nc.sync.dma_start(x_last[:], x_view[:, :, X_CUTS[2] :])
         load_w1(1)
-        gate_view = gate.rearrange("(a d) p v -> a p d v", d=2)
         nc.sync.dma_start(pos[0][:], pos1)
         nc.sync.dma_start(pos[1][:], pos2)
-        nc.sync.dma_start(gate_pairs[0][:], gate_view[0])
         load_w1(2)
-        nc.sync.dma_start(pos[2][:], pos3)
-        nc.sync.dma_start(gate_pairs[1][:], gate_view[1])
         nc.sync.dma_start(pos[3][:], pos4)
+        nc.sync.dma_start(pos[2][:], pos3)
         load_w1(3)
         load_w1(4)
         nc.sync.dma_start(w2_raw[0][:], w2_view[0])
         nc.sync.dma_start(w2_raw[1][:], w2_view[1])
 
-        w1_grouped = [new_tile(f"w1_grouped{a}", [P, (b - a) * P, J], BF16) for a, b in lots]
         w1_codes = keep.tile([P, H], U32, name="w1_codes", align_bytes=64)
         w1_scales = keep.tile([P, H], U8, name="w1_scales", align_bytes=64)
         x_grouped = [keep.tile([P, b - a, J], BF16, name=f"x_grouped{a}", align_bytes=64) for a, b in pieces]
         x_codes = keep.tile([P, T], U32, name="x_codes", align_bytes=64)
         x_scales = keep.tile([P, T], U8, name="x_scales", align_bytes=64)
-        w2_grouped = [new_tile(f"w2_grouped{g}", [P, N, J], BF16) for g in range(PASSES)]
         w2_scales = [keep.tile([P, N], U8, name=f"w2_scales{g}", align_bytes=64) for g in range(PASSES)]
-        h = [new_tile(f"h{i}", [P, T], F32) for i in range(TILES)]
-        picked = {i: new_tile(f"picked{i}", [P, len(ds), V], F32) for i, ds in PLAIN.items()}
-        weighed = {i: new_tile(f"prod{i}_{ds[0]}", [P, len(ds), V], F32) for i, ds in PLAIN.items()}
-        prods = [
-            [
-                weighed[i][:, d - PLAIN[i][0], :] if d in PLAIN.get(i, ()) else new_tile(f"prod{i}_{d}", [P, V], F32)[:]
-                for d in range(D)
-            ]
-            for i in range(TILES)
-        ]
-        z_turned = [[new_tile(f"z_turned{g}_{s}", [P, 2, P, 2], BF16)[:] for s in range(HALVES)] for g in range(PASSES)]
-        z_grouped = [keep.tile([P, V, J], BF16, name=f"z_grouped{g}", align_bytes=64) for g in range(PASSES)]
+        h = {}
+        prods = {}
+        z_turned = {}
+        z_grouped = {}
         z_scales = [keep.tile([P, V], U8, name=f"z_scales{g}", align_bytes=64) for g in range(PASSES)]
-
-        vcopy, scopy = nc.vector.tensor_copy, nc.scalar.copy
 
         def group(copy, dst, src):
             copy(out=dst.rearrange("p (c i) j -> p c j i", i=2), in_=src.rearrange("p j (c i) -> p c j i", i=2))
@@ -150,26 +141,19 @@ def tile_picked_gcn_mlp_none_sub_l_kernel(tc, xT, w1, w2, gate, pos1, pos2, pos3
         def quantize(codes, scales, grouped):
             nc.vector.quantize_mx(out=codes.bitcast(FP8X4), scales=scales, in_=grouped.rearrange("p n j -> p (n j)"))
 
-        def prepare_w1(q):
-            a, b = lots[q]
-            for i in range(a, min(b, PAIRED)):
-                c = (i - a) * P
-                group(vcopy if i == VECTOR_W1_TILE else scopy, w1_grouped[q][:, c : c + P, :], w1_raw[q][:, :, c : c + P])
-            if b > PAIRED:
-                c = (PAIRED - a) * P
-                dst = w1_grouped[q][:, c:, :].rearrange("k (u p e) j -> k p u j e", u=2, e=2)
-                src = w1_raw[q][:, :, c:].rearrange("k j (p u e) -> k p u j e", u=2, e=2)
-                for r in range(0, P // 2, P // 4):
-                    scopy(out=dst[:, r : r + P // 4], in_=src[:, r : r + P // 4])
-            for i in range(a, b, 2):
-                e = min(i + 2, b)
-                quantize(w1_codes[:, i * P : e * P], w1_scales[:, i * P : e * P], w1_grouped[q][:, (i - a) * P : (e - a) * P, :])
+        def prepare_w1(i):
+            q = max(q for q, (a, b) in enumerate(lots) if a <= i)
+            grouped = new_tile(f"w1_grouped{i}", [P, P, J], BF16)
+            if i < PAIRED:
+                c = (i - lots[q][0]) * P
+                group(vcopy if i == VECTOR_W1_TILE else scopy, grouped[:], w1_raw[q][:, :, c : c + P])
+            else:
+                c = (PAIRED - lots[q][0]) * P
+                src = w1_raw[q][:, :, c:].rearrange("k j (p u e) -> k u p j e", u=2, e=2)
+                scopy(out=grouped[:].rearrange("k (p e) j -> k p j e", e=2), in_=src[:, i - PAIRED])
+            quantize(w1_codes[:, i * P : (i + 1) * P], w1_scales[:, i * P : (i + 1) * P], grouped[:])
 
-        def group_w2(g):
-            for a in range(0, N, W2_PIECE):
-                group(scopy, w2_grouped[g][:, a : a + W2_PIECE, :], w2_raw[g][:, :, a : a + W2_PIECE])
-
-        def project(i, a, b, bank, copy):
+        def multiply(i, a, b, bank):
             nc.tensor.matmul_mx(
                 out=bank[:, : b - a],
                 lhsT=w1_codes[:, i * P : (i + 1) * P].bitcast(FP8X4),
@@ -179,61 +163,91 @@ def tile_picked_gcn_mlp_none_sub_l_kernel(tc, xT, w1, w2, gate, pos1, pos2, pos3
                 start=True,
                 stop=True,
             )
-            copy(out=h[i][:, a:b], in_=bank[:, : b - a])
+
+        def project(i, copy):
+            h[i] = new_tile(f"h{i}", [P, T], F32)
+            multiply(i, 0, T, banks[H_BANK[i]])
+            copy(out=h[i][:], in_=banks[H_BANK[i]][:])
+
+        factor = keep.tile([P, HALVES], F32, name="factor")
+        ratios = [new_tile(f"ratio{d}", [P, V], F32) for d in range(D - 1)]
+
+        def make_ratios():
+            for s in range(HALVES):
+                nc.tensor.transpose(banks[6][:, s * P : (s + 1) * P], gate_rows[:, s * P : (s + 1) * P], ident[:])
+            g = banks[6][:, : HALVES * P].rearrange("v (s j) -> v s j", s=HALVES)[:, :, 0:QUAD:QUAD // D]
+            weights = keep.tile([P, 2, D], F32, name="weights")
+            bounds = keep.tile([P, HALVES, 2 * D + 1], F32, name="bounds")
+            for n, sign in enumerate((1.0, -1.0)):
+                nc.vector.memset(weights[:, n, : D - 1], sign * SMALL)
+                nc.vector.memset(weights[:, n, D - 1 :], sign)
+            nc.vector.memset(bounds[:, :, 2 * D :], TINY)
+            nc.vector.tensor_tensor(
+                bounds[:, :, : 2 * D].rearrange("v s (n d) -> v s n d", n=2),
+                g.unsqueeze(2).to_broadcast([P, HALVES, 2, D]),
+                weights[:].unsqueeze(1).to_broadcast([P, HALVES, 2, D]),
+                MULT,
+            )
+            twice_sign = keep.tile([P, HALVES], F32, name="twice_sign")
+            nc.vector.tensor_scalar(twice_sign[:], g[:, :, D - 1], 0.0, 2.0, IS_GE, MULT)
+            size = keep.tile([P, HALVES], F32, name="size")
+            nc.vector.tensor_reduce(size[:], bounds[:], mybir.AxisListType.X, MAX)
+            nc.vector.scalar_tensor_tensor(factor[:], twice_sign[:], -1.0, size[:], ADD, MULT)
+            inverse = keep.tile([P, HALVES], F32, name="inverse")
+            nc.vector.reciprocal(inverse[:], factor[:])
+            columns = keep.tile([P, HALVES, D - 1], F32, name="columns")
+            nc.vector.tensor_tensor(columns[:], g[:, :, : D - 1], inverse[:].unsqueeze(2).to_broadcast([P, HALVES, D - 1]), MULT)
+            for d in range(D - 1):
+                place = banks[7 - d // 2][:, d % 2 * V : (d % 2 + 1) * V]
+                for s in range(HALVES):
+                    nc.tensor.transpose(place[:, s * P : (s + 1) * P], columns[:, s, d : d + 1].to_broadcast([P, P]), ident[:])
+            for d in range(D - 1):
+                scopy(out=ratios[d][:], in_=banks[7 - d // 2][:, d % 2 * V : (d % 2 + 1) * V])
+
+        def bank_of(i, s):
+            return last_banks[s] if i == LAST else sum_banks[i // J][s]
+
+        def add(i, d, halves=(0, 1), order=range(D)):
+            t = i % J
+            for s in halves:
+                nc.tensor.matmul(
+                    bank_of(i, s)[:, t * P : (t + 1) * P],
+                    lhsT=prods[i, d][:, s * P : (s + 1) * P],
+                    rhs=ident[:],
+                    start=(d == order[0]),
+                    stop=(d == order[-1]),
+                    is_transpose=True,
+                )
+
+        def fused(i, d):
+            prods[i, d] = new_tile(f"prod{i}_{d}", [P, V], F32)
+            nc.vector.tensor_tensor(prods[i, d][:], h[i][:].indirect(pos[d][:]), ratios[d][:], MULT)
 
         def pick(i):
-            for d in PLAIN.get(i, ()):
-                nc.scalar.activation(picked[i][:, d - PLAIN[i][0], :], h[i][:].indirect(pos[d][:]), COPY)
-
-        def project_all(i):
-            project(i, 0, T, banks[H_BANK[i]], scopy)
-            pick(i)
-
-        def banks_of(i):
-            return last_banks if i == LAST else sum_banks
-
-        def weigh(i):
-            first, last = PLAIN[i][0], PLAIN[i][-1]
-            nc.vector.tensor_tensor(weighed[i][:], picked[i][:], gate_pairs[first // 2][:, first % 2 : last % 2 + 1, :], MULT)
-
-        def gather_and_add(i):
-            t = i % J
-            steps = [(d, (0, 1)) for d in range(D)]
-            if i == LAST:
-                steps = steps[:-1] + [(D - 1, (s,)) for s in range(HALVES)]
-            for d, halves in steps:
-                v0, v1 = halves[0] * P, (halves[-1] + 1) * P
-                if i == 0 and d in PLAIN[0]:
-                    weigh(0)
-                if d not in PLAIN.get(i, ()):
-                    offsets = pos[d][:, v0 // 16 : v1 // 16]
-                    nc.vector.tensor_tensor(prods[i][d][:, v0:v1], h[i][:].indirect(offsets), gates[d][:, v0:v1], MULT)
-                for s in halves:
-                    nc.tensor.matmul(
-                        banks_of(i)[s][:, t * P : (t + 1) * P],
-                        lhsT=prods[i][d][:, s * P : (s + 1) * P],
-                        rhs=ident[:],
-                        start=(d == 0),
-                        stop=(d == D - 1),
-                        is_transpose=True,
-                    )
+            prods[i, D - 1] = new_tile(f"prod{i}_{D - 1}", [P, V], F32)
+            nc.scalar.activation(prods[i, D - 1][:], h[i][:].indirect(pos[D - 1][:]), COPY)
 
         def round_sums(i0, i1, s):
             g, t0, t1 = i0 // J, i0 % J, (i1 - 1) % J + 1
-            scopy(
-                out=z_turned[g][s][:, :, P // J * t0 : P // J * t1, :],
-                in_=sum_banks[s][:, t0 * P : t1 * P].rearrange("v (p u e) -> v u p e", u=2, e=2),
+            z_turned[g, s] = new_tile(f"z_turned{g}_{s}", [P, 2, P, 2], BF16)
+            nc.scalar.activation(
+                z_turned[g, s][:, :, P // J * t0 : P // J * t1, :],
+                sum_banks[g][s][:, t0 * P : t1 * P].rearrange("v (p u e) -> v u p e", u=2, e=2),
+                COPY,
+                scale=factor[:, s : s + 1],
             )
 
         def round_pairs(i, s):
             t = i % J
-            scopy(
-                out=z_turned[1][s][:, i - PAIRED, P // 2 :, :].rearrange("v p e -> v (p e)"),
-                in_=banks_of(i)[s][:, t * P : (t + 1) * P],
+            nc.scalar.activation(
+                z_turned[1, s][:, i - PAIRED, P // 2 :, :].rearrange("v p e -> v (p e)"),
+                bank_of(i, s)[:, t * P : (t + 1) * P],
+                COPY,
+                scale=factor[:, s : s + 1],
             )
 
         def turn_back(g, s, u):
-            words = z_turned[g][s][:, u, :, :].rearrange("v p e -> v (p e)").bitcast(F32)
+            words = z_turned[g, s][:, u, :, :].rearrange("v p e -> v (p e)").bitcast(F32)
             nc.tensor.transpose(word_banks[s][:, u * P : (u + 1) * P], words, ident[:])
 
         def interleave(g, s):
@@ -250,73 +264,94 @@ def tile_picked_gcn_mlp_none_sub_l_kernel(tc, xT, w1, w2, gate, pos1, pos2, pos3
             if cut < b - a:
                 group(scopy, x_grouped[c][:, cut:, :], x_raw[c][:, :, cut:])
             quantize(x_codes[:, a:b], x_scales[:, a:b], x_grouped[c][:])
+        make_ratios()
+        h[0] = new_tile("h0", [P, T], F32)
         for c, (a, b) in enumerate(pieces):
-            project(0, a, b, banks[X_BANK[c]], vcopy if b == T else scopy)
+            multiply(0, a, b, banks[X_BANK[c]])
+            (vcopy if b == T else scopy)(out=h[0][:, a:b], in_=banks[X_BANK[c]][:, : b - a])
 
         prepare_w1(1)
         prepare_w1(2)
-        project_all(1)
-        pick(0)
-        gather_and_add(0)
-        prepare_w1(3)
-        project_all(2)
-        gather_and_add(1)
-        prepare_w1(4)
-        for i in range(3, TILES):
-            project_all(i)
-        gather_and_add(2)
-        gather_and_add(3)
-        for s in range(HALVES):
-            round_sums(0, J, s)
+        for i in range(LAST):
+            project(i + 1, scopy)
+            pick(i)
+            if i == 1:
+                prepare_w1(5)
+            if i >= J and i - J < HALVES:
+                round_sums(0, J, i - J)
+            for d in range(D - 1):
+                fused(i, d)
+                add(i, d)
+            add(i, D - 1)
+            if i in (0, 2):
+                for k in range(2):
+                    prepare_w1(3 * i // 2 + 3 + k)
+        pick(LAST)
+        w2_grouped = [new_tile("w2_grouped0", [P, N, J], BF16)]
+        group(vcopy, w2_grouped[0][:], w2_raw[0][:])
+        z_grouped[0] = new_tile("z_grouped0", [P, V, J], BF16)
         for s in range(HALVES):
             turn_back(0, s, 0)
             turn_back(0, s, 1)
             interleave(0, s)
-
-        gather_and_add(4)
-        gather_and_add(5)
-        for g in range(PASSES):
-            group_w2(g)
-        weigh(PAIRED)
-        gather_and_add(PAIRED)
-        weigh(LAST)
+        w2_grouped.append(new_tile("w2_grouped1", [P, P, J], BF16))
+        middle = new_tile("w2_middle", [P, 2 * P, J], BF16)
+        group(vcopy, middle[:], w2_raw[1][:, :, LATE : LATE + 2 * P])
+        group(scopy, w2_grouped[1][:], w2_raw[1][:, :, LATE + 2 * P :])
         for s in range(HALVES):
             round_sums(J, PAIRED, s)
+        for s in range(HALVES):
             round_pairs(PAIRED, s)
             turn_back(1, s, 0)
-        gather_and_add(LAST)
+        order = (3, 0, 1, 2)
+        add(LAST, 3, order=order)
+        for d in range(2):
+            fused(LAST, d)
+            add(LAST, d, order=order)
+        prods[LAST, 2] = new_tile(f"prod{LAST}_2", [P, V], F32)
+        for s in range(HALVES):
+            cols = slice(s * P, (s + 1) * P)
+            offsets = pos[2][:, s * P // 16 : (s + 1) * P // 16]
+            nc.vector.tensor_tensor(prods[LAST, 2][:, cols], h[LAST][:].indirect(offsets), ratios[2][:, cols], MULT)
+            add(LAST, 2, (s,), order=order)
 
         late_codes = new_tile("late_codes", [P, PASSES * N + V], U32)
         w2_codes = [late_codes[:, g * N : (g + 1) * N] for g in range(PASSES)]
         z_codes = [late_codes[:, PASSES * N :], keep.tile([P, V], U32, name="z_codes1", align_bytes=64)[:]]
+        z_grouped[1] = new_tile("z_grouped1", [P, V, J], BF16)
 
-        def quantize_w2(g, first, end):
-            cols = slice(first * P, end * P)
-            quantize(w2_codes[g][:, cols], w2_scales[g][:, cols], w2_grouped[g][:, cols, :])
+        def quantize_w2(g, cols, grouped):
+            quantize(w2_codes[g][:, cols], w2_scales[g][:, cols], grouped)
 
+        late_grouped = new_tile("late_grouped", [P, LATE, J], BF16)
         quantize(z_codes[0], z_scales[0][:], z_grouped[0][:])
-        quantize_w2(0, 3, 4)
-        quantize_w2(1, 0, 4)
-        quantize_w2(0, 2, 3)
-        quantize_w2(0, 0, 2)
+        quantize_w2(0, slice(2 * P, N), w2_grouped[0][:, 2 * P :, :])
+        group(vcopy, late_grouped[:], w2_raw[1][:, :, :LATE])
+        quantize_w2(1, slice(3 * P, N), w2_grouped[1][:])
+        quantize_w2(1, slice(P, 3 * P), middle[:])
+        quantize_w2(0, slice(0, 2 * P), w2_grouped[0][:, : 2 * P, :])
+        quantize_w2(1, slice(0, LATE), late_grouped[:])
         for s in range(HALVES):
             round_pairs(LAST, s)
             turn_back(1, s, 1)
             interleave(1, s)
             quantize(z_codes[1][:, s * P : (s + 1) * P], z_scales[1][:, s * P : (s + 1) * P], z_grouped[1][:, s * P : (s + 1) * P, :])
-        for g, blocks in enumerate((FIRST_PASS_BLOCKS, range(N // P))):
-            for a in blocks:
+        for g in range(PASSES):
+            for a in (BLOCKS, LAST_BLOCKS)[g]:
                 nc.tensor.matmul_mx(
-                    out=out_banks[a][:, :V],
+                    out=out_places[a],
                     lhsT=w2_codes[g][:, a * P : (a + 1) * P].bitcast(FP8X4),
                     lhsT_scale=w2_scales[g][:, a * P : (a + 1) * P],
                     rhs=z_codes[g].bitcast(FP8X4),
                     rhs_scale=z_scales[g][:],
-                    start=(g == 0),
-                    stop=(g == PASSES - 1),
+                    start=(g == 0 and a != 3),
+                    stop=(g == PASSES - 1 and a != 2),
                 )
 
-        for a in range(N // P):
+        both = keep.tile([P, 2, V], F32, name="result23")
+        vcopy(out=both[:].rearrange("p a v -> p (a v)"), in_=last_banks[1][:])
+        nc.sync.dma_start(out=out_view[:, 2:, :], in_=both[:])
+        for a in (1, 0):
             result = keep.tile([P, V], F32, name=f"result{a}")
-            (scopy if a % 2 else vcopy)(out=result[:], in_=out_banks[a][:, :V])
-            (nc.scalar if a == N // P - 1 else nc.sync).dma_start(out=out_view[:, a, :], in_=result[:])
+            scopy(out=result[:], in_=out_places[a])
+            (nc.sync if a else nc.scalar).dma_start(out=out_view[:, a, :], in_=result[:])

@@ -41,13 +41,10 @@ PLACE = {
     "w1_grouped1": 0, "w1_grouped2": 0,
     "w1_raw2": 100, "h1": 100,
     "w1_raw3": 108, "h2": 108, "prod1_1": 116,
-    "w1_raw5": 124, "h4": 124,
-    "prod2_0": 4, "w1_grouped6": 4,
-    "prod2_1": 64, "w1_grouped7": 64,
-    "prod6_0": 28, "w2_middle": 28,
+    "w1_raw5": 124, "h4": 124, "prod1_3": 132, "prod2_3": 136, "prod3_3": 140,
     "x_first": 72, "ratio0": 72, "ratio1": 76, "ratio2": 80,
     "prod5_0": 8, "w2_grouped0": 8,
-    "z_turned0_1": 24, "w2_grouped1": 24,
+    "prod5_1": 24, "w2_grouped1": 24,
     "late_grouped": 37, "h7": 40, "late_codes": 44,
 }
 H_BANK = {1: 5, 2: 0, 3: 1, 4: 6, 5: 7, 6: 0, 7: 1}
@@ -65,9 +62,9 @@ def tile_picked_gcn_mlp_none_sub_l_kernel(tc, xT, w1, w2, gate, pos1, pos2, pos3
 
         banks = [psum.tile([P, BANK], F32, name=f"bank{b}") for b in range(8)]
         sum_banks = [banks[2:4], banks[4:6]]
-        word_banks = banks[2:4]
-        last_banks = banks[6:8]
-        out_places = [word_banks[0][:, :V], word_banks[1][:, :V], last_banks[1][:, :V], last_banks[1][:, V:]]
+        word_banks = sum_banks
+        last_banks = banks[2:4]
+        out_places = [word_banks[1][0][:, :V], word_banks[1][1][:, :V], last_banks[1][:, :V], last_banks[1][:, V:]]
 
         pos = [lists.tile([P, V // 16], U16, name=f"pos{d}") for d in range(D)]
         vcopy, scopy = nc.vector.tensor_copy, nc.scalar.copy
@@ -205,17 +202,17 @@ def tile_picked_gcn_mlp_none_sub_l_kernel(tc, xT, w1, w2, gate, pos1, pos2, pos3
                 scopy(out=ratios[d][:], in_=banks[7 - d // 2][:, d % 2 * V : (d % 2 + 1) * V])
 
         def bank_of(i, s):
-            return last_banks[s] if i == LAST else sum_banks[i // J][s]
+            return banks[6 + s] if i == PAIRED else sum_banks[i in (4, 5)][s]
 
-        def add(i, d, halves=(0, 1), order=range(D)):
+        def add(i, d, halves=(0, 1)):
             t = i % J
             for s in halves:
                 nc.tensor.matmul(
                     bank_of(i, s)[:, t * P : (t + 1) * P],
                     lhsT=prods[i, d][:, s * P : (s + 1) * P],
                     rhs=ident[:],
-                    start=(d == order[0]),
-                    stop=(d == order[-1]),
+                    start=(i, d) in ((0, 0), (4, 0), (6, 3), (7, 3)),
+                    stop=(i, d) in ((3, 3), (5, 3), (6, 2), (7, 2)),
                     is_transpose=True,
                 )
 
@@ -248,12 +245,12 @@ def tile_picked_gcn_mlp_none_sub_l_kernel(tc, xT, w1, w2, gate, pos1, pos2, pos3
 
         def turn_back(g, s, u):
             words = z_turned[g, s][:, u, :, :].rearrange("v p e -> v (p e)").bitcast(F32)
-            nc.tensor.transpose(word_banks[s][:, u * P : (u + 1) * P], words, ident[:])
+            nc.tensor.transpose(word_banks[g][s][:, u * P : (u + 1) * P], words, ident[:])
 
         def interleave(g, s):
             scopy(
                 out=z_grouped[g][:, s * P : (s + 1) * P, :].rearrange("p v j -> p (v j)").bitcast(F32).rearrange("p (v u) -> p v u", u=2),
-                in_=word_banks[s][:, : 2 * P].rearrange("p (u v) -> p v u", u=2),
+                in_=word_banks[g][s][:, : 2 * P].rearrange("p (u v) -> p v u", u=2),
             )
 
         prepare_w1(0)
@@ -272,48 +269,66 @@ def tile_picked_gcn_mlp_none_sub_l_kernel(tc, xT, w1, w2, gate, pos1, pos2, pos3
 
         prepare_w1(1)
         prepare_w1(2)
-        for i in range(LAST):
-            project(i + 1, scopy)
-            pick(i)
-            if i == 1:
-                prepare_w1(5)
-            if i >= J and i - J < HALVES:
-                round_sums(0, J, i - J)
+        def gather(i):
             for d in range(D - 1):
                 fused(i, d)
                 add(i, d)
+
+        def pick_and_add(i):
+            pick(i)
             add(i, D - 1)
-            if i in (0, 2):
-                for k in range(2):
-                    prepare_w1(3 * i // 2 + 3 + k)
-        pick(LAST)
+
+        project(1, scopy)
+        gather(0)
+        pick_and_add(0)
+        prepare_w1(3)
+        prepare_w1(4)
+        project(2, scopy)
+        gather(1)
+        project(3, scopy)
+        for k in range(5, TILES):
+            prepare_w1(k)
+        gather(2)
+        project(4, scopy)
+        gather(3)
+        pick_and_add(1)
+        project(5, scopy)
+        pick_and_add(2)
+        pick_and_add(3)
+        project(6, scopy)
+        project(7, scopy)
+        gather(4)
+        z_grouped[0] = new_tile("z_grouped0", [P, V, J], BF16)
+        for s in range(HALVES):
+            round_sums(0, J, s)
+        gather(5)
         w2_grouped = [new_tile("w2_grouped0", [P, N, J], BF16)]
         group(vcopy, w2_grouped[0][:], w2_raw[0][:])
-        z_grouped[0] = new_tile("z_grouped0", [P, V, J], BF16)
+        w2_grouped.append(new_tile("w2_grouped1", [P, N - LATE, J], BF16))
+        group(vcopy, w2_grouped[1][:], w2_raw[1][:, :, LATE:])
+        pick_and_add(4)
+        pick_and_add(5)
         for s in range(HALVES):
             turn_back(0, s, 0)
             turn_back(0, s, 1)
             interleave(0, s)
-        w2_grouped.append(new_tile("w2_grouped1", [P, P, J], BF16))
-        middle = new_tile("w2_middle", [P, 2 * P, J], BF16)
-        group(vcopy, middle[:], w2_raw[1][:, :, LATE : LATE + 2 * P])
-        group(scopy, w2_grouped[1][:], w2_raw[1][:, :, LATE + 2 * P :])
+        pick_and_add(6)
+        pick_and_add(7)
+        gather(6)
         for s in range(HALVES):
             round_sums(J, PAIRED, s)
         for s in range(HALVES):
             round_pairs(PAIRED, s)
             turn_back(1, s, 0)
-        order = (3, 0, 1, 2)
-        add(LAST, 3, order=order)
         for d in range(2):
             fused(LAST, d)
-            add(LAST, d, order=order)
+            add(LAST, d)
         prods[LAST, 2] = new_tile(f"prod{LAST}_2", [P, V], F32)
         for s in range(HALVES):
             cols = slice(s * P, (s + 1) * P)
             offsets = pos[2][:, s * P // 16 : (s + 1) * P // 16]
             nc.vector.tensor_tensor(prods[LAST, 2][:, cols], h[LAST][:].indirect(offsets), ratios[2][:, cols], MULT)
-            add(LAST, 2, (s,), order=order)
+            add(LAST, 2, (s,))
 
         late_codes = new_tile("late_codes", [P, PASSES * N + V], U32)
         w2_codes = [late_codes[:, g * N : (g + 1) * N] for g in range(PASSES)]
@@ -327,8 +342,7 @@ def tile_picked_gcn_mlp_none_sub_l_kernel(tc, xT, w1, w2, gate, pos1, pos2, pos3
         quantize(z_codes[0], z_scales[0][:], z_grouped[0][:])
         quantize_w2(0, slice(2 * P, N), w2_grouped[0][:, 2 * P :, :])
         group(vcopy, late_grouped[:], w2_raw[1][:, :, :LATE])
-        quantize_w2(1, slice(3 * P, N), w2_grouped[1][:])
-        quantize_w2(1, slice(P, 3 * P), middle[:])
+        quantize_w2(1, slice(LATE, N), w2_grouped[1][:])
         quantize_w2(0, slice(0, 2 * P), w2_grouped[0][:, : 2 * P, :])
         quantize_w2(1, slice(0, LATE), late_grouped[:])
         for s in range(HALVES):

@@ -43,8 +43,8 @@ PLACE = {
     "w1_raw3": 108, "h2": 108, "prod1_1": 116,
     "w1_raw5": 124, "h4": 124, "prod1_3": 132, "prod2_3": 136, "prod3_3": 140,
     "x_first": 72, "ratio0": 72, "ratio1": 76, "ratio2": 80,
-    "prod5_0": 8, "w2_grouped0": 8,
-    "prod5_1": 24, "w2_grouped1": 24,
+    "prod3_0": 8, "w2_grouped0": 8,
+    "prod4_1": 24, "w2_grouped1": 24,
     "late_grouped": 37, "h7": 40, "late_codes": 44,
 }
 H_BANK = {1: 5, 2: 0, 3: 1, 4: 6, 5: 7, 6: 0, 7: 1}
@@ -291,6 +291,8 @@ def tile_picked_gcn_mlp_none_sub_l_kernel(tc, xT, w1, w2, gate, pos1, pos2, pos3
         gather(2)
         project(4, scopy)
         gather(3)
+        w2_grouped = [new_tile("w2_grouped0", [P, N, J], BF16)]
+        group(vcopy, w2_grouped[0][:], w2_raw[0][:])
         pick_and_add(1)
         project(5, scopy)
         pick_and_add(2)
@@ -298,14 +300,12 @@ def tile_picked_gcn_mlp_none_sub_l_kernel(tc, xT, w1, w2, gate, pos1, pos2, pos3
         project(6, scopy)
         project(7, scopy)
         gather(4)
+        w2_grouped.append(new_tile("w2_grouped1", [P, N - LATE, J], BF16))
+        group(vcopy, w2_grouped[1][:], w2_raw[1][:, :, LATE:])
         z_grouped[0] = new_tile("z_grouped0", [P, V, J], BF16)
         for s in range(HALVES):
             round_sums(0, J, s)
         gather(5)
-        w2_grouped = [new_tile("w2_grouped0", [P, N, J], BF16)]
-        group(vcopy, w2_grouped[0][:], w2_raw[0][:])
-        w2_grouped.append(new_tile("w2_grouped1", [P, N - LATE, J], BF16))
-        group(vcopy, w2_grouped[1][:], w2_raw[1][:, :, LATE:])
         pick_and_add(4)
         pick_and_add(5)
         for s in range(HALVES):

@@ -40,11 +40,12 @@ Q = 256
 PLACE = {
     "w1_grouped1": 0, "w1_grouped2": 0,
     "w1_raw2": 100, "h1": 100,
-    "w1_raw3": 108, "h2": 108, "prod1_1": 116,
-    "w1_raw5": 124, "h4": 124, "prod1_3": 132, "prod2_3": 136, "prod3_3": 140,
+    "w1_raw3": 108, "h2": 108, "prod1_1": 116, "prod1_3": 120,
+    "w1_raw5": 124, "h4": 124, "prod2_3": 136, "prod3_3": 140,
     "x_first": 72, "ratio0": 72, "ratio1": 76, "ratio2": 80,
     "prod3_0": 8, "w2_grouped0": 8,
     "prod4_1": 24, "w2_grouped1": 24,
+    "z_turned0_1": 148, "end_grouped": 148,
     "late_grouped": 37, "h7": 40, "late_codes": 44,
 }
 H_BANK = {1: 5, 2: 0, 3: 1, 4: 6, 5: 7, 6: 0, 7: 1}
@@ -80,10 +81,10 @@ def tile_picked_gcn_mlp_none_sub_l_kernel(tc, xT, w1, w2, gate, pos1, pos2, pos3
         for a in range(0, P, QUAD):
             nc.vector.tensor_tensor(ident[a : a + QUAD, a : a + QUAD], column[a : a + QUAD, :], row[a : a + QUAD, :], IS_EQUAL)
 
-        gate_rows = keep.tile([P, V], F32, name="gate_rows")
+        gate_rows = keep.tile([P, P], F32, name="gate_rows")
         nc.vector.memset(gate_rows[QUAD : 2 * QUAD, :], 0.0)
         nc.vector.memset(gate_rows[2 * QUAD :, :], 0.0)
-        nc.sync.dma_start(gate_rows[:QUAD, :], gate.rearrange("d p v -> (d p) v")[:: D * P // QUAD, :])
+        nc.sync.dma_start(gate_rows[:QUAD, :], gate.rearrange("d p (s e) -> (d p s) e", s=HALVES)[:: D * P * HALVES // QUAD + 1, :])
 
         def new_tile(name, shape, dtype):
             if name in PLACE:
@@ -122,7 +123,7 @@ def tile_picked_gcn_mlp_none_sub_l_kernel(tc, xT, w1, w2, gate, pos1, pos2, pos3
 
         w1_codes = keep.tile([P, H], U32, name="w1_codes", align_bytes=64)
         w1_scales = keep.tile([P, H], U8, name="w1_scales", align_bytes=64)
-        x_grouped = [keep.tile([P, b - a, J], BF16, name=f"x_grouped{a}", align_bytes=64) for a, b in pieces]
+        x_grouped = [new_tile(f"x_grouped{a}", [P, b - a, J], BF16) for a, b in pieces]
         x_codes = keep.tile([P, T], U32, name="x_codes", align_bytes=64)
         x_scales = keep.tile([P, T], U8, name="x_scales", align_bytes=64)
         w2_scales = [keep.tile([P, N], U8, name=f"w2_scales{g}", align_bytes=64) for g in range(PASSES)]
@@ -170,9 +171,8 @@ def tile_picked_gcn_mlp_none_sub_l_kernel(tc, xT, w1, w2, gate, pos1, pos2, pos3
         ratios = [new_tile(f"ratio{d}", [P, V], F32) for d in range(D - 1)]
 
         def make_ratios():
-            for s in range(HALVES):
-                nc.tensor.transpose(banks[6][:, s * P : (s + 1) * P], gate_rows[:, s * P : (s + 1) * P], ident[:])
-            g = banks[6][:, : HALVES * P].rearrange("v (s j) -> v s j", s=HALVES)[:, :, 0:QUAD:QUAD // D]
+            nc.tensor.transpose(banks[6][:, :P], gate_rows[:], ident[:])
+            g = banks[6][:, :QUAD].rearrange("v (d r s) -> v r s d", d=D, s=HALVES)[:, 0]
             weights = keep.tile([P, 2, D], F32, name="weights")
             bounds = keep.tile([P, HALVES, 2 * D + 1], F32, name="bounds")
             for n, sign in enumerate((1.0, -1.0)):
@@ -189,15 +189,20 @@ def tile_picked_gcn_mlp_none_sub_l_kernel(tc, xT, w1, w2, gate, pos1, pos2, pos3
             nc.vector.tensor_scalar(twice_sign[:], g[:, :, D - 1], 0.0, 2.0, IS_GE, MULT)
             size = keep.tile([P, HALVES], F32, name="size")
             nc.vector.tensor_reduce(size[:], bounds[:], mybir.AxisListType.X, MAX)
+            signed = keep.tile([P, HALVES, D - 1], F32, name="signed")
+            wide = [P, HALVES, D - 1]
+            nc.vector.scalar_tensor_tensor(signed[:], twice_sign[:].unsqueeze(2).to_broadcast(wide), -1.0, g[:, :, : D - 1], ADD, MULT)
+            inverse = new_tile("inverse", [P, HALVES], F32)
+            nc.vector.reciprocal(inverse[:], size[:])
             nc.vector.scalar_tensor_tensor(factor[:], twice_sign[:], -1.0, size[:], ADD, MULT)
-            inverse = keep.tile([P, HALVES], F32, name="inverse")
-            nc.vector.reciprocal(inverse[:], factor[:])
-            columns = keep.tile([P, HALVES, D - 1], F32, name="columns")
-            nc.vector.tensor_tensor(columns[:], g[:, :, : D - 1], inverse[:].unsqueeze(2).to_broadcast([P, HALVES, D - 1]), MULT)
+            columns = keep.tile(wide, F32, name="columns")
+            nc.vector.tensor_tensor(columns[:], signed[:], inverse[:].unsqueeze(2).to_broadcast(wide), MULT)
             for d in range(D - 1):
                 place = banks[7 - d // 2][:, d % 2 * V : (d % 2 + 1) * V]
                 for s in range(HALVES):
                     nc.tensor.transpose(place[:, s * P : (s + 1) * P], columns[:, s, d : d + 1].to_broadcast([P, P]), ident[:])
+
+        def copy_ratios():
             for d in range(D - 1):
                 scopy(out=ratios[d][:], in_=banks[7 - d // 2][:, d % 2 * V : (d % 2 + 1) * V])
 
@@ -253,6 +258,7 @@ def tile_picked_gcn_mlp_none_sub_l_kernel(tc, xT, w1, w2, gate, pos1, pos2, pos3
                 in_=word_banks[g][s][:, : 2 * P].rearrange("p (u v) -> p v u", u=2),
             )
 
+        make_ratios()
         prepare_w1(0)
         for c, (a, b) in enumerate(pieces):
             cut = X_VECTOR[c]
@@ -261,7 +267,7 @@ def tile_picked_gcn_mlp_none_sub_l_kernel(tc, xT, w1, w2, gate, pos1, pos2, pos3
             if cut < b - a:
                 group(scopy, x_grouped[c][:, cut:, :], x_raw[c][:, :, cut:])
             quantize(x_codes[:, a:b], x_scales[:, a:b], x_grouped[c][:])
-        make_ratios()
+        copy_ratios()
         h[0] = new_tile("h0", [P, T], F32)
         for c, (a, b) in enumerate(pieces):
             multiply(0, a, b, banks[X_BANK[c]])
@@ -285,6 +291,7 @@ def tile_picked_gcn_mlp_none_sub_l_kernel(tc, xT, w1, w2, gate, pos1, pos2, pos3
         prepare_w1(4)
         project(2, scopy)
         gather(1)
+        pick_and_add(1)
         project(3, scopy)
         for k in range(5, TILES):
             prepare_w1(k)
@@ -293,15 +300,14 @@ def tile_picked_gcn_mlp_none_sub_l_kernel(tc, xT, w1, w2, gate, pos1, pos2, pos3
         gather(3)
         w2_grouped = [new_tile("w2_grouped0", [P, N, J], BF16)]
         group(vcopy, w2_grouped[0][:], w2_raw[0][:])
-        pick_and_add(1)
         project(5, scopy)
         pick_and_add(2)
         pick_and_add(3)
         project(6, scopy)
         project(7, scopy)
         gather(4)
-        w2_grouped.append(new_tile("w2_grouped1", [P, N - LATE, J], BF16))
-        group(vcopy, w2_grouped[1][:], w2_raw[1][:, :, LATE:])
+        w2_grouped.append(new_tile("w2_grouped1", [P, P, J], BF16))
+        group(vcopy, w2_grouped[1][:], w2_raw[1][:, :, LATE : 2 * P])
         z_grouped[0] = new_tile("z_grouped0", [P, V, J], BF16)
         for s in range(HALVES):
             round_sums(0, J, s)
@@ -315,6 +321,9 @@ def tile_picked_gcn_mlp_none_sub_l_kernel(tc, xT, w1, w2, gate, pos1, pos2, pos3
         pick_and_add(6)
         pick_and_add(7)
         gather(6)
+        end_grouped = new_tile("end_grouped", [P, 2 * P, J], BF16)
+        for a in range(0, 2 * P, P):
+            group(scopy, end_grouped[:, a : a + P, :], w2_raw[1][:, :, 2 * P + a : 3 * P + a])
         for s in range(HALVES):
             round_sums(J, PAIRED, s)
         for s in range(HALVES):
@@ -342,8 +351,9 @@ def tile_picked_gcn_mlp_none_sub_l_kernel(tc, xT, w1, w2, gate, pos1, pos2, pos3
         quantize(z_codes[0], z_scales[0][:], z_grouped[0][:])
         quantize_w2(0, slice(2 * P, N), w2_grouped[0][:, 2 * P :, :])
         group(vcopy, late_grouped[:], w2_raw[1][:, :, :LATE])
-        quantize_w2(1, slice(LATE, N), w2_grouped[1][:])
+        quantize_w2(1, slice(2 * P, N), end_grouped[:])
         quantize_w2(0, slice(0, 2 * P), w2_grouped[0][:, : 2 * P, :])
+        quantize_w2(1, slice(LATE, 2 * P), w2_grouped[1][:])
         quantize_w2(1, slice(0, LATE), late_grouped[:])
         for s in range(HALVES):
             round_pairs(LAST, s)

@@ -46,11 +46,10 @@ PLACE = {
     "prod3_0": 8, "w2_grouped0": 8,
     "prod4_1": 24, "w2_grouped1": 24,
     "z_turned0_1": 148, "end_grouped": 148,
+    "factor": 156, "z_codes0": 156,
     "late_grouped": 37, "h7": 40, "late_codes": 44,
 }
 H_BANK = {1: 5, 2: 0, 3: 1, 4: 6, 5: 7, 6: 0, 7: 1}
-BLOCKS = (2, 3, 0, 1)
-LAST_BLOCKS = (2, 3, 1, 0)
 
 
 def tile_picked_gcn_mlp_none_sub_l_kernel(tc, xT, w1, w2, gate, pos1, pos2, pos3, pos4, out):
@@ -64,8 +63,7 @@ def tile_picked_gcn_mlp_none_sub_l_kernel(tc, xT, w1, w2, gate, pos1, pos2, pos3
         banks = [psum.tile([P, BANK], F32, name=f"bank{b}") for b in range(8)]
         sum_banks = [banks[2:4], banks[4:6]]
         word_banks = sum_banks
-        last_banks = banks[2:4]
-        out_places = [word_banks[1][0][:, :V], word_banks[1][1][:, :V], last_banks[1][:, :V], last_banks[1][:, V:]]
+        out_places = [banks[b][:, :V] for b in (0, 1, 6, 7)]
 
         pos = [lists.tile([P, V // 16], U16, name=f"pos{d}") for d in range(D)]
         vcopy, scopy = nc.vector.tensor_copy, nc.scalar.copy
@@ -167,7 +165,7 @@ def tile_picked_gcn_mlp_none_sub_l_kernel(tc, xT, w1, w2, gate, pos1, pos2, pos3
             multiply(i, 0, T, banks[H_BANK[i]])
             copy(out=h[i][:], in_=banks[H_BANK[i]][:])
 
-        factor = keep.tile([P, HALVES], F32, name="factor")
+        factor = new_tile("factor", [P, HALVES], F32)
         ratios = [new_tile(f"ratio{d}", [P, V], F32) for d in range(D - 1)]
 
         def make_ratios():
@@ -306,8 +304,8 @@ def tile_picked_gcn_mlp_none_sub_l_kernel(tc, xT, w1, w2, gate, pos1, pos2, pos3
         project(6, scopy)
         project(7, scopy)
         gather(4)
-        w2_grouped.append(new_tile("w2_grouped1", [P, P, J], BF16))
-        group(vcopy, w2_grouped[1][:], w2_raw[1][:, :, LATE : 2 * P])
+        w2_grouped.append(new_tile("w2_grouped1", [P, 2 * P, J], BF16))
+        group(vcopy, w2_grouped[1][:], w2_raw[1][:, :, P : 3 * P])
         z_grouped[0] = new_tile("z_grouped0", [P, V, J], BF16)
         for s in range(HALVES):
             round_sums(0, J, s)
@@ -321,9 +319,8 @@ def tile_picked_gcn_mlp_none_sub_l_kernel(tc, xT, w1, w2, gate, pos1, pos2, pos3
         pick_and_add(6)
         pick_and_add(7)
         gather(6)
-        end_grouped = new_tile("end_grouped", [P, 2 * P, J], BF16)
-        for a in range(0, 2 * P, P):
-            group(scopy, end_grouped[:, a : a + P, :], w2_raw[1][:, :, 2 * P + a : 3 * P + a])
+        end_grouped = new_tile("end_grouped", [P, P, J], BF16)
+        group(scopy, end_grouped[:], w2_raw[1][:, :, :P])
         for s in range(HALVES):
             round_sums(J, PAIRED, s)
         for s in range(HALVES):
@@ -339,43 +336,40 @@ def tile_picked_gcn_mlp_none_sub_l_kernel(tc, xT, w1, w2, gate, pos1, pos2, pos3
             nc.vector.tensor_tensor(prods[LAST, 2][:, cols], h[LAST][:].indirect(offsets), ratios[2][:, cols], MULT)
             add(LAST, 2, (s,))
 
-        late_codes = new_tile("late_codes", [P, PASSES * N + V], U32)
+        late_codes = new_tile("late_codes", [P, PASSES * N], U32)
         w2_codes = [late_codes[:, g * N : (g + 1) * N] for g in range(PASSES)]
-        z_codes = [late_codes[:, PASSES * N :], keep.tile([P, V], U32, name="z_codes1", align_bytes=64)[:]]
+        z_codes = [new_tile(f"z_codes{g}", [P, V], U32)[:] for g in range(PASSES)]
         z_grouped[1] = new_tile("z_grouped1", [P, V, J], BF16)
 
         def quantize_w2(g, cols, grouped):
             quantize(w2_codes[g][:, cols], w2_scales[g][:, cols], grouped)
 
         late_grouped = new_tile("late_grouped", [P, LATE, J], BF16)
-        quantize(z_codes[0], z_scales[0][:], z_grouped[0][:])
-        quantize_w2(0, slice(2 * P, N), w2_grouped[0][:, 2 * P :, :])
-        group(vcopy, late_grouped[:], w2_raw[1][:, :, :LATE])
-        quantize_w2(1, slice(2 * P, N), end_grouped[:])
-        quantize_w2(0, slice(0, 2 * P), w2_grouped[0][:, : 2 * P, :])
-        quantize_w2(1, slice(LATE, 2 * P), w2_grouped[1][:])
-        quantize_w2(1, slice(0, LATE), late_grouped[:])
+        group(vcopy, late_grouped[:], w2_raw[1][:, :, N - LATE :])
+        quantize_w2(0, slice(0, N), w2_grouped[0][:])
+        quantize_w2(1, slice(0, P), end_grouped[:])
+        quantize_w2(1, slice(P, 3 * P), w2_grouped[1][:])
+        quantize_w2(1, slice(N - LATE, N), late_grouped[:])
         for s in range(HALVES):
             round_pairs(LAST, s)
             turn_back(1, s, 1)
+        quantize(z_codes[0], z_scales[0][:], z_grouped[0][:])
+        for s in range(HALVES):
             interleave(1, s)
             quantize(z_codes[1][:, s * P : (s + 1) * P], z_scales[1][:, s * P : (s + 1) * P], z_grouped[1][:, s * P : (s + 1) * P, :])
         for g in range(PASSES):
-            for a in (BLOCKS, LAST_BLOCKS)[g]:
+            for a in range(N // P):
                 nc.tensor.matmul_mx(
                     out=out_places[a],
                     lhsT=w2_codes[g][:, a * P : (a + 1) * P].bitcast(FP8X4),
                     lhsT_scale=w2_scales[g][:, a * P : (a + 1) * P],
                     rhs=z_codes[g].bitcast(FP8X4),
                     rhs_scale=z_scales[g][:],
-                    start=(g == 0 and a != 3),
-                    stop=(g == PASSES - 1 and a != 2),
+                    start=(g == 0),
+                    stop=(g == PASSES - 1),
                 )
 
-        both = keep.tile([P, 2, V], F32, name="result23")
-        vcopy(out=both[:].rearrange("p a v -> p (a v)"), in_=last_banks[1][:])
-        nc.sync.dma_start(out=out_view[:, 2:, :], in_=both[:])
-        for a in (1, 0):
+        for a in range(N // P):
             result = keep.tile([P, V], F32, name=f"result{a}")
-            scopy(out=result[:], in_=out_places[a])
-            (nc.sync if a else nc.scalar).dma_start(out=out_view[:, a, :], in_=result[:])
+            (scopy if a % 2 else vcopy)(out=result[:], in_=out_places[a])
+            (nc.scalar if a == N // P - 1 else nc.sync).dma_start(out=out_view[:, a, :], in_=result[:])

@@ -26,30 +26,33 @@ HALVES = V // P
 PAIRED = TILES - 2
 PASSES = H // (P * J)
 BANK = 512
+QUAD = 32
+FLOOR = 2.0**-32
+TINY = 2.0**-126
 
 X_CUTS = (0, 256, 384, 512)
 X_VECTOR = (208, 0, 128)
 X_BANK = (0, 1, 4)
 W1_CUTS = (0, 1, 2, 3, 5, 8)
 VECTOR_W1_TILE = 1
-QUAD = 32
-SMALL = 2.0**-32
-TINY = 2.0**-126
-LATE = 128
-Q = 256
-PLACE = {
-    "w1_grouped1": 0, "w1_grouped2": 0,
-    "w1_raw2": 100, "h1": 100,
-    "w1_raw3": 108, "h2": 108, "prod1_1": 116, "prod1_3": 120,
-    "w1_raw5": 124, "h4": 124, "prod2_3": 136, "prod3_3": 140,
-    "x_first": 72, "ratio0": 72, "ratio1": 76, "ratio2": 80,
-    "prod3_0": 8, "w2_grouped0": 8,
-    "prod4_1": 24, "w2_grouped1": 24,
-    "z_turned0_1": 148, "end_grouped": 148,
-    "factor": 156, "z_codes0": 156,
-    "late_grouped": 37, "h7": 40, "late_codes": 44,
-}
+PLAIN = range(3, LAST)
 H_BANK = {1: 5, 2: 0, 3: 1, 4: 6, 5: 7, 6: 0, 7: 1}
+OPENS = ((0, 1), (4, 3), (6, 3), (7, 1))
+CLOSES = ((3, 2), (5, 2), (6, 2), (7, 3))
+W2_PARTS = {"early": (0, 0, 2), "between": (1, 0, 1), "next": (0, 2, 4), "last": (1, 1, 3), "tail": (1, 3, 4)}
+UNIT = 256
+PLACE = {
+    **{"x_first": 72, "ratio0": 72, "ratio1": 76, "ratio2": 80},
+    **{"w1_grouped1": 0, "w1_grouped2": 0},
+    **{"w1_raw2": 100, "h1": 100},
+    **{"w1_raw3": 108, "h2": 108, "term1_3": 116},
+    **{"w1_raw5": 124, "term2_2": 121, "h3": 130, "h4": 138, "w2_early": 146},
+    **{"h5": 114, "h6": 122, "term3_0": 40, "h7": 40},
+    **{"term3_2": 4, "w2_between": 4},
+    **{"z_turned0_1": 24, "w2_next": 17, "w2_last": 25},
+    **{"w2_tail": 37, "w2_codes0": 44},
+    **{"factor": 156, "late_codes": 156},
+}
 
 
 def tile_picked_gcn_mlp_none_sub_l_kernel(tc, xT, w1, w2, gate, pos1, pos2, pos3, pos4, out):
@@ -61,9 +64,8 @@ def tile_picked_gcn_mlp_none_sub_l_kernel(tc, xT, w1, w2, gate, pos1, pos2, pos3
         psum = ctx.enter_context(tc.psum_pool(name="psum", bufs=1))
 
         banks = [psum.tile([P, BANK], F32, name=f"bank{b}") for b in range(8)]
-        sum_banks = [banks[2:4], banks[4:6]]
-        word_banks = sum_banks
-        out_places = [banks[b][:, :V] for b in (0, 1, 6, 7)]
+        pass_banks, pair_banks = [banks[2:4], banks[4:6]], banks[6:8]
+        out_banks = banks[0:2] + pair_banks
 
         pos = [lists.tile([P, V // 16], U16, name=f"pos{d}") for d in range(D)]
         vcopy, scopy = nc.vector.tensor_copy, nc.scalar.copy
@@ -86,7 +88,7 @@ def tile_picked_gcn_mlp_none_sub_l_kernel(tc, xT, w1, w2, gate, pos1, pos2, pos3
 
         def new_tile(name, shape, dtype):
             if name in PLACE:
-                return shared.tile(shape, dtype, name=name, offset=PLACE[name] * Q, align_bytes=64)
+                return shared.tile(shape, dtype, name=name, offset=PLACE[name] * UNIT, align_bytes=64)
             return keep.tile(shape, dtype, name=name, align_bytes=64)
 
         pieces = list(zip(X_CUTS[:-1], X_CUTS[1:]))
@@ -112,8 +114,8 @@ def tile_picked_gcn_mlp_none_sub_l_kernel(tc, xT, w1, w2, gate, pos1, pos2, pos3
         nc.sync.dma_start(pos[0][:], pos1)
         nc.sync.dma_start(pos[1][:], pos2)
         load_w1(2)
-        nc.sync.dma_start(pos[3][:], pos4)
         nc.sync.dma_start(pos[2][:], pos3)
+        nc.sync.dma_start(pos[3][:], pos4)
         load_w1(3)
         load_w1(4)
         nc.sync.dma_start(w2_raw[0][:], w2_view[0])
@@ -126,9 +128,10 @@ def tile_picked_gcn_mlp_none_sub_l_kernel(tc, xT, w1, w2, gate, pos1, pos2, pos3
         x_scales = keep.tile([P, T], U8, name="x_scales", align_bytes=64)
         w2_scales = [keep.tile([P, N], U8, name=f"w2_scales{g}", align_bytes=64) for g in range(PASSES)]
         h = {}
-        prods = {}
+        terms = {}
         z_turned = {}
-        z_grouped = {}
+        z_grouped = [new_tile(f"z_grouped{g}", [P, V, J], BF16) for g in range(PASSES)]
+        w2_grouped = {}
         z_scales = [keep.tile([P, V], U8, name=f"z_scales{g}", align_bytes=64) for g in range(PASSES)]
 
         def group(copy, dst, src):
@@ -149,6 +152,12 @@ def tile_picked_gcn_mlp_none_sub_l_kernel(tc, xT, w1, w2, gate, pos1, pos2, pos3
                 scopy(out=grouped[:].rearrange("k (p e) j -> k p j e", e=2), in_=src[:, i - PAIRED])
             quantize(w1_codes[:, i * P : (i + 1) * P], w1_scales[:, i * P : (i + 1) * P], grouped[:])
 
+        def group_w2(copy, part):
+            g, first, end = W2_PARTS[part]
+            w2_grouped[part] = new_tile(f"w2_{part}", [P, (end - first) * P, J], BF16)
+            for a in range(first, end):
+                group(copy, w2_grouped[part][:, (a - first) * P : (a - first + 1) * P, :], w2_raw[g][:, :, a * P : (a + 1) * P])
+
         def multiply(i, a, b, bank):
             nc.tensor.matmul_mx(
                 out=bank[:, : b - a],
@@ -160,21 +169,23 @@ def tile_picked_gcn_mlp_none_sub_l_kernel(tc, xT, w1, w2, gate, pos1, pos2, pos3
                 stop=True,
             )
 
-        def project(i, copy):
+        def project(i):
             h[i] = new_tile(f"h{i}", [P, T], F32)
             multiply(i, 0, T, banks[H_BANK[i]])
-            copy(out=h[i][:], in_=banks[H_BANK[i]][:])
+            scopy(out=h[i][:], in_=banks[H_BANK[i]][:])
 
         factor = new_tile("factor", [P, HALVES], F32)
         ratios = [new_tile(f"ratio{d}", [P, V], F32) for d in range(D - 1)]
 
+        ratio_places = [pair_banks[1 - d // 2][:, d % 2 * V : (d % 2 + 1) * V] for d in range(D - 1)]
+
         def make_ratios():
-            nc.tensor.transpose(banks[6][:, :P], gate_rows[:], ident[:])
-            g = banks[6][:, :QUAD].rearrange("v (d r s) -> v r s d", d=D, s=HALVES)[:, 0]
+            nc.tensor.transpose(pair_banks[0][:, :P], gate_rows[:], ident[:])
+            g = pair_banks[0][:, :QUAD].rearrange("v (d r s) -> v r s d", d=D, s=HALVES)[:, 0]
             weights = keep.tile([P, 2, D], F32, name="weights")
             bounds = keep.tile([P, HALVES, 2 * D + 1], F32, name="bounds")
             for n, sign in enumerate((1.0, -1.0)):
-                nc.vector.memset(weights[:, n, : D - 1], sign * SMALL)
+                nc.vector.memset(weights[:, n, : D - 1], sign * FLOOR)
                 nc.vector.memset(weights[:, n, D - 1 :], sign)
             nc.vector.memset(bounds[:, :, 2 * D :], TINY)
             nc.vector.tensor_tensor(
@@ -183,56 +194,61 @@ def tile_picked_gcn_mlp_none_sub_l_kernel(tc, xT, w1, w2, gate, pos1, pos2, pos3
                 weights[:].unsqueeze(1).to_broadcast([P, HALVES, 2, D]),
                 MULT,
             )
-            twice_sign = keep.tile([P, HALVES], F32, name="twice_sign")
-            nc.vector.tensor_scalar(twice_sign[:], g[:, :, D - 1], 0.0, 2.0, IS_GE, MULT)
+            sign_plus_one = keep.tile([P, HALVES], F32, name="sign_plus_one")
+            nc.vector.tensor_scalar(sign_plus_one[:], g[:, :, D - 1], 0.0, 2.0, IS_GE, MULT)
             size = keep.tile([P, HALVES], F32, name="size")
             nc.vector.tensor_reduce(size[:], bounds[:], mybir.AxisListType.X, MAX)
             signed = keep.tile([P, HALVES, D - 1], F32, name="signed")
             wide = [P, HALVES, D - 1]
-            nc.vector.scalar_tensor_tensor(signed[:], twice_sign[:].unsqueeze(2).to_broadcast(wide), -1.0, g[:, :, : D - 1], ADD, MULT)
-            inverse = new_tile("inverse", [P, HALVES], F32)
+            nc.vector.scalar_tensor_tensor(signed[:], sign_plus_one[:].unsqueeze(2).to_broadcast(wide), -1.0, g[:, :, : D - 1], ADD, MULT)
+            inverse = keep.tile([P, HALVES], F32, name="inverse")
             nc.vector.reciprocal(inverse[:], size[:])
-            nc.vector.scalar_tensor_tensor(factor[:], twice_sign[:], -1.0, size[:], ADD, MULT)
+            nc.vector.scalar_tensor_tensor(factor[:], sign_plus_one[:], -1.0, size[:], ADD, MULT)
             columns = keep.tile(wide, F32, name="columns")
             nc.vector.tensor_tensor(columns[:], signed[:], inverse[:].unsqueeze(2).to_broadcast(wide), MULT)
             for d in range(D - 1):
-                place = banks[7 - d // 2][:, d % 2 * V : (d % 2 + 1) * V]
                 for s in range(HALVES):
-                    nc.tensor.transpose(place[:, s * P : (s + 1) * P], columns[:, s, d : d + 1].to_broadcast([P, P]), ident[:])
-
-        def copy_ratios():
-            for d in range(D - 1):
-                scopy(out=ratios[d][:], in_=banks[7 - d // 2][:, d % 2 * V : (d % 2 + 1) * V])
+                    nc.tensor.transpose(ratio_places[d][:, s * P : (s + 1) * P], columns[:, s, d : d + 1].to_broadcast([P, P]), ident[:])
 
         def bank_of(i, s):
-            return banks[6 + s] if i == PAIRED else sum_banks[i in (4, 5)][s]
+            return pair_banks[s] if i == PAIRED else pass_banks[J <= i < PAIRED][s]
 
-        def add(i, d, halves=(0, 1)):
+        def add(i, d, halves=range(HALVES)):
             t = i % J
             for s in halves:
                 nc.tensor.matmul(
                     bank_of(i, s)[:, t * P : (t + 1) * P],
-                    lhsT=prods[i, d][:, s * P : (s + 1) * P],
+                    lhsT=terms[i, d][:, s * P : (s + 1) * P],
                     rhs=ident[:],
-                    start=(i, d) in ((0, 0), (4, 0), (6, 3), (7, 3)),
-                    stop=(i, d) in ((3, 3), (5, 3), (6, 2), (7, 2)),
+                    start=(i, d) in OPENS,
+                    stop=(i, d) in CLOSES,
                     is_transpose=True,
                 )
 
-        def fused(i, d):
-            prods[i, d] = new_tile(f"prod{i}_{d}", [P, V], F32)
-            nc.vector.tensor_tensor(prods[i, d][:], h[i][:].indirect(pos[d][:]), ratios[d][:], MULT)
+        def gather(i):
+            for d in range(D - 1):
+                terms[i, d] = new_tile(f"term{i}_{d}", [P, V], F32)
+                nc.vector.tensor_tensor(terms[i, d][:], h[i][:].indirect(pos[d][:]), ratios[d][:], MULT)
+                if d > 0 or i in PLAIN:
+                    add(i, d)
+            if i not in PLAIN:
+                terms[i, D - 1] = new_tile(f"term{i}_{D - 1}", [P, V], F32)
+                for halves in [(s,) for s in range(HALVES)] if i == LAST else [range(HALVES)]:
+                    v0, v1 = halves[0] * P, (halves[-1] + 1) * P
+                    window = h[i][:].indirect(pos[D - 1][:, v0 // 16 : v1 // 16])
+                    nc.vector.tensor_tensor(terms[i, D - 1][:, v0:v1], window, terms[i, 0][:, v0:v1], ADD)
+                    add(i, D - 1, halves)
 
         def pick(i):
-            prods[i, D - 1] = new_tile(f"prod{i}_{D - 1}", [P, V], F32)
-            nc.scalar.activation(prods[i, D - 1][:], h[i][:].indirect(pos[D - 1][:]), COPY)
+            terms[i, D - 1] = new_tile(f"term{i}_{D - 1}", [P, V], F32)
+            nc.scalar.activation(terms[i, D - 1][:], h[i][:].indirect(pos[D - 1][:]), COPY)
 
         def round_sums(i0, i1, s):
             g, t0, t1 = i0 // J, i0 % J, (i1 - 1) % J + 1
             z_turned[g, s] = new_tile(f"z_turned{g}_{s}", [P, 2, P, 2], BF16)
             nc.scalar.activation(
                 z_turned[g, s][:, :, P // J * t0 : P // J * t1, :],
-                sum_banks[g][s][:, t0 * P : t1 * P].rearrange("v (p u e) -> v u p e", u=2, e=2),
+                pass_banks[g][s][:, t0 * P : t1 * P].rearrange("v (p u e) -> v u p e", u=2, e=2),
                 COPY,
                 scale=factor[:, s : s + 1],
             )
@@ -248,12 +264,12 @@ def tile_picked_gcn_mlp_none_sub_l_kernel(tc, xT, w1, w2, gate, pos1, pos2, pos3
 
         def turn_back(g, s, u):
             words = z_turned[g, s][:, u, :, :].rearrange("v p e -> v (p e)").bitcast(F32)
-            nc.tensor.transpose(word_banks[g][s][:, u * P : (u + 1) * P], words, ident[:])
+            nc.tensor.transpose(pass_banks[g][s][:, u * P : (u + 1) * P], words, ident[:])
 
         def interleave(g, s):
             scopy(
                 out=z_grouped[g][:, s * P : (s + 1) * P, :].rearrange("p v j -> p (v j)").bitcast(F32).rearrange("p (v u) -> p v u", u=2),
-                in_=word_banks[g][s][:, : 2 * P].rearrange("p (u v) -> p v u", u=2),
+                in_=pass_banks[g][s][:, : 2 * P].rearrange("p (u v) -> p v u", u=2),
             )
 
         make_ratios()
@@ -265,7 +281,8 @@ def tile_picked_gcn_mlp_none_sub_l_kernel(tc, xT, w1, w2, gate, pos1, pos2, pos3
             if cut < b - a:
                 group(scopy, x_grouped[c][:, cut:, :], x_raw[c][:, :, cut:])
             quantize(x_codes[:, a:b], x_scales[:, a:b], x_grouped[c][:])
-        copy_ratios()
+        for d in range(D - 1):
+            scopy(out=ratios[d][:], in_=ratio_places[d])
         h[0] = new_tile("h0", [P, T], F32)
         for c, (a, b) in enumerate(pieces):
             multiply(0, a, b, banks[X_BANK[c]])
@@ -273,94 +290,76 @@ def tile_picked_gcn_mlp_none_sub_l_kernel(tc, xT, w1, w2, gate, pos1, pos2, pos3
 
         prepare_w1(1)
         prepare_w1(2)
-        def gather(i):
-            for d in range(D - 1):
-                fused(i, d)
-                add(i, d)
-
-        def pick_and_add(i):
-            pick(i)
-            add(i, D - 1)
-
-        project(1, scopy)
+        project(1)
         gather(0)
-        pick_and_add(0)
         prepare_w1(3)
         prepare_w1(4)
-        project(2, scopy)
+        project(2)
         gather(1)
-        pick_and_add(1)
-        project(3, scopy)
-        for k in range(5, TILES):
-            prepare_w1(k)
+        for i in range(5, TILES):
+            prepare_w1(i)
+        project(3)
+        project(4)
+        group_w2(scopy, "early")
         gather(2)
-        project(4, scopy)
+        pick(3)
+        pick(4)
+        project(5)
+        project(6)
+        add(3, D - 1)
         gather(3)
-        w2_grouped = [new_tile("w2_grouped0", [P, N, J], BF16)]
-        group(vcopy, w2_grouped[0][:], w2_raw[0][:])
-        project(5, scopy)
-        pick_and_add(2)
-        pick_and_add(3)
-        project(6, scopy)
-        project(7, scopy)
-        gather(4)
-        w2_grouped.append(new_tile("w2_grouped1", [P, 2 * P, J], BF16))
-        group(vcopy, w2_grouped[1][:], w2_raw[1][:, :, P : 3 * P])
-        z_grouped[0] = new_tile("z_grouped0", [P, V, J], BF16)
+        pick(5)
+        pick(6)
+        project(7)
         for s in range(HALVES):
             round_sums(0, J, s)
-        gather(5)
-        pick_and_add(4)
-        pick_and_add(5)
+        group_w2(scopy, "between")
+
+        add(4, D - 1)
+        gather(4)
         for s in range(HALVES):
             turn_back(0, s, 0)
             turn_back(0, s, 1)
             interleave(0, s)
-        pick_and_add(6)
-        pick_and_add(7)
-        gather(6)
-        end_grouped = new_tile("end_grouped", [P, P, J], BF16)
-        group(scopy, end_grouped[:], w2_raw[1][:, :, :P])
+        add(5, D - 1)
+        gather(5)
+        group_w2(scopy, "next")
+        group_w2(scopy, "last")
+        add(PAIRED, D - 1)
+        gather(PAIRED)
         for s in range(HALVES):
             round_sums(J, PAIRED, s)
         for s in range(HALVES):
             round_pairs(PAIRED, s)
             turn_back(1, s, 0)
-        for d in range(2):
-            fused(LAST, d)
-            add(LAST, d)
-        prods[LAST, 2] = new_tile(f"prod{LAST}_2", [P, V], F32)
-        for s in range(HALVES):
-            cols = slice(s * P, (s + 1) * P)
-            offsets = pos[2][:, s * P // 16 : (s + 1) * P // 16]
-            nc.vector.tensor_tensor(prods[LAST, 2][:, cols], h[LAST][:].indirect(offsets), ratios[2][:, cols], MULT)
-            add(LAST, 2, (s,))
+        gather(LAST)
 
-        late_codes = new_tile("late_codes", [P, PASSES * N], U32)
-        w2_codes = [late_codes[:, g * N : (g + 1) * N] for g in range(PASSES)]
-        z_codes = [new_tile(f"z_codes{g}", [P, V], U32)[:] for g in range(PASSES)]
-        z_grouped[1] = new_tile("z_grouped1", [P, V, J], BF16)
+        late_codes = new_tile("late_codes", [P, V + N], U32)
+        w2_codes = [new_tile("w2_codes0", [P, N], U32)[:], late_codes[:, V:]]
+        z_codes = [late_codes[:, :V], new_tile("z_codes1", [P, V], U32)[:]]
 
-        def quantize_w2(g, cols, grouped):
-            quantize(w2_codes[g][:, cols], w2_scales[g][:, cols], grouped)
+        def quantize_w2(part):
+            g, first, end = W2_PARTS[part]
+            cols = slice(first * P, end * P)
+            quantize(w2_codes[g][:, cols], w2_scales[g][:, cols], w2_grouped[part][:])
 
-        late_grouped = new_tile("late_grouped", [P, LATE, J], BF16)
-        group(vcopy, late_grouped[:], w2_raw[1][:, :, N - LATE :])
-        quantize_w2(0, slice(0, N), w2_grouped[0][:])
-        quantize_w2(1, slice(0, P), end_grouped[:])
-        quantize_w2(1, slice(P, 3 * P), w2_grouped[1][:])
-        quantize_w2(1, slice(N - LATE, N), late_grouped[:])
+        group_w2(vcopy, "tail")
+        quantize_w2("early")
+        quantize_w2("next")
         for s in range(HALVES):
             round_pairs(LAST, s)
             turn_back(1, s, 1)
         quantize(z_codes[0], z_scales[0][:], z_grouped[0][:])
+        quantize_w2("between")
+        quantize_w2("last")
+        quantize_w2("tail")
         for s in range(HALVES):
             interleave(1, s)
             quantize(z_codes[1][:, s * P : (s + 1) * P], z_scales[1][:, s * P : (s + 1) * P], z_grouped[1][:, s * P : (s + 1) * P, :])
         for g in range(PASSES):
             for a in range(N // P):
                 nc.tensor.matmul_mx(
-                    out=out_places[a],
+                    out=out_banks[a][:, :V],
                     lhsT=w2_codes[g][:, a * P : (a + 1) * P].bitcast(FP8X4),
                     lhsT_scale=w2_scales[g][:, a * P : (a + 1) * P],
                     rhs=z_codes[g].bitcast(FP8X4),
@@ -371,5 +370,5 @@ def tile_picked_gcn_mlp_none_sub_l_kernel(tc, xT, w1, w2, gate, pos1, pos2, pos3
 
         for a in range(N // P):
             result = keep.tile([P, V], F32, name=f"result{a}")
-            (scopy if a % 2 else vcopy)(out=result[:], in_=out_places[a])
+            (scopy if a % 2 else vcopy)(out=result[:], in_=out_banks[a][:, :V])
             (nc.scalar if a == N // P - 1 else nc.sync).dma_start(out=out_view[:, a, :], in_=result[:])

@@ -35,22 +35,26 @@ X_VECTOR = (208, 0, 128)
 X_BANK = (0, 1, 4)
 W1_CUTS = (0, 1, 2, 3, 5, 8)
 VECTOR_W1_TILE = 1
-PLAIN = range(3, LAST)
+PLAIN = range(2, TILES)
 H_BANK = {1: 5, 2: 0, 3: 1, 4: 6, 5: 7, 6: 0, 7: 1}
-OPENS = ((0, 1), (4, 3), (6, 3), (7, 1))
-CLOSES = ((3, 2), (5, 2), (6, 2), (7, 3))
-W2_PARTS = {"early": (0, 0, 2), "between": (1, 0, 1), "next": (0, 2, 4), "last": (1, 1, 3), "tail": (1, 3, 4)}
+OPENS = ((0, 1), (4, 3), (6, 3), (7, 3))
+CLOSES = ((3, 2), (5, 2), (6, 2), (7, 2))
+W2_PARTS = {"early": (0, 0, 2), "middle": (1, 0, 1), "next": (0, 2, 4), "tail": (1, 2, 3), "gap": (1, 1, 2), "end": (1, 3, 4)}
 UNIT = 256
 PLACE = {
     **{"x_first": 72, "ratio0": 72, "ratio1": 76, "ratio2": 80},
     **{"w1_grouped1": 0, "w1_grouped2": 0},
-    **{"w1_raw2": 100, "h1": 100},
+    **{"w1_raw2": 96, "h1": 97, "term0_1": 93},
     **{"w1_raw3": 108, "h2": 108, "term1_3": 116},
-    **{"w1_raw5": 124, "term2_2": 121, "h3": 130, "h4": 138, "w2_early": 146},
+    **{"w1_raw5": 124, "term2_2": 121, "h3": 130, "h4": 138},
+    **{"w2_early": 146, "term2_3": 126},
     **{"h5": 114, "h6": 122, "term3_0": 40, "h7": 40},
-    **{"term3_2": 4, "w2_between": 4},
-    **{"z_turned0_1": 24, "w2_next": 17, "w2_last": 25},
+    **{"term3_2": 4, "term7_3": 4},
+    **{"z_turned0_1": 24, "w2_next": 17},
+    **{"term5_0": 8, "w2_middle": 8},
     **{"w2_tail": 37, "w2_codes0": 44},
+    **{"term7_2": 25, "w2_gap": 25},
+    **{"z_turned1_1": 30, "w2_end": 30},
     **{"factor": 156, "late_codes": 156},
 }
 
@@ -140,17 +144,19 @@ def tile_picked_gcn_mlp_none_sub_l_kernel(tc, xT, w1, w2, gate, pos1, pos2, pos3
         def quantize(codes, scales, grouped):
             nc.vector.quantize_mx(out=codes.bitcast(FP8X4), scales=scales, in_=grouped.rearrange("p n j -> p (n j)"))
 
-        def prepare_w1(i):
-            q = max(q for q, (a, b) in enumerate(lots) if a <= i)
-            grouped = new_tile(f"w1_grouped{i}", [P, P, J], BF16)
-            if i < PAIRED:
-                c = (i - lots[q][0]) * P
-                group(vcopy if i == VECTOR_W1_TILE else scopy, grouped[:], w1_raw[q][:, :, c : c + P])
-            else:
-                c = (PAIRED - lots[q][0]) * P
-                src = w1_raw[q][:, :, c:].rearrange("k j (p u e) -> k u p j e", u=2, e=2)
-                scopy(out=grouped[:].rearrange("k (p e) j -> k p j e", e=2), in_=src[:, i - PAIRED])
-            quantize(w1_codes[:, i * P : (i + 1) * P], w1_scales[:, i * P : (i + 1) * P], grouped[:])
+        def prepare_w1(first, end):
+            q = max(q for q, (a, b) in enumerate(lots) if a <= first)
+            grouped = new_tile(f"w1_grouped{first}", [P, (end - first) * P, J], BF16)
+            for i in range(first, end):
+                dst = grouped[:, (i - first) * P : (i - first + 1) * P, :]
+                if i < PAIRED:
+                    c = (i - lots[q][0]) * P
+                    group(vcopy if i == VECTOR_W1_TILE else scopy, dst, w1_raw[q][:, :, c : c + P])
+                else:
+                    c = (PAIRED - lots[q][0]) * P
+                    src = w1_raw[q][:, :, c:].rearrange("k j (p u e) -> k u p j e", u=2, e=2)
+                    scopy(out=dst.rearrange("k (p e) j -> k p j e", e=2), in_=src[:, i - PAIRED])
+            quantize(w1_codes[:, first * P : end * P], w1_scales[:, first * P : end * P], grouped[:])
 
         def group_w2(copy, part):
             g, first, end = W2_PARTS[part]
@@ -228,16 +234,16 @@ def tile_picked_gcn_mlp_none_sub_l_kernel(tc, xT, w1, w2, gate, pos1, pos2, pos3
         def gather(i):
             for d in range(D - 1):
                 terms[i, d] = new_tile(f"term{i}_{d}", [P, V], F32)
-                nc.vector.tensor_tensor(terms[i, d][:], h[i][:].indirect(pos[d][:]), ratios[d][:], MULT)
-                if d > 0 or i in PLAIN:
-                    add(i, d)
+                for halves in [(s,) for s in range(HALVES)] if (i, d) == (LAST, D - 2) else [range(HALVES)]:
+                    v0, v1 = halves[0] * P, (halves[-1] + 1) * P
+                    window = h[i][:].indirect(pos[d][:, v0 // 16 : v1 // 16])
+                    nc.vector.tensor_tensor(terms[i, d][:, v0:v1], window, ratios[d][:, v0:v1], MULT)
+                    if d > 0 or i in PLAIN:
+                        add(i, d, halves)
             if i not in PLAIN:
                 terms[i, D - 1] = new_tile(f"term{i}_{D - 1}", [P, V], F32)
-                for halves in [(s,) for s in range(HALVES)] if i == LAST else [range(HALVES)]:
-                    v0, v1 = halves[0] * P, (halves[-1] + 1) * P
-                    window = h[i][:].indirect(pos[D - 1][:, v0 // 16 : v1 // 16])
-                    nc.vector.tensor_tensor(terms[i, D - 1][:, v0:v1], window, terms[i, 0][:, v0:v1], ADD)
-                    add(i, D - 1, halves)
+                nc.vector.tensor_tensor(terms[i, D - 1][:], h[i][:].indirect(pos[D - 1][:]), terms[i, 0][:], ADD)
+                add(i, D - 1)
 
         def pick(i):
             terms[i, D - 1] = new_tile(f"term{i}_{D - 1}", [P, V], F32)
@@ -273,7 +279,7 @@ def tile_picked_gcn_mlp_none_sub_l_kernel(tc, xT, w1, w2, gate, pos1, pos2, pos3
             )
 
         make_ratios()
-        prepare_w1(0)
+        prepare_w1(0, 1)
         for c, (a, b) in enumerate(pieces):
             cut = X_VECTOR[c]
             if cut > 0:
@@ -288,20 +294,20 @@ def tile_picked_gcn_mlp_none_sub_l_kernel(tc, xT, w1, w2, gate, pos1, pos2, pos3
             multiply(0, a, b, banks[X_BANK[c]])
             (vcopy if b == T else scopy)(out=h[0][:, a:b], in_=banks[X_BANK[c]][:, : b - a])
 
-        prepare_w1(1)
-        prepare_w1(2)
+        prepare_w1(1, 2)
+        prepare_w1(2, 3)
         project(1)
         gather(0)
-        prepare_w1(3)
-        prepare_w1(4)
+        prepare_w1(3, 5)
         project(2)
         gather(1)
-        for i in range(5, TILES):
-            prepare_w1(i)
+        prepare_w1(5, TILES)
         project(3)
         project(4)
         group_w2(scopy, "early")
         gather(2)
+        pick(2)
+        add(2, D - 1)
         pick(3)
         pick(4)
         project(5)
@@ -313,7 +319,7 @@ def tile_picked_gcn_mlp_none_sub_l_kernel(tc, xT, w1, w2, gate, pos1, pos2, pos3
         project(7)
         for s in range(HALVES):
             round_sums(0, J, s)
-        group_w2(scopy, "between")
+        pick(LAST)
 
         add(4, D - 1)
         gather(4)
@@ -323,8 +329,8 @@ def tile_picked_gcn_mlp_none_sub_l_kernel(tc, xT, w1, w2, gate, pos1, pos2, pos3
             interleave(0, s)
         add(5, D - 1)
         gather(5)
+        group_w2(vcopy, "middle")
         group_w2(scopy, "next")
-        group_w2(scopy, "last")
         add(PAIRED, D - 1)
         gather(PAIRED)
         for s in range(HALVES):
@@ -332,6 +338,7 @@ def tile_picked_gcn_mlp_none_sub_l_kernel(tc, xT, w1, w2, gate, pos1, pos2, pos3
         for s in range(HALVES):
             round_pairs(PAIRED, s)
             turn_back(1, s, 0)
+        add(LAST, D - 1)
         gather(LAST)
 
         late_codes = new_tile("late_codes", [P, V + N], U32)
@@ -349,13 +356,16 @@ def tile_picked_gcn_mlp_none_sub_l_kernel(tc, xT, w1, w2, gate, pos1, pos2, pos3
         for s in range(HALVES):
             round_pairs(LAST, s)
             turn_back(1, s, 1)
+        group_w2(scopy, "gap")
         quantize(z_codes[0], z_scales[0][:], z_grouped[0][:])
-        quantize_w2("between")
-        quantize_w2("last")
+        quantize_w2("middle")
         quantize_w2("tail")
+        quantize_w2("gap")
         for s in range(HALVES):
             interleave(1, s)
             quantize(z_codes[1][:, s * P : (s + 1) * P], z_scales[1][:, s * P : (s + 1) * P], z_grouped[1][:, s * P : (s + 1) * P, :])
+        group_w2(scopy, "end")
+        quantize_w2("end")
         for g in range(PASSES):
             for a in range(N // P):
                 nc.tensor.matmul_mx(

@@ -25,37 +25,25 @@ LAST = TILES - 1
 HALVES = V // P
 PAIRED = TILES - 2
 PASSES = H // (P * J)
+BLOCKS = N // P
 BANK = 512
 QUAD = 32
 FLOOR = 2.0**-32
 TINY = 2.0**-126
+PLAIN = D - 1
 
 X_CUTS = (0, 256, 384, 512)
 X_VECTOR = (208, 0, 128)
 X_BANK = (0, 1, 4)
-W1_CUTS = (0, 1, 2, 3, 5, 8)
-VECTOR_W1_TILE = 1
-PLAIN = range(2, TILES)
+W1_CUTS = (0, 1, 2, 3, 5, 6, 8)
 H_BANK = {1: 5, 2: 0, 3: 1, 4: 6, 5: 7, 6: 0, 7: 1}
-OPENS = ((0, 1), (4, 3), (6, 3), (7, 3))
-CLOSES = ((3, 2), (5, 2), (6, 2), (7, 2))
-W2_PARTS = {"early": (0, 0, 2), "middle": (1, 0, 1), "next": (0, 2, 4), "tail": (1, 2, 3), "gap": (1, 1, 2), "end": (1, 3, 4)}
 UNIT = 256
 PLACE = {
-    **{"x_first": 72, "ratio0": 72, "ratio1": 76, "ratio2": 80},
-    **{"w1_grouped1": 0, "w1_grouped2": 0},
-    **{"w1_raw2": 96, "h1": 97, "term0_1": 93},
-    **{"w1_raw3": 108, "h2": 108, "term1_3": 116},
-    **{"w1_raw5": 124, "term2_2": 121, "h3": 130, "h4": 138},
-    **{"w2_early": 146, "term2_3": 126},
-    **{"h5": 114, "h6": 122, "term3_0": 40, "h7": 40},
-    **{"term3_2": 4, "term7_3": 4},
-    **{"z_turned0_1": 24, "w2_next": 17},
-    **{"term5_0": 8, "w2_middle": 8},
-    **{"w2_tail": 37, "w2_codes0": 44},
-    **{"term7_2": 25, "w2_gap": 25},
-    **{"z_turned1_1": 30, "w2_end": 30},
-    **{"factor": 156, "late_codes": 156},
+    **{"x_first": 60, "ratio0": 72, "ratio1": 76, "ratio2": 80},
+    **{"x_grouped384": 0, "w1_grouped2": 0},
+    **{"w1_raw2": 90, "h1": 90, "w1_raw3": 100, "h2": 100, "term1_3": 108, "w1_raw5": 116, "h3": 116, "w1_raw6": 132, "h4": 146, "z_turned0_0": 132, "z_turned0_1": 136, "h6": 126, "h7": 138, "w2_early": 116},
+    **{"w2_late": 64, "z_turned1_0": 30, "w2_last": 30},
+    **{"rest_codes": 76},
 }
 
 
@@ -69,7 +57,7 @@ def tile_picked_gcn_mlp_none_sub_l_kernel(tc, xT, w1, w2, gate, pos1, pos2, pos3
 
         banks = [psum.tile([P, BANK], F32, name=f"bank{b}") for b in range(8)]
         pass_banks, pair_banks = [banks[2:4], banks[4:6]], banks[6:8]
-        out_banks = banks[0:2] + pair_banks
+        out_banks = [banks[0], banks[1], banks[3], banks[4]]
 
         pos = [lists.tile([P, V // 16], U16, name=f"pos{d}") for d in range(D)]
         vcopy, scopy = nc.vector.tensor_copy, nc.scalar.copy
@@ -122,6 +110,7 @@ def tile_picked_gcn_mlp_none_sub_l_kernel(tc, xT, w1, w2, gate, pos1, pos2, pos3
         nc.sync.dma_start(pos[3][:], pos4)
         load_w1(3)
         load_w1(4)
+        load_w1(5)
         nc.sync.dma_start(w2_raw[0][:], w2_view[0])
         nc.sync.dma_start(w2_raw[1][:], w2_view[1])
 
@@ -130,13 +119,15 @@ def tile_picked_gcn_mlp_none_sub_l_kernel(tc, xT, w1, w2, gate, pos1, pos2, pos3
         x_grouped = [new_tile(f"x_grouped{a}", [P, b - a, J], BF16) for a, b in pieces]
         x_codes = keep.tile([P, T], U32, name="x_codes", align_bytes=64)
         x_scales = keep.tile([P, T], U8, name="x_scales", align_bytes=64)
+        w2_codes = [keep.tile([P, N], U32, name=f"w2_codes{g}", align_bytes=64) for g in range(PASSES)]
         w2_scales = [keep.tile([P, N], U8, name=f"w2_scales{g}", align_bytes=64) for g in range(PASSES)]
+        z_codes = [keep.tile([P, V], U32, name=f"z_codes{g}", align_bytes=64) for g in range(PASSES)]
+        z_scales = [keep.tile([P, V], U8, name=f"z_scales{g}", align_bytes=64) for g in range(PASSES)]
+        z_grouped = [new_tile(f"z_grouped{g}", [P, V, J], BF16) for g in range(PASSES)]
         h = {}
         terms = {}
         z_turned = {}
-        z_grouped = [new_tile(f"z_grouped{g}", [P, V, J], BF16) for g in range(PASSES)]
-        w2_grouped = {}
-        z_scales = [keep.tile([P, V], U8, name=f"z_scales{g}", align_bytes=64) for g in range(PASSES)]
+        w1_grouped = {}
 
         def group(copy, dst, src):
             copy(out=dst.rearrange("p (c i) j -> p c j i", i=2), in_=src.rearrange("p j (c i) -> p c j i", i=2))
@@ -144,25 +135,23 @@ def tile_picked_gcn_mlp_none_sub_l_kernel(tc, xT, w1, w2, gate, pos1, pos2, pos3
         def quantize(codes, scales, grouped):
             nc.vector.quantize_mx(out=codes.bitcast(FP8X4), scales=scales, in_=grouped.rearrange("p n j -> p (n j)"))
 
-        def prepare_w1(first, end):
-            q = max(q for q, (a, b) in enumerate(lots) if a <= first)
-            grouped = new_tile(f"w1_grouped{first}", [P, (end - first) * P, J], BF16)
-            for i in range(first, end):
-                dst = grouped[:, (i - first) * P : (i - first + 1) * P, :]
-                if i < PAIRED:
-                    c = (i - lots[q][0]) * P
-                    group(vcopy if i == VECTOR_W1_TILE else scopy, dst, w1_raw[q][:, :, c : c + P])
-                else:
-                    c = (PAIRED - lots[q][0]) * P
-                    src = w1_raw[q][:, :, c:].rearrange("k j (p u e) -> k u p j e", u=2, e=2)
-                    scopy(out=dst.rearrange("k (p e) j -> k p j e", e=2), in_=src[:, i - PAIRED])
-            quantize(w1_codes[:, first * P : end * P], w1_scales[:, first * P : end * P], grouped[:])
+        def prepare_w1(i, copy):
+            q = max(q for q, (a, b) in enumerate(lots) if a <= i)
+            dst = new_tile(f"w1_grouped{i}", [P, P, J], BF16)
+            if i < PAIRED:
+                c = (i - lots[q][0]) * P
+                group(copy, dst[:], w1_raw[q][:, :, c : c + P])
+            else:
+                c = (PAIRED - lots[q][0]) * P
+                src = w1_raw[q][:, :, c:].rearrange("k j (p u e) -> k u p j e", u=2, e=2)
+                copy(out=dst[:].rearrange("k (p e) j -> k p j e", e=2), in_=src[:, i - PAIRED])
+            quantize(w1_codes[:, i * P : (i + 1) * P], w1_scales[:, i * P : (i + 1) * P], dst[:])
 
-        def group_w2(copy, part):
-            g, first, end = W2_PARTS[part]
-            w2_grouped[part] = new_tile(f"w2_{part}", [P, (end - first) * P, J], BF16)
-            for a in range(first, end):
-                group(copy, w2_grouped[part][:, (a - first) * P : (a - first + 1) * P, :], w2_raw[g][:, :, a * P : (a + 1) * P])
+        def group_w2(copy, dst, g, a):
+            group(copy, dst, w2_raw[g][:, :, a * P : (a + 1) * P])
+
+        def quantize_w2(grouped, g, first, end):
+            quantize(w2_codes[g][:, first * P : end * P], w2_scales[g][:, first * P : end * P], grouped)
 
         def multiply(i, a, b, bank):
             nc.tensor.matmul_mx(
@@ -192,7 +181,8 @@ def tile_picked_gcn_mlp_none_sub_l_kernel(tc, xT, w1, w2, gate, pos1, pos2, pos3
             bounds = keep.tile([P, HALVES, 2 * D + 1], F32, name="bounds")
             for n, sign in enumerate((1.0, -1.0)):
                 nc.vector.memset(weights[:, n, : D - 1], sign * FLOOR)
-                nc.vector.memset(weights[:, n, D - 1 :], sign)
+            scopy(out=weights[:, 0, D - 1 :], in_=ones[:, :1])
+            nc.vector.memset(weights[:, 1, D - 1 :], -1.0)
             nc.vector.memset(bounds[:, :, 2 * D :], TINY)
             nc.vector.tensor_tensor(
                 bounds[:, :, : 2 * D].rearrange("v s (n d) -> v s n d", n=2),
@@ -217,44 +207,42 @@ def tile_picked_gcn_mlp_none_sub_l_kernel(tc, xT, w1, w2, gate, pos1, pos2, pos3
                     nc.tensor.transpose(ratio_places[d][:, s * P : (s + 1) * P], columns[:, s, d : d + 1].to_broadcast([P, P]), ident[:])
 
         def bank_of(i, s):
-            return pair_banks[s] if i == PAIRED else pass_banks[J <= i < PAIRED][s]
+            return pair_banks[s] if i == PAIRED else pass_banks[i == J][s]
 
-        def add(i, d, halves=range(HALVES)):
+        def add(i, d, halves=range(HALVES), start=False, stop=False):
             t = i % J
             for s in halves:
                 nc.tensor.matmul(
                     bank_of(i, s)[:, t * P : (t + 1) * P],
                     lhsT=terms[i, d][:, s * P : (s + 1) * P],
                     rhs=ident[:],
-                    start=(i, d) in OPENS,
-                    stop=(i, d) in CLOSES,
+                    start=start,
+                    stop=stop,
                     is_transpose=True,
                 )
 
-        def gather(i):
-            for d in range(D - 1):
+        def gather(i, d, halves=range(HALVES)):
+            if (i, d) not in terms:
                 terms[i, d] = new_tile(f"term{i}_{d}", [P, V], F32)
-                for halves in [(s,) for s in range(HALVES)] if (i, d) == (LAST, D - 2) else [range(HALVES)]:
-                    v0, v1 = halves[0] * P, (halves[-1] + 1) * P
-                    window = h[i][:].indirect(pos[d][:, v0 // 16 : v1 // 16])
-                    nc.vector.tensor_tensor(terms[i, d][:, v0:v1], window, ratios[d][:, v0:v1], MULT)
-                    if d > 0 or i in PLAIN:
-                        add(i, d, halves)
-            if i not in PLAIN:
-                terms[i, D - 1] = new_tile(f"term{i}_{D - 1}", [P, V], F32)
-                nc.vector.tensor_tensor(terms[i, D - 1][:], h[i][:].indirect(pos[D - 1][:]), terms[i, 0][:], ADD)
-                add(i, D - 1)
+            v0, v1 = halves[0] * P, (halves[-1] + 1) * P
+            nc.vector.tensor_tensor(terms[i, d][:, v0:v1], h[i][:].indirect(pos[d][:, v0 // 16 : v1 // 16]), ratios[d][:, v0:v1], MULT)
 
         def pick(i):
-            terms[i, D - 1] = new_tile(f"term{i}_{D - 1}", [P, V], F32)
-            nc.scalar.activation(terms[i, D - 1][:], h[i][:].indirect(pos[D - 1][:]), COPY)
+            terms[i, PLAIN] = new_tile(f"term{i}_{PLAIN}", [P, V], F32)
+            nc.scalar.activation(terms[i, PLAIN][:], h[i][:].indirect(pos[PLAIN][:]), COPY)
+
+        def fetch(i, opens=False):
+            for d in range(PLAIN):
+                gather(i, d)
+                add(i, d, start=opens and d == 0)
 
         def round_sums(i0, i1, s):
             g, t0, t1 = i0 // J, i0 % J, (i1 - 1) % J + 1
-            z_turned[g, s] = new_tile(f"z_turned{g}_{s}", [P, 2, P, 2], BF16)
+            if t0 == 0:
+                z_turned[g, s] = new_tile(f"z_turned{g}_{s}", [P, 2, P, 2], BF16)
             nc.scalar.activation(
                 z_turned[g, s][:, :, P // J * t0 : P // J * t1, :],
-                pass_banks[g][s][:, t0 * P : t1 * P].rearrange("v (p u e) -> v u p e", u=2, e=2),
+                bank_of(i0, s)[:, t0 * P : t1 * P].rearrange("v (p u e) -> v u p e", u=2, e=2),
                 COPY,
                 scale=factor[:, s : s + 1],
             )
@@ -278,8 +266,19 @@ def tile_picked_gcn_mlp_none_sub_l_kernel(tc, xT, w1, w2, gate, pos1, pos2, pos3
                 in_=pass_banks[g][s][:, : 2 * P].rearrange("p (u v) -> p v u", u=2),
             )
 
+        def second_layer(g, a, v0=0, v1=V):
+            nc.tensor.matmul_mx(
+                out=out_banks[a][:, v0:v1],
+                lhsT=(rest_codes[:, (a - 2) * P : (a - 1) * P] if (g, a) == (1, 2) else w2_codes[g][:, a * P : (a + 1) * P]).bitcast(FP8X4),
+                lhsT_scale=w2_scales[g][:, a * P : (a + 1) * P],
+                rhs=z_codes[g][:, v0:v1].bitcast(FP8X4),
+                rhs_scale=z_scales[g][:, v0:v1],
+                start=(g == 0),
+                stop=(g == PASSES - 1 and v1 == V),
+            )
+
         make_ratios()
-        prepare_w1(0, 1)
+        prepare_w1(0, scopy)
         for c, (a, b) in enumerate(pieces):
             cut = X_VECTOR[c]
             if cut > 0:
@@ -287,98 +286,106 @@ def tile_picked_gcn_mlp_none_sub_l_kernel(tc, xT, w1, w2, gate, pos1, pos2, pos3
             if cut < b - a:
                 group(scopy, x_grouped[c][:, cut:, :], x_raw[c][:, :, cut:])
             quantize(x_codes[:, a:b], x_scales[:, a:b], x_grouped[c][:])
-        for d in range(D - 1):
+        for d in range(PLAIN):
             scopy(out=ratios[d][:], in_=ratio_places[d])
         h[0] = new_tile("h0", [P, T], F32)
         for c, (a, b) in enumerate(pieces):
             multiply(0, a, b, banks[X_BANK[c]])
             (vcopy if b == T else scopy)(out=h[0][:, a:b], in_=banks[X_BANK[c]][:, : b - a])
 
-        prepare_w1(1, 2)
-        prepare_w1(2, 3)
+        prepare_w1(1, vcopy)
+        prepare_w1(2, scopy)
+        pick(0)
         project(1)
-        gather(0)
-        prepare_w1(3, 5)
+        prepare_w1(3, scopy)
+        fetch(0, opens=True)
+        add(0, PLAIN)
+        prepare_w1(4, scopy)
         project(2)
-        gather(1)
-        prepare_w1(5, TILES)
-        project(3)
-        project(4)
-        group_w2(scopy, "early")
-        gather(2)
-        pick(2)
-        add(2, D - 1)
-        pick(3)
-        pick(4)
-        project(5)
-        project(6)
-        add(3, D - 1)
-        gather(3)
-        pick(5)
-        pick(6)
-        project(7)
+        fetch(1)
+        for i in range(2, J + 1):
+            for tile in {2: (5,), 3: (6, 7), 4: ()}[i]:
+                prepare_w1(tile, scopy)
+            pick(i - 1)
+            add(i - 1, PLAIN, stop=i == J)
+            project(i + 1)
+            fetch(i, opens=i == J)
+        early = new_tile("w2_early", [P, 2 * P, J], BF16)
+        for a in range(2):
+            group_w2(vcopy, early[:, a * P : (a + 1) * P, :], 0, a)
+        quantize_w2(early[:], 0, 0, 2)
+        rest = new_tile("w2_rest", [P, P, J], BF16)
+        rest_codes = new_tile("rest_codes", [P, P], U32)
+        pick(J)
+        add(J, PLAIN, stop=True)
         for s in range(HALVES):
             round_sums(0, J, s)
-        pick(LAST)
-
-        add(4, D - 1)
-        gather(4)
-        for s in range(HALVES):
             turn_back(0, s, 0)
             turn_back(0, s, 1)
-            interleave(0, s)
-        add(5, D - 1)
-        gather(5)
-        group_w2(vcopy, "middle")
-        group_w2(scopy, "next")
-        add(PAIRED, D - 1)
-        gather(PAIRED)
-        for s in range(HALVES):
-            round_sums(J, PAIRED, s)
+        pick(5)
+        interleave(0, 0)
+        project(6)
+        interleave(0, 1)
+        group_w2(scopy, rest[:], 1, 2)
+        add(5, PLAIN, start=True)
+        for d in range(PLAIN):
+            gather(5, d)
+            add(5, d, stop=d == PLAIN - 1)
+        quantize(z_codes[0][:], z_scales[0][:], z_grouped[0][:])
+        project(LAST)
+        pick(PAIRED)
+        pick(LAST)
+        second_layer(0, 0)
+        second_layer(0, 1)
+        for d in range(PLAIN):
+            gather(PAIRED, d)
+            add(PAIRED, d, start=d == 0)
+        add(PAIRED, PLAIN, stop=True)
+        for i in (J, J + 1):
+            for s in range(HALVES):
+                round_sums(i, i + 1, s)
         for s in range(HALVES):
             round_pairs(PAIRED, s)
+        gather(LAST, 0)
+        add(LAST, 0, start=True)
+        add(LAST, PLAIN)
+        for s in range(HALVES):
+            for d in (1, 2):
+                gather(LAST, d, (s,))
+                add(LAST, d, (s,), stop=d == 2)
+        for s in range(HALVES):
             turn_back(1, s, 0)
-        add(LAST, D - 1)
-        gather(LAST)
 
-        late_codes = new_tile("late_codes", [P, V + N], U32)
-        w2_codes = [new_tile("w2_codes0", [P, N], U32)[:], late_codes[:, V:]]
-        z_codes = [late_codes[:, :V], new_tile("z_codes1", [P, V], U32)[:]]
+        def quantize_z(s):
+            cols = slice(s * P, (s + 1) * P)
+            quantize(z_codes[1][:, cols], z_scales[1][:, cols], z_grouped[1][:, cols, :])
 
-        def quantize_w2(part):
-            g, first, end = W2_PARTS[part]
-            cols = slice(first * P, end * P)
-            quantize(w2_codes[g][:, cols], w2_scales[g][:, cols], w2_grouped[part][:])
-
-        group_w2(vcopy, "tail")
-        quantize_w2("early")
-        quantize_w2("next")
+        late = new_tile("w2_late", [P, 3 * P, J], BF16)
+        last = new_tile("w2_last", [P, 2 * P, J], BF16)
         for s in range(HALVES):
             round_pairs(LAST, s)
             turn_back(1, s, 1)
-        group_w2(scopy, "gap")
-        quantize(z_codes[0], z_scales[0][:], z_grouped[0][:])
-        quantize_w2("middle")
-        quantize_w2("tail")
-        quantize_w2("gap")
+        for a in range(2):
+            group_w2(vcopy, late[:, a * P : (a + 1) * P, :], 0, a + 2)
+        group_w2(vcopy, late[:, 2 * P :, :], 1, 3)
+        quantize_w2(late[:, : 2 * P, :], 0, 2, 4)
+        quantize(rest_codes[:], w2_scales[1][:, 2 * P : 3 * P], rest[:])
+        quantize_w2(late[:, 2 * P :, :], 1, 3, 4)
         for s in range(HALVES):
             interleave(1, s)
-            quantize(z_codes[1][:, s * P : (s + 1) * P], z_scales[1][:, s * P : (s + 1) * P], z_grouped[1][:, s * P : (s + 1) * P, :])
-        group_w2(scopy, "end")
-        quantize_w2("end")
-        for g in range(PASSES):
-            for a in range(N // P):
-                nc.tensor.matmul_mx(
-                    out=out_banks[a][:, :V],
-                    lhsT=w2_codes[g][:, a * P : (a + 1) * P].bitcast(FP8X4),
-                    lhsT_scale=w2_scales[g][:, a * P : (a + 1) * P],
-                    rhs=z_codes[g].bitcast(FP8X4),
-                    rhs_scale=z_scales[g][:],
-                    start=(g == 0),
-                    stop=(g == PASSES - 1),
-                )
-
-        for a in range(N // P):
+            quantize_z(s)
+        second_layer(0, 2)
+        second_layer(0, 3)
+        for s in range(HALVES):
+            for a in range(2, BLOCKS):
+                second_layer(1, a, s * P, (s + 1) * P)
+        for a in range(2):
+            group_w2(vcopy, last[:, a * P : (a + 1) * P, :], 1, a)
+        for a in range(2):
+            quantize_w2(last[:, a * P : (a + 1) * P, :], 1, a, a + 1)
+            second_layer(1, a)
+        order = (2, 3, 0, 1)
+        for n, a in enumerate(order):
             result = keep.tile([P, V], F32, name=f"result{a}")
-            (scopy if a % 2 else vcopy)(out=result[:], in_=out_banks[a][:, :V])
-            (nc.scalar if a == N // P - 1 else nc.sync).dma_start(out=out_view[:, a, :], in_=result[:])
+            (scopy if n % 2 else vcopy)(out=result[:], in_=out_banks[a][:, :V])
+            (nc.scalar if n == BLOCKS - 1 else nc.sync).dma_start(out=out_view[:, a, :], in_=result[:])

from contextlib import ExitStack

import concourse.mybir as mybir

F32 = mybir.dt.float32
BF16 = mybir.dt.bfloat16
U32 = mybir.dt.uint32
U16 = mybir.dt.uint16
U8 = mybir.dt.uint8
FP8X4 = mybir.dt.float8_e4m3fn_x4
MULT = mybir.AluOpType.mult
ADD = mybir.AluOpType.add
MAX = mybir.AluOpType.max
IS_GE = mybir.AluOpType.is_ge
IS_EQUAL = mybir.AluOpType.is_equal
COPY = mybir.ActivationFunctionType.Copy

K, T, D, V, H, N = 512, 512, 4, 256, 1024, 512
FLOPS = 2 * K * H * T + 2 * H * N * V

P = 128
J = 4
TILES = H // P
LAST = TILES - 1
HALVES = V // P
PAIRED = TILES - 2
PASSES = H // (P * J)
BLOCKS = N // P
BANK = 512
QUAD = 32
FLOOR = 2.0**-32
TINY = 2.0**-126
PLAIN = D - 1

X_CUTS = (0, 256, 384, 512)
X_VECTOR = (208, 0, 128)
X_BANK = (0, 1, 4)
W1_CUTS = (0, 1, 2, 3, 5, 6, 8)
H_BANK = {1: 5, 2: 0, 3: 1, 4: 6, 5: 7, 6: 0, 7: 1}
UNIT = 256
PLACE = {
    **{"x_first": 60, "ratio0": 72, "ratio1": 76, "ratio2": 80},
    **{"x_grouped384": 0, "w1_grouped2": 0},
    **{"w1_raw2": 90, "h1": 90, "w1_raw3": 100, "h2": 100, "term1_3": 108, "w1_raw5": 116, "h3": 116, "w1_raw6": 132, "h4": 146, "z_turned0_0": 132, "z_turned0_1": 136, "h6": 126, "h7": 138, "w2_early": 116},
    **{"w2_late": 64, "z_turned1_0": 30, "w2_last": 30},
    **{"rest_codes": 76},
}


def tile_picked_gcn_mlp_none_sub_l_kernel(tc, xT, w1, w2, gate, pos1, pos2, pos3, pos4, out):
    nc = tc.nc
    with ExitStack() as ctx:
        lists = ctx.enter_context(tc.tile_pool(name="lists", bufs=1))
        keep = ctx.enter_context(tc.tile_pool(name="keep", bufs=1))
        shared = ctx.enter_context(tc.tile_pool(name="shared", bufs=1))
        psum = ctx.enter_context(tc.psum_pool(name="psum", bufs=1))

        banks = [psum.tile([P, BANK], F32, name=f"bank{b}") for b in range(8)]
        pass_banks, pair_banks = [banks[2:4], banks[4:6]], banks[6:8]
        out_banks = [banks[0], banks[1], banks[3], banks[4]]

        pos = [lists.tile([P, V // 16], U16, name=f"pos{d}") for d in range(D)]
        vcopy, scopy = nc.vector.tensor_copy, nc.scalar.copy

        ones = keep.tile([P, QUAD], F32, name="ones")
        column = keep.tile([P, QUAD], F32, name="column", align_bytes=64)
        row = keep.tile([P, QUAD], F32, name="row", align_bytes=64)
        ident = keep.tile([P, P], F32, name="ident")
        nc.vector.memset(ones[:], 1.0)
        nc.vector.memset(ident[:], 0.0)
        nc.vector.tensor_tensor_scan(column[:], ones[:], ones[:], 0.0, MULT, ADD)
        nc.vector.transpose(row[:], column[:])
        for a in range(0, P, QUAD):
            nc.vector.tensor_tensor(ident[a : a + QUAD, a : a + QUAD], column[a : a + QUAD, :], row[a : a + QUAD, :], IS_EQUAL)

        gate_rows = keep.tile([P, P], F32, name="gate_rows")
        nc.vector.memset(gate_rows[QUAD : 2 * QUAD, :], 0.0)
        nc.vector.memset(gate_rows[2 * QUAD :, :], 0.0)
        nc.sync.dma_start(gate_rows[:QUAD, :], gate.rearrange("d p (s e) -> (d p s) e", s=HALVES)[:: D * P * HALVES // QUAD + 1, :])

        def new_tile(name, shape, dtype):
            if name in PLACE:
                return shared.tile(shape, dtype, name=name, offset=PLACE[name] * UNIT, align_bytes=64)
            return keep.tile(shape, dtype, name=name, align_bytes=64)

        pieces = list(zip(X_CUTS[:-1], X_CUTS[1:]))
        x_first = new_tile("x_first", [P, J, X_CUTS[2]], F32)
        x_last = keep.tile([P, J, T - X_CUTS[2]], F32, name="x_last")
        x_raw = [x_first[:, :, : X_CUTS[1]], x_first[:, :, X_CUTS[1] :], x_last[:]]
        lots = list(zip(W1_CUTS[:-1], W1_CUTS[1:]))
        w1_raw = [new_tile(f"w1_raw{a}", [P, J, (b - a) * P], F32) for a, b in lots]
        w2_raw = [new_tile(f"w2_raw{g}", [P, J, N], F32) for g in range(PASSES)]

        x_view = xT.rearrange("(p j) t -> p j t", j=J)
        w1_view = w1.rearrange("(p j) i -> p j i", j=J)
        w2_view = w2.rearrange("(g p j) n -> g p j n", g=PASSES, j=J)
        out_view = out.rearrange("(a p) v -> p a v", p=P)

        def load_w1(q):
            nc.sync.dma_start(w1_raw[q][:], w1_view[:, :, lots[q][0] * P : lots[q][1] * P])

        load_w1(0)
        nc.sync.dma_start(x_first[:], x_view[:, :, : X_CUTS[2]])
        nc.sync.dma_start(x_last[:], x_view[:, :, X_CUTS[2] :])
        load_w1(1)
        nc.sync.dma_start(pos[0][:], pos1)
        nc.sync.dma_start(pos[1][:], pos2)
        load_w1(2)
        nc.sync.dma_start(pos[2][:], pos3)
        nc.sync.dma_start(pos[3][:], pos4)
        load_w1(3)
        load_w1(4)
        load_w1(5)
        nc.sync.dma_start(w2_raw[0][:], w2_view[0])
        nc.sync.dma_start(w2_raw[1][:], w2_view[1])

        w1_codes = keep.tile([P, H], U32, name="w1_codes", align_bytes=64)
        w1_scales = keep.tile([P, H], U8, name="w1_scales", align_bytes=64)
        x_grouped = [new_tile(f"x_grouped{a}", [P, b - a, J], BF16) for a, b in pieces]
        x_codes = keep.tile([P, T], U32, name="x_codes", align_bytes=64)
        x_scales = keep.tile([P, T], U8, name="x_scales", align_bytes=64)
        w2_codes = [keep.tile([P, N], U32, name=f"w2_codes{g}", align_bytes=64) for g in range(PASSES)]
        w2_scales = [keep.tile([P, N], U8, name=f"w2_scales{g}", align_bytes=64) for g in range(PASSES)]
        z_codes = [keep.tile([P, V], U32, name=f"z_codes{g}", align_bytes=64) for g in range(PASSES)]
        z_scales = [keep.tile([P, V], U8, name=f"z_scales{g}", align_bytes=64) for g in range(PASSES)]
        z_grouped = [new_tile(f"z_grouped{g}", [P, V, J], BF16) for g in range(PASSES)]
        h = {}
        terms = {}
        z_turned = {}
        w1_grouped = {}

        def group(copy, dst, src):
            copy(out=dst.rearrange("p (c i) j -> p c j i", i=2), in_=src.rearrange("p j (c i) -> p c j i", i=2))

        def quantize(codes, scales, grouped):
            nc.vector.quantize_mx(out=codes.bitcast(FP8X4), scales=scales, in_=grouped.rearrange("p n j -> p (n j)"))

        def prepare_w1(i, copy):
            q = max(q for q, (a, b) in enumerate(lots) if a <= i)
            dst = new_tile(f"w1_grouped{i}", [P, P, J], BF16)
            if i < PAIRED:
                c = (i - lots[q][0]) * P
                group(copy, dst[:], w1_raw[q][:, :, c : c + P])
            else:
                c = (PAIRED - lots[q][0]) * P
                src = w1_raw[q][:, :, c:].rearrange("k j (p u e) -> k u p j e", u=2, e=2)
                copy(out=dst[:].rearrange("k (p e) j -> k p j e", e=2), in_=src[:, i - PAIRED])
            quantize(w1_codes[:, i * P : (i + 1) * P], w1_scales[:, i * P : (i + 1) * P], dst[:])

        def group_w2(copy, dst, g, a):
            group(copy, dst, w2_raw[g][:, :, a * P : (a + 1) * P])

        def quantize_w2(grouped, g, first, end):
            quantize(w2_codes[g][:, first * P : end * P], w2_scales[g][:, first * P : end * P], grouped)

        def multiply(i, a, b, bank):
            nc.tensor.matmul_mx(
                out=bank[:, : b - a],
                lhsT=w1_codes[:, i * P : (i + 1) * P].bitcast(FP8X4),
                lhsT_scale=w1_scales[:, i * P : (i + 1) * P],
                rhs=x_codes[:, a:b].bitcast(FP8X4),
                rhs_scale=x_scales[:, a:b],
                start=True,
                stop=True,
            )

        def project(i):
            h[i] = new_tile(f"h{i}", [P, T], F32)
            multiply(i, 0, T, banks[H_BANK[i]])
            scopy(out=h[i][:], in_=banks[H_BANK[i]][:])

        factor = new_tile("factor", [P, HALVES], F32)
        ratios = [new_tile(f"ratio{d}", [P, V], F32) for d in range(D - 1)]

        ratio_places = [pair_banks[1 - d // 2][:, d % 2 * V : (d % 2 + 1) * V] for d in range(D - 1)]

        def make_ratios():
            nc.tensor.transpose(pair_banks[0][:, :P], gate_rows[:], ident[:])
            g = pair_banks[0][:, :QUAD].rearrange("v (d r s) -> v r s d", d=D, s=HALVES)[:, 0]
            weights = keep.tile([P, 2, D], F32, name="weights")
            bounds = keep.tile([P, HALVES, 2 * D + 1], F32, name="bounds")
            for n, sign in enumerate((1.0, -1.0)):
                nc.vector.memset(weights[:, n, : D - 1], sign * FLOOR)
            scopy(out=weights[:, 0, D - 1 :], in_=ones[:, :1])
            nc.vector.memset(weights[:, 1, D - 1 :], -1.0)
            nc.vector.memset(bounds[:, :, 2 * D :], TINY)
            nc.vector.tensor_tensor(
                bounds[:, :, : 2 * D].rearrange("v s (n d) -> v s n d", n=2),
                g.unsqueeze(2).to_broadcast([P, HALVES, 2, D]),
                weights[:].unsqueeze(1).to_broadcast([P, HALVES, 2, D]),
                MULT,
            )
            sign_plus_one = keep.tile([P, HALVES], F32, name="sign_plus_one")
            nc.vector.tensor_scalar(sign_plus_one[:], g[:, :, D - 1], 0.0, 2.0, IS_GE, MULT)
            size = keep.tile([P, HALVES], F32, name="size")
            nc.vector.tensor_reduce(size[:], bounds[:], mybir.AxisListType.X, MAX)
            signed = keep.tile([P, HALVES, D - 1], F32, name="signed")
            wide = [P, HALVES, D - 1]
            nc.vector.scalar_tensor_tensor(signed[:], sign_plus_one[:].unsqueeze(2).to_broadcast(wide), -1.0, g[:, :, : D - 1], ADD, MULT)
            inverse = keep.tile([P, HALVES], F32, name="inverse")
            nc.vector.reciprocal(inverse[:], size[:])
            nc.vector.scalar_tensor_tensor(factor[:], sign_plus_one[:], -1.0, size[:], ADD, MULT)
            columns = keep.tile(wide, F32, name="columns")
            nc.vector.tensor_tensor(columns[:], signed[:], inverse[:].unsqueeze(2).to_broadcast(wide), MULT)
            for d in range(D - 1):
                for s in range(HALVES):
                    nc.tensor.transpose(ratio_places[d][:, s * P : (s + 1) * P], columns[:, s, d : d + 1].to_broadcast([P, P]), ident[:])

        def bank_of(i, s):
            return pair_banks[s] if i == PAIRED else pass_banks[i == J][s]

        def add(i, d, halves=range(HALVES), start=False, stop=False):
            t = i % J
            for s in halves:
                nc.tensor.matmul(
                    bank_of(i, s)[:, t * P : (t + 1) * P],
                    lhsT=terms[i, d][:, s * P : (s + 1) * P],
                    rhs=ident[:],
                    start=start,
                    stop=stop,
                    is_transpose=True,
                )

        def gather(i, d, halves=range(HALVES)):
            if (i, d) not in terms:
                terms[i, d] = new_tile(f"term{i}_{d}", [P, V], F32)
            v0, v1 = halves[0] * P, (halves[-1] + 1) * P
            nc.vector.tensor_tensor(terms[i, d][:, v0:v1], h[i][:].indirect(pos[d][:, v0 // 16 : v1 // 16]), ratios[d][:, v0:v1], MULT)

        def pick(i):
            terms[i, PLAIN] = new_tile(f"term{i}_{PLAIN}", [P, V], F32)
            nc.scalar.activation(terms[i, PLAIN][:], h[i][:].indirect(pos[PLAIN][:]), COPY)

        def fetch(i, opens=False):
            for d in range(PLAIN):
                gather(i, d)
                add(i, d, start=opens and d == 0)

        def round_sums(i0, i1, s):
            g, t0, t1 = i0 // J, i0 % J, (i1 - 1) % J + 1
            if t0 == 0:
                z_turned[g, s] = new_tile(f"z_turned{g}_{s}", [P, 2, P, 2], BF16)
            nc.scalar.activation(
                z_turned[g, s][:, :, P // J * t0 : P // J * t1, :],
                bank_of(i0, s)[:, t0 * P : t1 * P].rearrange("v (p u e) -> v u p e", u=2, e=2),
                COPY,
                scale=factor[:, s : s + 1],
            )

        def round_pairs(i, s):
            t = i % J
            nc.scalar.activation(
                z_turned[1, s][:, i - PAIRED, P // 2 :, :].rearrange("v p e -> v (p e)"),
                bank_of(i, s)[:, t * P : (t + 1) * P],
                COPY,
                scale=factor[:, s : s + 1],
            )

        def turn_back(g, s, u):
            words = z_turned[g, s][:, u, :, :].rearrange("v p e -> v (p e)").bitcast(F32)
            nc.tensor.transpose(pass_banks[g][s][:, u * P : (u + 1) * P], words, ident[:])

        def interleave(g, s):
            scopy(
                out=z_grouped[g][:, s * P : (s + 1) * P, :].rearrange("p v j -> p (v j)").bitcast(F32).rearrange("p (v u) -> p v u", u=2),
                in_=pass_banks[g][s][:, : 2 * P].rearrange("p (u v) -> p v u", u=2),
            )

        def second_layer(g, a, v0=0, v1=V):
            nc.tensor.matmul_mx(
                out=out_banks[a][:, v0:v1],
                lhsT=(rest_codes[:, (a - 2) * P : (a - 1) * P] if (g, a) == (1, 2) else w2_codes[g][:, a * P : (a + 1) * P]).bitcast(FP8X4),
                lhsT_scale=w2_scales[g][:, a * P : (a + 1) * P],
                rhs=z_codes[g][:, v0:v1].bitcast(FP8X4),
                rhs_scale=z_scales[g][:, v0:v1],
                start=(g == 0),
                stop=(g == PASSES - 1 and v1 == V),
            )

        make_ratios()
        prepare_w1(0, scopy)
        for c, (a, b) in enumerate(pieces):
            cut = X_VECTOR[c]
            if cut > 0:
                group(vcopy, x_grouped[c][:, :cut, :], x_raw[c][:, :, :cut])
            if cut < b - a:
                group(scopy, x_grouped[c][:, cut:, :], x_raw[c][:, :, cut:])
            quantize(x_codes[:, a:b], x_scales[:, a:b], x_grouped[c][:])
        for d in range(PLAIN):
            scopy(out=ratios[d][:], in_=ratio_places[d])
        h[0] = new_tile("h0", [P, T], F32)
        for c, (a, b) in enumerate(pieces):
            multiply(0, a, b, banks[X_BANK[c]])
            (vcopy if b == T else scopy)(out=h[0][:, a:b], in_=banks[X_BANK[c]][:, : b - a])

        prepare_w1(1, vcopy)
        prepare_w1(2, scopy)
        pick(0)
        project(1)
        prepare_w1(3, scopy)
        fetch(0, opens=True)
        add(0, PLAIN)
        prepare_w1(4, scopy)
        project(2)
        fetch(1)
        for i in range(2, J + 1):
            for tile in {2: (5,), 3: (6, 7), 4: ()}[i]:
                prepare_w1(tile, scopy)
            pick(i - 1)
            add(i - 1, PLAIN, stop=i == J)
            project(i + 1)
            fetch(i, opens=i == J)
        early = new_tile("w2_early", [P, 2 * P, J], BF16)
        for a in range(2):
            group_w2(vcopy, early[:, a * P : (a + 1) * P, :], 0, a)
        quantize_w2(early[:], 0, 0, 2)
        rest = new_tile("w2_rest", [P, P, J], BF16)
        rest_codes = new_tile("rest_codes", [P, P], U32)
        pick(J)
        add(J, PLAIN, stop=True)
        for s in range(HALVES):
            round_sums(0, J, s)
            turn_back(0, s, 0)
            turn_back(0, s, 1)
        pick(5)
        interleave(0, 0)
        project(6)
        interleave(0, 1)
        group_w2(scopy, rest[:], 1, 2)
        add(5, PLAIN, start=True)
        for d in range(PLAIN):
            gather(5, d)
            add(5, d, stop=d == PLAIN - 1)
        quantize(z_codes[0][:], z_scales[0][:], z_grouped[0][:])
        project(LAST)
        pick(PAIRED)
        pick(LAST)
        second_layer(0, 0)
        second_layer(0, 1)
        for d in range(PLAIN):
            gather(PAIRED, d)
            add(PAIRED, d, start=d == 0)
        add(PAIRED, PLAIN, stop=True)
        for i in (J, J + 1):
            for s in range(HALVES):
                round_sums(i, i + 1, s)
        for s in range(HALVES):
            round_pairs(PAIRED, s)
        gather(LAST, 0)
        add(LAST, 0, start=True)
        add(LAST, PLAIN)
        for s in range(HALVES):
            for d in (1, 2):
                gather(LAST, d, (s,))
                add(LAST, d, (s,), stop=d == 2)
        for s in range(HALVES):
            turn_back(1, s, 0)

        def quantize_z(s):
            cols = slice(s * P, (s + 1) * P)
            quantize(z_codes[1][:, cols], z_scales[1][:, cols], z_grouped[1][:, cols, :])

        late = new_tile("w2_late", [P, 3 * P, J], BF16)
        last = new_tile("w2_last", [P, 2 * P, J], BF16)
        for s in range(HALVES):
            round_pairs(LAST, s)
            turn_back(1, s, 1)
        for a in range(2):
            group_w2(vcopy, late[:, a * P : (a + 1) * P, :], 0, a + 2)
        group_w2(vcopy, late[:, 2 * P :, :], 1, 3)
        quantize_w2(late[:, : 2 * P, :], 0, 2, 4)
        quantize(rest_codes[:], w2_scales[1][:, 2 * P : 3 * P], rest[:])
        quantize_w2(late[:, 2 * P :, :], 1, 3, 4)
        for s in range(HALVES):
            interleave(1, s)
            quantize_z(s)
        second_layer(0, 2)
        second_layer(0, 3)
        for s in range(HALVES):
            for a in range(2, BLOCKS):
                second_layer(1, a, s * P, (s + 1) * P)
        for a in range(2):
            group_w2(vcopy, last[:, a * P : (a + 1) * P, :], 1, a)
        for a in range(2):
            quantize_w2(last[:, a * P : (a + 1) * P, :], 1, a, a + 1)
            second_layer(1, a)
        order = (2, 3, 0, 1)
        for n, a in enumerate(order):
            result = keep.tile([P, V], F32, name=f"result{a}")
            (scopy if n % 2 else vcopy)(out=result[:], in_=out_banks[a][:, :V])
            (nc.scalar if n == BLOCKS - 1 else nc.sync).dma_start(out=out_view[:, a, :], in_=result[:])
